import numpy as np, ml_dtypes
CORES = [8,136,40,168]
N = 4
BF = ml_dtypes.bfloat16
Q, B, H, L, CAP, TR, ST, LN = 4096, 1024, 512, 256, 48, 3, 4, 2
def code(rng, r):
    m = rng.integers(0, 2, (r, 16)); m[0] = 1
    return (((np.arange(2 ** r)[:, None] >> np.arange(r)) & 1) @ m) & 1
def lay(rng, cb, n, noise, wild):
    v = 63 * cb[rng.integers(0, len(cb), n)].T
    v = np.abs(v - rng.integers(1, 4, (16, n)) * (rng.random((16, n)) < noise))
    return np.where(rng.random((1, n)) < wild, rng.integers(0, 64, (16, n)), v)
def coefs(rng):
    co = rng.integers(1, 256, (N, 8, 16, 3)); co[..., 2] = co[0, ..., 2].copy()
    return co
def home(v, c):
    s = np.add.reduce(c[:, None] * (v >> 2), axis=0)
    return s & (N - 1), (s >> LN) & (H - 1)
def store(p, g, v, words, at=None):
    d, h = home(v if at is None else at, p["co"][0, g, :, 2])
    for j in range(v.shape[1]):
        p["xst"][d[j], g, :, h[j]] = v[:, j]; p["vst"][d[j], g, h[j]] = words[j]
def fill(u):
    c = np.zeros(16, np.int64)
    for i in range(6):
        c[i] = min(255, u); u = u - int(c[i])
    return c
def parts(rng, co, noise, wild):
    p = dict(co=co, gen=np.zeros((N, 8, 16, Q), np.int64), hlp=rng.integers(0, Q, (N, 8, 16, B)), xl=np.zeros((N, 8, 16, L), np.int64), wl=rng.integers(0, Q, (N, 8, L)), vst=rng.integers(0, Q, (N, 8, H)), cb=[])
    p["xst"] = np.where(rng.random((N, 8, 1, H)) < 0.1, rng.integers(0, 256, (N, 8, 16, H)), 255)
    for g in range(8):
        cb = code(rng, int(rng.integers(5, 9))); p["cb"].append(cb)
        for a in range(N):
            p["gen"][a, g] = lay(rng, cb, Q, noise, wild); p["xl"][a, g] = lay(rng, cb, L, noise, 4 * wild)
        v = lay(rng, cb, len(cb), noise, 0.0); store(p, g, v, rng.integers(0, Q, len(cb)))
    return p
def pack(p):
    def b(a, n): return np.ascontiguousarray(a.reshape(N, 128, n)).astype(np.float32).astype(BF)
    return {"gen": b(p["gen"], Q), "hlp": np.ascontiguousarray(p["hlp"].reshape(N, 128, B)).astype(np.int32), "xl": b(p["xl"], L), "wl": p["wl"].astype(np.int32),
            "xst": b(p["xst"], H), "vst": p["vst"].astype(np.int32), "co": b(p["co"], 3)}
def setup_inputs(rng):
    return pack(parts(rng, coefs(rng), 0.008, 0.02))
def setup_inputs_spread(rng):
    co = coefs(rng); co[..., 0] = np.minimum(np.exp2(8 * rng.random((N, 8, 16))).astype(np.int64), 255)
    p = parts(rng, co, 0.02, 0.02)
    for g in range(1, 8, 2):
        p["gen"][:, g] = np.minimum((np.exp2(1 + 5 * rng.random((N, 1, Q))) * 2 * rng.random((N, 16, Q))).astype(np.int64), 63)
        p["xl"][:, g] = np.minimum((np.exp2(1 + 5 * rng.random((N, 1, L))) * 2 * rng.random((N, 16, L))).astype(np.int64), 63)
        p["xst"][:, g] = np.where(rng.random((N, 1, H)) < 0.5, (256 * rng.random((N, 16, H)) ** 3).astype(np.int64), p["xst"][:, g])
    p["hlp"][:, ::2] = (Q * rng.random((N, 4, 16, B)) ** 3).astype(np.int64)
    p["wl"] = (Q * rng.random((N, 8, L)) ** 2).astype(np.int64)
    return pack(p)
def setup_inputs_ends(rng):
    co = 255 * rng.integers(0, 2, (N, 8, 16, 3)); mid = rng.integers(1, 256, co.shape); half = rng.random(co.shape) < 0.5
    co[:, 0::4] = np.where(half, mid, co)[:, 0::4]; co[:, 3::4] = 255
    co[:, 2, :, 0] = 0; co[:, 2, 15, 0] = 255; co[:, 5, :, 0] = 0; co[:, 5, :, 2] = 255; co[..., 2] = co[0, ..., 2].copy()
    p = parts(rng, co, 0.0, 0.0)
    def e(hi, sh): return np.where(rng.random(sh) < 0.7, hi * rng.integers(0, 2, sh), rng.integers(0, hi + 1, sh))
    p["hlp"] = e(Q - 1, (N, 8, 16, B)); p["wl"] = e(Q - 1, (N, 8, L)); p["vst"] = e(Q - 1, (N, 8, H))
    xs = p["xst"]; p["xst"] = np.where((xs == 0) | (xs == 63) | (xs == 255), xs, 255 * rng.integers(0, 2, xs.shape))
    bb = (255 * 15 * 16) & (B - 1)
    for a in range(N):
        for g in range(8):
            G = p["gen"][a, g]
            if g % 4 == 3:
                G[:, 0] = 0; G[:, Q - 1] = 63; G[:, Q - 2] = 63; G[:, 1] = 0; G[15, 1] = 1; G[:, Q - 3] = G[:, 1]
                h = np.zeros(16, np.int64)
                if a % 2 == 1: h[9] = Q - 3; h[15] = 1
                else: h[6] = Q - 2; h[15] = Q - 1
                p["hlp"][a, g, :, bb] = h
                pick = rng.random(L) < 0.15; pick[0] = True; pick[3] = True; pick[L - 1] = True
                p["xl"][a, g][:, pick] = 63
            elif g % 4 == 0: G[:, 0] = 63; G[:, Q - 1] = 0
            else: G[:, 0] = 63 * p["cb"][g][int(rng.integers(1, len(p["cb"][g])))]; G[:, Q - 1] = G[:, 0]
    p["hlp"][:, 7, :, B - 1] = Q - 1; p["hlp"][:, 7, :, B - 2] = 0
    v = np.full(16, 63); v[15] = 0
    p["xl"][:, 5] = v[:, None]; store(p, 5, v[:, None], [Q - 1])
    p["wl"][:, 5, 0] = Q - 1; p["wl"][:, 5, 1] = 0
    return pack(p)
def setup_inputs_corners(rng):
    co = coefs(rng)
    for g in range(0, 8, 2):
        co[:, g, :, 0] = 0; co[:, g, :, 2] = N * rng.integers(1, 31, 16); co[:, g, 0, 2] = 1
        co[:, g + 1, :, 0] = 255 * rng.integers(0, 2, (N, 16))
    p = parts(rng, co, 0.008, 0.02)
    p["wl"] = np.where(rng.random((N, 8, L)) < 0.3, (Q - 1) * rng.integers(0, 2, (N, 8, L)), p["wl"])
    p["xst"][:, 3] = 255
    for a in range(N): p["xst"][a, 1] = lay(rng, p["cb"][1], H, 0.008, 0.02)
    for g in range(0, 8, 2):
        for a in range(N):
            if g == 2: to = [(a + 1) % N] * L
            elif g == 6: to = [N - 1] * L
            else: to = [(a + 1) % N] * CAP + [(a + 2) % N] * (CAP + 1) + [(a + 3) % N] * (CAP - 1) + [(a + 4) % N] + [a] * (L - 3 * CAP - 1)
            p["xl"][a, g, 0] = 4 * rng.permutation(np.array(to)) + rng.integers(0, 4, L)
            ls = rng.permutation(L)[:60]; its = p["xl"][a, g][:, ls]
            far = (its == 63) & (rng.random((1, 60)) < 0.3); far[0] = False
            store(p, g, np.where(far, 255, its), np.where(rng.random(60) < 0.5, p["wl"][a, g, ls], rng.integers(0, Q, 60)), its)
    return pack(p)
def setup_inputs_crowd(rng):
    co = coefs(rng); co[:, 3:, :, 0] = 0; co[:, 1, :, 0] = 0
    v = np.full(16, 21); v[:6] = 63; v[11] = 5; v[12] = 0; v[13] = 1
    u, rem = divmod(N * H - 1, 15); c = fill(u); c[13] = (-u) & (N - 1); c[15] = 1; v[15] = 4 * rem + 1; co[:, 3:, :, 2] = c
    u, rem = divmod(B - 1, 15); c = fill(u); c[11] = rem
    co[:, 4, :, 1] = c; co[:, 7, :, 1] = c
    gw = v.copy(); gw[12] = 63; aft = (63 - np.abs(v - gw))[:, None]
    p = parts(rng, co, 0.008, 0.02)
    for g, far in ((3, 0), (4, 1), (5, 7), (6, 7), (7, 5)):
        w0 = int(rng.integers(0, Q)); word = w0 ^ 1
        if g == 4: w0, word = Q - 9, Q - 7
        if g == 7: w0, word = Q - 7, Q - 9
        p["gen"][:, g, :, w0] = gw; p["xl"][:, g] = v[:, None]; p["wl"][:, g] = w0
        store(p, g, v[:, None], [word]); s = aft.copy(); s[3, 0] = 63 - far
        if g == 3: s[12, 0] = 255
        store(p, g, s, [int(rng.integers(0, Q))], aft)
        if g in (3, 5, 6): p["xl"][int(rng.integers(0, N)), g, 14, CAP - 1] = 22
    for g in (0, 1, 2):
        cb = p["cb"][g]; few = 63 * cb[rng.integers(1, len(cb), 4)].T
        if g == 0: p["xl"][:, g] = few[:, rng.integers(0, 4, (N, L))].transpose(1, 0, 2)
        else:
            p["xl"][:, g] = few[:, :1]
            if g == 2:
                for a in range(N): p["xl"][a, g, :, int(rng.integers(0, L))] = rng.integers(0, 64, 16)
            else: store(p, g, np.full((16, 1), 255), [0], few[:, :1])
    for a in range(N):
        it = rng.integers(1, 64, 16); bb = int(np.add.reduce(co[a, 0, :, 1] * (it >> 2))) & (B - 1)
        p["gen"][a, 0, :, Q - 9] = it; p["hlp"][a, 0, 0, bb] = Q - 9
        ls = np.array([0, 9, L - 1]); p["xl"][a, 0][:, ls] = it[:, None]; p["wl"][a, 0, ls] = Q - 7
    return pack(p)
def check_inputs(d):
    bad = []
    for k, lo, hi in (("gen", 0, 63), ("hlp", 0, Q - 1), ("xl", 0, 63), ("wl", 0, Q - 1), ("xst", 0, 255), ("vst", 0, Q - 1), ("co", 0, 255)):
        a = np.asarray(d[k]).astype(np.float64)
        if not (np.all(a >= lo) and np.all(a <= hi)): bad.append("range of " + k)
        elif np.any(a != np.floor(a)): bad.append("whole numbers in " + k)
    c = np.asarray(d["co"]).astype(np.float64)[..., 2]
    if np.any(c != c[:1]): bad.append("column 2 of co alike on all ranks")
    return bad
def reference(gen, hlp, xl, wl, xst, vst, co):
    G = gen.astype(np.float32).astype(np.int32).reshape(N, 8, 16, Q); S = hlp.astype(np.int32).reshape(N, 8, 16, B)
    x = xl.astype(np.float32).astype(np.int32).reshape(N, 8, 16, L); W = wl.astype(np.int32)
    X = xst.astype(np.float32).astype(np.int32).reshape(N, 8, 16, H); V = vst.astype(np.int32)
    cc = co.astype(np.float32).astype(np.int32).reshape(N, 8, 16, 3); cw, ca, cp = cc[..., 0:1], cc[..., 1:2], cc[..., 2:3]
    A = np.zeros((N, 8), np.int64)
    for t in range(TR):
        for step in range(ST):
            b = np.add.reduce(ca * (x >> 2), axis=2) & (B - 1)
            hs = np.take_along_axis(S, b[:, :, None, :], 3)
            y = np.take_along_axis(G, hs.reshape(N, 8, 1, 16 * L), 3).reshape(N, 8, 16, 16, L)
            y = np.abs(x[:, :, :, None, :] - y)
            sc = np.add.reduce(cw[..., None] * y, axis=2)
            k = np.argmin(sc, axis=2)
            go = np.min(sc, axis=2) < np.add.reduce(cw * x, axis=2)
            yk = np.take_along_axis(y, k[:, :, None, None, :], 3)[:, :, :, 0]
            s = np.take_along_axis(hs, k[:, :, None, :], 2)[:, :, 0]
            x = np.where(go[:, :, None], yk, x)
            W = np.where(go, ((W * s >> 5) + W + 37 * s) & (Q - 1), W)
        f = np.add.reduce(cp * (x >> 2), axis=2); to = f & (N - 1); pl = (f >> LN) & (H - 1)
        ret = np.full((N, 8, L), -1, np.int32)
        for d in range(N):
            m = to == d; sent = m & (np.add.accumulate(m.astype(np.int32), axis=2) <= CAP)
            dist = np.add.reduce(np.abs(np.take_along_axis(X[d][None], pl[:, :, None, :], 3) - x), axis=2)
            kn = sent & (dist <= (A[d] & 7)[None, :, None]); un = sent & ~kn
            ret = np.where(kn, np.take_along_axis(V[d][None], pl, 2), ret)
            A[d] = np.count_nonzero(kn, axis=(0, 2))
            for g in range(8):
                aa, ll = np.nonzero(un[:, g])
                u, first = np.unique(pl[aa, g, ll], return_index=True); aa, ll = aa[first], ll[first]
                X[d, g][:, u] = x[aa, g, :, ll].T; V[d, g, u] = W[aa, g, ll]
        up = (ret >= 0) & (ret != W); new = ((ret * W >> 5) + ret + W) & (Q - 1)
        for r in range(N):
            for g in range(8):
                ll = np.nonzero(up[r, g])[0]
                u, first = np.unique(b[r, g, ll], return_index=True); ll = ll[first]
                S[r, g, (ll + t) & 15, u] = new[r, g, ll]
        x = 63 - np.abs(x - np.take_along_axis(G, W[:, :, None, :], 3))
    sh = np.add.reduce(S * np.arange(1, 17, dtype=np.int32)[:, None], axis=2)
    return {"yx": x.reshape(N, 128, L).astype(np.float32).astype(BF), "yw": W.astype(np.float32), "ys": X.reshape(N, 128, H).astype(np.float32).astype(BF),
            "yv": V.astype(np.float32), "yh": sh.astype(np.float32)}

@@ -1,0 +1,690 @@
+import numpy as np
+from concourse.bass import DstId, RemoteDMATransfer
+from concourse.mybir import dt, AluOpType, AxisListType, ActivationFunctionType
+
+A = AluOpType
+AF = ActivationFunctionType
+N, Q, B, H, L, CAP, TR, ST = 4, 4096, 1024, 512, 256, 48, 3, 4
+CFG = dict(bat=[8, 8], nch=2, wq=2, keymode="act", safe=True, blk=2, exv=4, vshare=[[0, 0]] * 4, xq="v", eng=[2, 2, 2], pes=4, gp=4,
+           stag=2500.0, heavy=600.0, seed=0, noise=0.0, passes=8)
+PAR = dict(cyc=1.0, gam=1.56, sig=3.8, pe=0.5, lat=80.0, vfix=0.0, afix=65.0, rem=3000.0, dma=2000.0)
+CFG.update(passes=6, gp=4, stag=2000.0, heavy=300.0, pes=2, vshare=[[2, 2], [1, 1], [1, 1], [1, 1]], blk=2, exv=5, noise=100.0, seed=9)
+PAR.update(lat=100.0)
+BAT = CFG["bat"]
+NB = len(BAT)
+WQ = CFG["wq"]
+Q0 = [sum(BAT[:h]) for h in range(NB)]
+BLK = CFG["blk"]
+PAIRS = [(a, b) for b in range(16) for a in range(b - b % BLK, b)]
+NP = len(PAIRS)
+BIG, RST = float(2 ** 40), float(2 ** 41)
+C32, C4, C1K = 1.5 * 2 ** 28, 1.5 * 2 ** 25, 1.5 * 2 ** 33
+f32, b16, i32, u16 = "float32", "bfloat16", "int32", "uint16"
+MATS = ["A4", "CC", "N8", "SEL4", "SELD", "ID", "DN", "BI", "NI", "MI"]
+ROWS = ["BMF", "RS", "DG", "NDG", "HM", "BR", "BB", "AG", "ZD", "WR", "SC", "A1"]
+R192 = ["RQ", "RD", "RA", "JK", "N2", "EE", "TRI", "D2"]
+F192 = ["VG", "ANS", "PR", "PB", "ES"]
+SCRATCH = {}
+for _n, _s, _t in [
+        ("G", [Q], b16), ("H32", [B], i32), ("S", [1280], f32), ("XLD", [L], b16), ("X", [704], b16), ("V", [704], f32),
+        ("COD", [16], b16), ("COL", [32], f32), ("PI", [8], i32), ("VI", [768], i32), ("VF", [768], f32),
+        ("IOT", [Q], f32), ("DI", [16, 128], b16), ("J", [544], b16),
+        ("W1", [16, 128], b16), ("W2", [16, 128], b16), ("ONE", [16, 128], f32), ("MAT", [len(MATS), 128], b16),
+        ("ROT", [3, 128], f32), ("SELG", [128], f32), ("KW", [128], f32), ("C768", [8], b16),
+        ("BM", [L], b16), ("BM20", [8, 20], b16), ("FD", [160], f32), ("FM", [len(ROWS), L], f32),
+        ("RB", [len(R192), 192], b16), ("RF", [len(F192), 192], f32), ("TT", [3, L], b16), ("OH", [528], b16),
+        ("KC", [8, 20], b16), ("KD", [320], f32), ("DM", [32], f32), ("BC", [16], u16), ("GM", [24], f32),
+        ("B16", [64], u16), ("BF", [16], f32), ("IXF", [64], f32), ("IX4", [64], u16), ("HF", [1024], f32), ("MK", [1024], f32),
+        ("SF", [128], f32), ("WI", [16], i32), ("WP", [48], i32), ("WT", [16], f32), ("W16", [16], u16),
+        ("TQ", [128], f32), ("MQ", [L], b16), ("CN", [L], b16), ("MC", [L], b16), ("SL", [16], u16),
+        ("SE", [3, 1056], b16), ("SW", [1056], f32), ("AR", [1056], f32), ("R", [3, 192], b16), ("RW", [3, 192], f32),
+        ("PL", [32], i32), ("PL16", [16], u16), ("PLF", [16], f32),
+        ("SM", [48], f32), ("LS", [24], u16), ("TH", [8], f32), ("THI", [8], i32),
+        ("RT", [48], f32), ("RU", [64], f32), ("R16", [32], u16),
+        ("EX", [16 + NP, 128], b16), ("PX", [16 * max(NP, 1)], f32), ("EB", [L + 16 * NP], b16), ("PLS", [2 * max(NP, 1)], u16), ("ZI", [96], i32), ("ZF", [64], f32), ("UP", [16], b16),
+        ("LH", [32], u16), ("XO", [L], b16), ("YH", [1280], f32),
+        ("M", [L, 17], b16), ("XQ", [16, 20], b16), ("D", [L], b16), ("HS", [L], u16), ("KP", [320], f32),
+        ("SO", [320], f32), ("FS", [320], f32), ("SV", [32], f32), ("IX", [32], u16)]:
+    SCRATCH[_n] = ("sbuf", [128] + _s, _t)
+for _h in range(NB):
+    SCRATCH["GR%d" % _h] = ("sbuf", [128, BAT[_h] // WQ, 16 + 256 * WQ], b16)
+    SCRATCH["XF%d" % _h] = ("psum", [128, 512], f32)
+    SCRATCH["KEY%d" % _h] = ("psum", [128, 16, 32], f32)
+SCRATCH["P6"] = ("psum", [128, 512], f32)
+SCRATCH["P7"] = ("psum", [128, 512], f32)
+SEMAPHORES = ["v", "a", "p", "q"] + ["d%d" % k for k in range(12)] + ["%s%d" % (s, k) for s in ("ar", "lo") for k in range(9)]
+
+
+def build(g, core, T, topo, rank):
+    V, S, P = g.vector, g.scalar, g.tensor
+    ops = []
+    tag = [None]
+
+    def op(eng, fn, cost, r, w, kind="c", sem=None):
+        ops.append(dict(eng=eng, fn=fn, cost=cost, r=r.split(), w=w.split(), kind=kind, sem=sem, tag=tag[0]))
+
+    def cp(o, i, n, r, w, k="v"):
+        op("v", lambda: V.tensor_copy(o, i), (k, n), r, w)
+
+    def ts(o, i, s1, s2, o0, o1, n, r, w):
+        if o1 is None:
+            op("v", lambda: V.tensor_scalar(o, i, s1, None, o0), ("v", n), r, w)
+        else:
+            op("v", lambda: V.tensor_scalar(o, i, s1, s2, o0, o1), ("v", n), r, w)
+
+    def tt(o, a, b, o0, n, r, w, k="v"):
+        op("v", lambda: V.tensor_tensor(o, a, b, o0), (k, n), r, w)
+
+    def scan(o, a, b, init, o0, o1, n, r, w):
+        op("v", lambda: V.tensor_tensor_scan(o, a, b, init, o0, o1), ("v", n), r, w)
+
+    def ms(o, c, n, w):
+        op("v", lambda: V.memset(o, c), ("v", n), "", w)
+
+    def act(o, i, f, n, r, w, k="a", **kw):
+        op("a", lambda: S.activation(o, i, f, **kw), (k, n), r, w)
+
+    def mm(lst, r, w):
+        def fn():
+            ins = None
+            for (o, l, rh, st, sp, n) in lst:
+                ins = P.matmul(o, l, rh, st, sp)
+            return ins
+        op("p", fn, ("p", sum(max(64, x[5]) for x in lst)), r, w)
+
+    def iota(o, pat, base, ch, n, w, isint=False):
+        if isint:
+            op("q", lambda: g.iota(o, pat, base, ch), ("q", n), "", w)
+        else:
+            op("q", lambda: g.iota(o, pat, base, ch, allow_small_or_imprecise_dtypes=True), ("q", n), "", w)
+
+    nd = [0]
+
+    def dma(qn, o, i, kb, r, w):
+        e = g.sync if qn == "s" else S
+        op(qn, lambda: e.dma_start(o, i), ("d", kb), r, w, kind="d", sem=("d%d" % nd[0], 16))
+        nd[0] += 1
+
+    nr = [0]
+    peers = [(rank + j) % N for j in range(1, N)]
+
+    def remote(src, dst, r, w):
+        k = nr[0]
+        nr[0] += 1
+        cnt = CFG["eng"]
+
+        def fn():
+            trs = []
+            used = []
+            for j, d in enumerate(peers):
+                dc = T.cores[d]
+                rid, pid = topo.addr(dc, core)
+                es = topo.engines(core, dc)
+                free = [e for e in es[0::2] + es[1::2] if e not in used][:cnt[j]]
+                used.extend(free)
+                trs.append(RemoteDMATransfer(dst_ids=[DstId(rid=rid, pnc=pid)], dma_engine_mask=sum(1 << e for e in free),
+                                             remote_sem=T.sem["ar%d" % k], src=src(d), dst=dst))
+            return g.remote_dma_fused(trs, local_sem=T.sem["lo%d" % k])
+        op("q", fn, ("r", 0), r, "snd%d" % k, kind="r", sem=("lo%d" % k, sum(cnt)))
+        op("x", None, ("x", 0), "snd%d" % k, w, kind="x", sem=("ar%d" % k, sum(cnt)))
+
+    col = lambda j: T.COL[:, j:j + 1]
+    mat = lambda n, b=128: T.MAT[:, MATS.index(n), 0:b]
+    row = lambda n, a=0, b=L, st=1: T.FM[:, ROWS.index(n), a:b:st]
+    rb = lambda n: T.RB[:, R192.index(n), :]
+    rf = lambda n, a=0, b=192, st=1: T.RF[:, F192.index(n), a:b:st]
+    allh = lambda f: " ".join(f % h for h in range(NB))
+    reg = lambda d: slice(256 * d + 16, 256 * d + 16 + CAP)
+    ID, IDF = mat("ID"), T.ROT[:, 0, :]
+    dma("s", T.COD[:, 0:3], T.co[:], 1, "", "CO")
+    dma("s", T.XLD[:], T.xl[:], 64, "", "XL")
+    dma("a", T.H32[:], T.hlp[:], 512, "", "H32")
+    dma("s", T.G[:], T.gen[:], 1024, "", "G")
+    dma("a", T.VI[0:8, 512:768], T.wl[:], 8, "", "VIw")
+    dma("a", T.VI[0:8, 0:512], T.vst[:], 16, "", "VIv")
+    dma("a", T.X[:, 0:H], T.xst[:], 128, "", "X")
+    iota(T.PI[:, 0:1], [[0, 1]], 0, 1, 1, "PI0 gordq", True)
+    iota(T.J[:], [[0, 34], [1, 16]], 0, 0, 544, "J gordq")
+    iota(mat("BI"), [[16, 8], [0, 16]], 0, 0, 128, "BI gordq")
+    iota(mat("MI"), [[1, 128]], 0, 0, 128, "MI gordq")
+    iota(T.DI[:], [[-1, 16], [1, 128]], 0, 0, 2048, "DI gordq")
+    iota(T.KC[:], [[0, 8], [1, 20]], -1, 0, 160, "KC gordq")
+    iota(T.DM[:, 0:16], [[16, 16]], 0, 0, 16, "DM0 gordq")
+    iota(T.GM[:, 0:8], [[1, 8]], 0, 0, 8, "GM0 gordq")
+    iota(T.IOT[:], [[1, Q]], 0, 0, Q, "IOT gordq")
+    cp(col(0), T.PI[:, 0:1], 1, "PI0", "c0")
+    ts(T.PI[:, 1:2], T.PI[:, 0:1], 15, None, A.bitwise_and, None, 1, "PI0", "PI1")
+    ts(T.PI[:, 2:3], T.PI[:, 0:1], 3, None, A.bitwise_and, None, 1, "PI0", "PI2")
+    cp(col(1), T.PI[:, 1:2], 1, "PI1", "c1")
+    cp(col(3), T.PI[:, 2:3], 1, "PI2", "c3")
+    ts(col(2), col(0), col(1), None, A.subtract, None, 1, "c0 c1", "c2")
+    ts(T.COL[:, 9:11], T.COD[:, 1:3], 0.25, None, A.mult, None, 2, "CO", "c9")
+    ts(col(7), T.COD[:, 0:1], 64.0, None, A.mult, None, 1, "CO", "c7")
+    ts(col(8), T.COD[:, 0:1], -32.0, None, A.mult, None, 1, "CO", "c8")
+    ts(mat("A4"), mat("BI"), col(2), col(9), A.is_equal, A.mult, 64, "BI c2 c9", "A4")
+    ts(ID, mat("MI"), col(0), None, A.is_equal, None, 64, "MI c0", "ID")
+    ts(T.BM[:], T.J[:, 0:L], col(1), BIG, A.not_equal, A.mult, 128, "J c1", "BM")
+    ms(T.BM20[:], BIG, 80, "BM20")
+    ts(T.BM20[:, :, 0:16], T.J[:, 0:128], col(1), BIG, A.not_equal, A.mult, 64, "J c1", "BM20")
+    ms(T.XQ[:], 0.0, 160, allh("XQ%d"))
+    ms(T.C768[:], 768.0, 8, "C768")
+    ts(mat("CC"), mat("BI"), col(2), col(10), A.is_equal, A.mult, 64, "BI c2 c9", "CC")
+    mm([(T.P6[:, 0:1], mat("A4"), T.C768[:, 0:1], True, True, 1), (T.P6[:, 1:2], mat("CC"), T.C768[:, 0:1], True, True, 1)],
+       "A4 CC C768", "P6")
+    cp(T.COL[:, 13:15], T.P6[:, 0:2], 2, "P6", "c13")
+    ms(T.FD[:], 0.0, 160, "FD")
+    ms(T.FD[:, 0::20], RST, 8, "FD")
+    ms(T.FD[:, 17::20], C1K, 8, "FD")
+    ms(T.FD[:, 18::20], -C1K, 8, "FD")
+    ts(T.FD[:, 16::20], T.FD[:, 16::20], col(13), -511.5, A.subtract, A.add, 8, "FD c13", "FDa")
+    ts(T.FD[:, 19::20], T.FD[:, 19::20], col(13), None, A.add, None, 8, "FD c13", "FDb")
+    ts(T.W1[:], T.DI[:], col(2), col(7), A.is_equal, A.mult, 1024, "DI c2 c7", "W1")
+    ts(T.W2[:], T.DI[:], col(2), col(8), A.is_equal, A.mult, 1024, "DI c2 c8", "W2")
+    ms(T.KC[:, :, 0], -15.0, 8, "KC")
+    ms(T.KC[:, :, 17:20], BIG, 24, "KC")
+    ms(T.KD[:], 0.0, 320, "KD")
+    ms(T.KD[:, 0::20], RST, 16, "KD")
+    ms(T.KD[:, 17::20], C32, 16, "KD")
+    ms(T.KD[:, 18::20], -C32, 16, "KD")
+    for j in range(WQ):
+        ts(col(24 + j), col(1), -16.0, -16.0 - 256.0 * j, A.mult, A.add, 1, "c1", "c%d" % (24 + j))
+        for h in range(NB):
+            o = T.KD[:, 20 * (Q0[h] + j) + 19:20 * (Q0[h] + BAT[h]):20 * WQ]
+            ts(o, o, col(24 + j), None, A.add, None, 8, "KD c%d" % (24 + j), "KD%d_%d" % (h, j))
+    for h in range(NB):
+        ms(T["GR%d" % h][:, :, 0:16], 0.0, 64, "GZ%d" % h)
+    ms(T.TH[:], 0.0, 8, "TH THa")
+    ts(row("RS"), T.J[:, 0:L], 0.0, RST, A.is_equal, A.mult, 256, "J", "RS")
+    for u in range(4):
+        cp(T.S[:, 256 * u:256 * u + 256], T.H32[:, 256 * u:256 * u + 256], 256, "H32", "S")
+    ts(col(4), col(2), -1.0, None, A.mult, None, 1, "c2", "c4")
+    for u in range(8):
+        o = T.ONE[:, 2 * u:2 * u + 2, :]
+        act(o, T.DI[:, 2 * u:2 * u + 2, :], AF.Abs, 256, "DI c4", "ONE%d" % u, bias=col(4))
+        act(o, o, AF.Relu, 256, "ONE%d" % u, "ONE%d" % u, scale=-1.0, bias=1.0)
+    ts(mat("N8"), mat("BI"), col(2), -8192.0, A.is_equal, A.mult, 64, "BI c2", "N8")
+    ts(mat("NI"), mat("MI"), col(0), -2048.0, A.is_equal, A.mult, 64, "MI c0", "NI")
+    ts(col(11), col(1), 4.0, None, A.is_lt, None, 1, "c1", "c11")
+    ts(col(12), col(1), col(11), 256.0, A.mult, A.mult, 1, "c1 c11", "c12")
+    ts(mat("SEL4"), mat("BI"), col(2), col(11), A.is_equal, A.mult, 64, "BI c2 c11", "SEL4")
+    ts(mat("SELD"), mat("BI"), col(2), col(12), A.is_equal, A.mult, 64, "BI c2 c12", "SELD")
+    ts(mat("DN"), mat("BI"), 0.0, col(3), A.mult, A.subtract, 64, "BI c3", "DN")
+    ts(col(16), col(0), 16.0, None, A.mult, None, 1, "c0", "c16")
+    ts(T.SELG[:], mat("BI"), col(16), None, A.is_equal, None, 128, "BI c16", "SELG")
+    ts(col(15), col(1), 1.0, None, A.add, None, 1, "c1", "c15")
+    ts(col(23), col(2), 1.0 / 16, None, A.mult, None, 1, "c2", "c23")
+    ts(T.KW[:], mat("BI"), col(2), col(15), A.is_equal, A.mult, 128, "BI c2 c15", "KW")
+    ts(T.GM[:, 8:16], T.GM[:, 0:8], col(23), 2048.0, A.is_equal, A.mult, 8, "GM0 c23", "GM")
+    act(row("BMF"), T.BM[:], AF.Copy, 256, "BM", "BMF")
+    act(row("DG"), T.BM[:], AF.Identity, 256, "BM", "DG", scale=-1.0 / BIG, bias=1.0)
+    act(row("NDG"), T.BM[:], AF.Copy, 256, "BM", "NDG", scale=1.0 / BIG)
+    ts(rb("TRI"), T.J[:, 0:192], col(1), 4096.0, A.is_gt, A.mult, 96, "J c1", "TRI")
+    ts(rb("TRI"), rb("TRI"), 2048.0, None, A.add, None, 96, "TRI", "TRI")
+    ts(rb("D2"), T.J[:, 0:192], col(1), 1.0, A.is_equal, A.add, 96, "J c1", "D2")
+    ms(T.RB[:, R192.index("D2"), 0::16], 0.0, 12, "D2")
+    ts(T.OH[:], T.J[:, 0:528], col(1), None, A.is_equal, None, 264, "J c1", "OH")
+    ms(T.OH[:, 0:16], 0.0, 16, "OH")
+    cp(T.BC[:], T.IOT[:, 0:16], 16, "IOT", "BC")
+    ts(T.DM[:, 16:32], T.DM[:, 0:16], col(1), float(H), A.add, A.add, 16, "DM0 c1", "DM1")
+    ts(T.DM[:, 0:16], T.DM[:, 0:16], col(1), float(B), A.add, A.add, 16, "DM0 DM1 c1", "DM0")
+    for u, (qa, qb) in enumerate(PAIRS):
+        ts(T.PLS[:, u:u + 1], col(1), 16.0 * qb, None, A.add, None, 1, "c1", "PLS%d" % u)
+        ms(T.PLS[:, NP + u:NP + u + 1], qa, 1, "PLT%d" % u)
+    if NP:
+        ts(col(5), col(1), 0.0, None, A.add, None, 1, "c1 " + " ".join("PLS%d PLT%d" % (u, u) for u in range(NP)), "PLS")
+    for t in range(TR):
+        for sg, c in ((t, 17 + t), (16 - t, 20 + t)):
+            ts(T.PI[:, 4:5], T.PI[:, 1:2], float(sg), None, A.add, None, 1, "PI1", "PI4")
+            ts(T.PI[:, 5:6], T.PI[:, 4:5], 15, None, A.bitwise_and, None, 1, "PI4", "PI5")
+            cp(col(c), T.PI[:, 5:6], 1, "PI5", "c%d" % c)
+        ts(col(17 + t), col(17 + t), col(2), None, A.add, None, 1, "c%d c2" % (17 + t), "c%d" % (17 + t))
+        ts(T.ROT[:, t, :], mat("MI"), col(17 + t), None, A.is_equal, None, 128, "MI c%d" % (17 + t), "ROT%d" % t)
+        ts(T.TT[:, t, :], T.J[:, 16 - t:16 - t + L], col(20 + t), 4096.0, A.is_le, A.mult, 128, "J c%d" % (20 + t), "TT%d" % t)
+        for d in range(N):
+            act(T.SE[:, t, reg(d)], T.J[:, 0:CAP], AF.Identity, 48, "J", "SE%d" % t, scale=0.0, bias=-64.0)
+    for d in range(N):
+        act(T.SW[:, reg(d)], T.J[:, 0:CAP], AF.Copy, 48, "J", "SW")
+    for d in range(2):
+        act(T.AR[:, 528 * d:528 * d + 528], T.J[:, 0:528], AF.Identity, 528, "J", "AR ARx", scale=0.0, bias=-8192.0)
+    cp(T.VF[0:8, 0:H], T.VI[0:8, 0:H], 512, "VIv", "VFv")
+    cp(T.VF[0:8, H:H + L], T.VI[0:8, H:H + L], 256, "VIw", "VFw")
+    mm([(T.P6[:], T.SELG[0:8, :], T.VF[0:8, 0:H], True, True, 2048)], "SELG VFv", "P6")
+    act(T.V[:, 0:H], T.P6[:], AF.Copy, 512, "P6", "V")
+    mm([(T.P7[:, 0:L], T.SELG[0:8, :], T.VF[0:8, H:H + L], True, False, 1024), (T.P7[:, 0:L], ID, T.BM[:], False, True, 256)],
+       "SELG VFw ID BM", "P7")
+    scan(row("SC"), row("RS"), T.P7[:, 0:L], 0.0, A.add, A.min, 256, "RS P7", "SC")
+    cp(T.WI[:], row("SC", 15, L, 16), 16, "SC", "WI")
+
+    def xslot(h):
+        return T.M[:, 16 * Q0[h]:16 * (Q0[h] + BAT[h]), 0]
+
+    def quarter(h):
+        n = 16 * BAT[h]
+        o = T.XQ[:, Q0[h]:Q0[h] + BAT[h], 0:16]
+        if CFG["xq"] == "v":
+            ts(o, xslot(h), 766.5, None, A.add, None, n // 2, "x%d" % h, "XQ%d" % h)
+        else:
+            act(o, xslot(h), AF.Identity, n, "x%d" % h, "XQ%d" % h, bias=766.5)
+
+    def column(h, s):
+        nq, q0 = BAT[h], Q0[h]
+        n, n2, o = 16 * nq, 20 * nq, 20 * q0
+        XF, xf = T["XF%d" % h], "XF%d" % h
+        quarter(h)
+        mm([(XF[:, 0:n2], ID, T.BM20[:, 0:nq, :], True, False, n2)], "ID BM20", xf)
+        mm([(XF[:, 0:n2], mat("A4"), T.XQ[:, q0:q0 + nq, :], False, True, n2)], "A4 XQ%d" % h, xf)
+        scan(T.FS[:, o:o + n2], T.FD[:, 0:n2], XF[:, 0:n2], 0.0, A.add, A.min, n2, "FD FDa FDb " + xf, "FS%d" % h)
+        mm([(XF[:, 256:256 + n], ID, xslot(h), True, True, n)], "ID x%d" % h, xf)
+        bo = (T.RT if s == ST - 1 else T.BF)[:, q0:q0 + nq]
+        on = ("RTb%d" if s == ST - 1 else "BF%d") % h
+        tt(bo, T.FS[:, o + 15:o + n2:20], T.FS[:, o + 19:o + n2:20], A.subtract, 2 * nq, "FS%d" % h, on)
+        c = 16 * s + q0
+        cp(T.B16[:, c:c + nq], bo, nq, on, "B16_%d_%d" % (s, h))
+
+    def step(h, s, first):
+        nq, q0 = BAT[h], Q0[h]
+        n, n2, o, nw = 16 * nq, 20 * nq, 20 * q0, nq // WQ
+        GR, KEY, XF = T["GR%d" % h], T["KEY%d" % h], T["XF%d" % h]
+        key, xf, xn = "KEY%d" % h, "XF%d" % h, "x%d" % h
+        c = 16 * s + q0
+        win, wn = (T.H32[:], "H32") if first else (T.S[:, 0:B], "S")
+        cp(T.HS[:, 16 * q0:16 * q0 + n], win.indirect(T.B16[:, c:c + nq]), n, "%s B16_%d_%d" % (wn, s, h), "HS%d" % h, k="vg")
+        mm([(KEY[:, 0:nq, 0:20], ID, T.KC[:, 0:nq, :], True, False, n2)], "ID KC", key)
+        nch = CFG["nch"]
+        cut = [nq * j // nch for j in range(nch + 1)]
+        allg = []
+        for j in range(nch):
+            a, b = cut[j], cut[j + 1]
+            m = 16 * (b - a)
+            vs = nq - CFG["vshare"][s][h]
+            ends = sorted(set(list(range(a, b + 1, WQ)) + ([vs] if a < vs < b else [])))
+            for a2, b2 in zip(ends[:-1], ends[1:]):
+                nm = " ".join("GR%d_%d" % (h, q) for q in range(a2, b2))
+                off = 16 + 256 * (a2 % WQ)
+                go, gi = GR[:, a2 // WQ, off:off + 256 * (b2 - a2)], T.G[:].indirect(T.HS[:, 16 * (q0 + a2):16 * (q0 + b2)])
+                if a2 < vs:
+                    act(go, gi, AF.Copy, 256 * (b2 - a2), "G HS%d" % h, nm + " gord%d" % h, k="ag")
+                else:
+                    cp(go, gi, 256 * (b2 - a2), "G HS%d" % h, nm, k="vg")
+            gr = " ".join("GR%d_%d" % (h, q) for q in range(a, b))
+            allg.append(gr)
+            pes = CFG["pes"]
+            if WQ == 1 or j == nch - 1:
+                ga = a if WQ == 1 else 0
+                for u in range(pes * WQ):
+                    w, p0 = u // pes, 16 * (u % pes) // pes
+                    off = 16 + 256 * w
+                    mm([(KEY[:, ga + w:b:WQ, 1:17], T.W2[:, p, :], GR[:, ga // WQ:b // WQ, off + 16 * p:off + 16 + 16 * p], False, False,
+                         16 * (b - ga) // WQ) for p in range(p0, p0 + 16 // pes)], "W2 " + (gr if WQ == 1 else " ".join(allg)), key)
+            for k in range(16):
+                tt(T.M[:, 16 * (q0 + a):16 * (q0 + b), 1 + k], GR[:, a // WQ:b // WQ, 16 + k:16 + 256 * WQ:16],
+                   XF[:, 256 + 16 * a:256 + 16 * b], A.max, m, gr + " " + xf, "M%d_%d_%d" % (h, j, k))
+            for u in range(pes):
+                mm([(KEY[:, a:b, 0:17], T.W1[:, p, :], T.M[:, 16 * (q0 + a) + p:16 * (q0 + b):16, :], False, j == nch - 1 and p == 15,
+                     17 * (b - a))
+                    for p in range(16 * u // pes, 16 * (u + 1) // pes)],
+                   "W1 " + xn + "".join(" M%d_%d_%d" % (h, j, k) for k in range(16)), key)
+        kd = "KD" + "".join(" KD%d_%d" % (h, j) for j in range(WQ))
+        if CFG["keymode"] == "act":
+            act(T.KP[:, o:o + n2], KEY[:, 0:nq, 0:20], AF.Copy, n2, key, "KP%d" % h)
+            scan(T.SO[:, o:o + n2], T.KD[:, o:o + n2], T.KP[:, o:o + n2], 0.0, A.add, A.min, n2, kd + " KP%d" % h, "SO%d" % h)
+            so = "SO%d" % h
+        else:
+            for q in range(nq):
+                u = o + 20 * q
+                scan(T.SO[:, u:u + 20], T.KD[:, u:u + 20], KEY[:, q, 0:20], 0.0, A.add, A.min, 20, kd + " " + key, "SO%d_%d" % (h, q))
+            so = " ".join("SO%d_%d" % (h, q) for q in range(nq))
+        tt(T.SV[:, q0:q0 + nq], T.SO[:, o + 16:o + n2:20], T.SO[:, o + 19:o + n2:20], A.subtract, 2 * nq, so, "SVa%d" % h)
+        tt(T.SV[:, 16 + q0:16 + q0 + nq], T.SO[:, o + 16:o + n2:20], T.SO[:, o + 18:o + n2:20], A.is_ge, 2 * nq, so, "SVb%d" % h)
+        ixn = "IXF_%d_%d" % (s, h)
+        tt(T.IXF[:, c:c + nq], T.SV[:, q0:q0 + nq], T.SV[:, 16 + q0:16 + q0 + nq], A.mult, 2 * nq, "SVa%d SVb%d" % (h, h), ixn)
+        if WQ == 1:
+            cp(T.IX[:, 2 * q0:2 * q0 + 2 * nq:2], T.IXF[:, c:c + nq], nq, ixn, "IX%d" % h)
+        ix4 = "IX4_%d_%d" % (s, h)
+        cp(T.IX4[:, c:c + nq], T.IXF[:, c:c + nq], nq, ixn, ix4)
+        rd = " ".join(allg) + " GZ%d %s " % (h, xn) + ("IX%d" % h if WQ == 1 else ix4)
+        for a in range(nw):
+            ls = T.IX[:, 2 * (q0 + a):2 * (q0 + a) + 1] if WQ == 1 else T.IX4[:, c + 2 * a:c + 2 * a + 2]
+            l0, l1 = 16 * (q0 + a * WQ), 16 * (q0 + a * WQ + WQ)
+            tt(T.D[:, l0:l1], GR[:, a, :].indirect(ls), T.M[:, l0:l1, 0], A.subtract, 16 * WQ, rd, "D%d_%d" % (h, a), k="vg")
+        act(xslot(h), T.D[:, 16 * q0:16 * q0 + n], AF.Abs, n, " ".join("D%d_%d" % (h, a) for a in range(nw)), xn)
+
+    for h in range(NB):
+        a = 16 * Q0[h]
+        tag[0] = h
+        cp(xslot(h), T.XLD[:, a:a + 16 * BAT[h]], 8 * BAT[h], "XL", "x%d" % h)
+        column(h, 0)
+    mine = slice(CAP * rank, CAP * rank + CAP)
+    for t in range(TR):
+        last = t == TR - 1
+        sen, rn, rwn = "SE%d" % t, "R%d" % t, "RW%d" % t
+        R = T.R[:, t, :]
+        for s in range(ST):
+            for h in range(NB):
+                tag[0] = h
+                step(h, s, t == 0 and s == 0)
+                if s < ST - 1:
+                    column(h, s + 1)
+        for h in range(NB):
+            nq, q0 = BAT[h], Q0[h]
+            n, a, o = 16 * nq, 16 * q0, 20 * q0
+            XF, xf = T["XF%d" % h], "XF%d" % h
+            tag[0] = h
+            quarter(h)
+            mm([(XF[:, 0:n], ID, mat("DN", n), True, False, n)], "ID DN", xf)
+            mm([(XF[:, 0:n], mat("CC"), T.XQ[:, q0:q0 + nq, 0:16], False, True, n)], "CC XQ%d" % h, xf)
+            ts(T.TQ[:, 0:n], XF[:, 0:n], C4, C4, A.add, A.subtract, n, xf, "TQ")
+            tt(T.MQ[:, a:a + n], T.TQ[:, 0:n], XF[:, 0:n], A.is_equal, n, "TQ " + xf, "MQ%d" % h)
+            init = 0.0 if h == 0 else T.CN[:, a - 1:a]
+            scan(T.CN[:, a:a + n], T.MQ[:, a:a + n], T.MQ[:, a:a + n], init, A.add, A.max, n // 2,
+                 "MQ%d" % h + (" CN%d" % (h - 1) if h else ""), "CN%d" % h)
+            tt(T.MC[:, a:a + n], T.MQ[:, a:a + n], T.CN[:, a:a + n], A.mult, 2 * n, "MQ%d CN%d" % (h, h), "MC%d" % h)
+            mm([(XF[:, 0:n], ID, T.BM[:, 0:n], True, False, n), (XF[:, 0:n], mat("SELD"), T.MQ[:, a:a + n], False, False, n)],
+               "ID BM SELD MQ%d" % h, xf)
+            mm([(XF[:, 0:n], mat("SEL4"), T.MC[:, a:a + n], False, True, n)], "SEL4 MC%d" % h, xf)
+            scan(T.FS[:, o:o + n], row("RS", 0, n), XF[:, 0:n], 0.0, A.add, A.min, n, "RS " + xf, "FS%d" % h)
+            ts(T.SL[:, q0:q0 + nq], T.FS[:, o + 15:o + n:16], 15.0, None, A.add, None, nq, "FS%d" % h, "SL%d" % h)
+            cp(T.SE[:, t, :].indirect(T.SL[:, q0:q0 + nq]), xslot(h), n, "SL%d x%d" % (h, h), sen, k="vs")
+            act(T.RT[:, 16 + q0:16 + q0 + nq], T.FS[:, o + 15:o + n:16], AF.Identity, nq, "FS%d" % h, "RTs%d" % h, bias=15.0)
+        tag[0] = None
+        remote(lambda d, t=t: T.SE[:, t, reg(d)], T.R[:, t, mine], sen + " ARx", rn + "x")
+        cp(T.R[:, t, mine], T.SE[:, t, reg(rank)], 24, sen, rn)
+        mm([(T.P6[:, 64:96], T.ROT[:, t, :], T.RT[:, 0:32], True, True, 256)], "ROT%d %s %s" % (t, allh("RTb%d"), allh("RTs%d")), "P6")
+        cp(T.R16[:], T.P6[:, 64:96], 32, "P6", "R16")
+        act(T.RU[:, 0:16], T.P6[:, 64:80], AF.Copy, 16, "P6", "RUb")
+        act(T.RU[:, 48:64], T.P6[:, 64:80], AF.Identity, 16, "P6", "RUc", bias=2048.0)
+        for s in range(ST):
+            for h in range(NB):
+                c0, c1 = 16 * s + Q0[h], 16 * s + Q0[h] + BAT[h]
+                hf = T.HF[:, 16 * c0:16 * c1]
+                act(hf, T.S[:, 0:B].indirect(T.B16[:, c0:c1]), AF.Copy, 16 * BAT[h], "S B16_%d_%d" % (s, h), "HF%d_%d" % (s, h), k="ag")
+                tt(T.MK[:, 16 * c0:16 * c1], T.OH[:].indirect(T.IX4[:, c0:c1]), hf,
+                   A.mult, 16 * BAT[h], "OH IX4_%d_%d HF%d_%d" % (s, h, s, h), "MK%d_%d" % (s, h), k="vg")
+        for u in range(4):
+            mm([(T.P6[:, 0:64], T.ONE[:, p, :], T.MK[:, p::16], p == 0, p == 15, 256) for p in range(4 * u, 4 * u + 4)],
+               "ONE%d ONE%d " % (2 * u, 2 * u + 1) + " ".join(allh("MK%d_%%d" % s) for s in range(ST)), "P6")
+        act(T.SF[:, 0:64], T.P6[:, 0:64], AF.Copy, 64, "P6", "SFa")
+        act(T.SF[:, 64:128], T.P6[:, 0:64], AF.Copy, 64, "P6", "SFb", scale=37.0)
+        for s in range(ST):
+            tt(T.WP[:, 0:16], T.WI[:], T.SF[:, 16 * s:16 * s + 16], A.mult, 32, "WI SFa", "WPa")
+            tt(T.WT[:], T.WI[:], T.SF[:, 64 + 16 * s:80 + 16 * s], A.add, 32, "WI SFb", "WT")
+            ts(T.WP[:, 16:32], T.WP[:, 0:16], 5, None, A.arith_shift_right, None, 16, "WPa", "WPb")
+            tt(T.WP[:, 32:48], T.WP[:, 16:32], T.WT[:], A.add, 32, "WPb WT", "WPc")
+            ts(T.WI[:], T.WP[:, 32:48], Q - 1, None, A.bitwise_and, None, 16, "WPc", "WI")
+        cp(T.W16[:], T.WI[:], 16, "WI", "W16")
+        cp(T.RT[:, 32:48], T.WI[:], 16, "WI", "RTw")
+        rr = rn + " " + rn + "x"
+        ts(rb("RQ"), R, 766.5, None, A.add, None, 96, rr, "RQ")
+        mm([(T.P7[:, 0:192], ID, T.BM[:, 0:192], True, False, 192)], "ID BM", "P7")
+        mm([(T.P7[:, 0:192], mat("CC"), rb("RQ"), False, True, 192)], "CC RQ", "P7")
+        scan(row("SC", 0, 192), row("RS", 0, 192), T.P7[:, 0:192], 0.0, A.add, A.min, 192, "RS P7", "SC")
+        ts(T.PL[:, 0:12], row("SC", 15, 192, 16), col(14), None, A.subtract, None, 12, "SC c13", "PLa")
+        ts(T.PL[:, 16:28], T.PL[:, 0:12], 2, H - 1, A.arith_shift_right, A.bitwise_and, 12, "PLa", "PLb")
+        cp(T.PL16[:, 0:12], T.PL[:, 16:28], 12, "PLb", "PL16")
+        tt(rb("RD"), T.X[:, 0:H].indirect(T.PL16[:, 0:12]), R, A.subtract, 192, "X PL16 " + rr, "RD", k="vg")
+        act(rf("VG"), T.V[:, 0:H].indirect(T.PL16[:, 0:12]), AF.Identity, 192, "V PL16 TH", "VG", k="ag", bias=T.TH[:, 0:1])
+        act(rb("RA"), rb("RD"), AF.Abs, 192, "RD", "RA")
+        mm([(T.P7[:, 256:448], mat("N8"), rb("RA"), True, True, 192)], "N8 RA", "P7")
+        tt(rf("ANS"), rf("VG"), T.P7[:, 256:448], A.add, 192, "VG P7", "ANS")
+        remote(lambda d: rf("ANS", CAP * d, CAP * d + CAP), T.AR[:, reg(rank)], "ANS", "ARx")
+        act(T.AR[:, reg(rank)], rf("ANS", CAP * rank, CAP * rank + CAP), AF.Copy, 48, "ANS", "AR")
+        act(row("WR"), T.IOT[:].indirect(T.W16[:]), AF.Copy, 256, "IOT W16", "WR", k="ag")
+        for h in range(NB):
+            cp(T.SW[:].indirect(T.SL[:, Q0[h]:Q0[h] + BAT[h]]), row("WR", 16 * Q0[h], 16 * (Q0[h] + BAT[h])), 16 * BAT[h],
+               "WR SL%d" % h, "SW", k="vs")
+        remote(lambda d: T.SW[:, reg(d)], T.RW[:, t, mine], "SW", rwn + "x")
+        act(T.RW[:, t, mine], T.SW[:, reg(rank)], AF.Copy, 48, "SW", rwn)
+        for h in range(NB):
+            nq, q0 = BAT[h], Q0[h]
+            n = 16 * nq
+            D = T.D[:, 16 * q0:16 * q0 + n]
+            dn = " ".join("D%d_%d" % (h, a) for a in range(nq // WQ))
+            tt(D, T.G[:].indirect(T.W16[:, q0:q0 + nq]), xslot(h), A.subtract, n, "G W16 x%d" % h, dn, k="vg")
+            act(D, D, AF.Abs, n, dn, dn)
+            if last:
+                act(T.XO[:, 16 * q0:16 * q0 + n], D, AF.Identity, n, dn, "XO%d" % h, scale=-1.0, bias=63.0)
+            else:
+                act(xslot(h), D, AF.Identity, n, dn, "x%d" % h, scale=-1.0, bias=63.0)
+        tt(row("HM"), T.S[:, 0:B].indirect(T.R16[:, 0:16]), row("NDG"), A.mult, 256, "S R16 NDG", "HM", k="vg")
+        tt(row("BR"), T.IOT[:].indirect(T.R16[:, 0:16]), T.TT[:, t, :], A.add, 256, "IOT R16 TT%d" % t, "BR", k="vg")
+        tt(T.EB[:, 0:L], T.RU[:, 0:16].indirect(T.BC[:]), row("BR"), A.is_equal, 256, "RUb BC BR", "A1", k="vg")
+        ne = L + 16 * NP
+        if NP:
+            act(row("BB"), T.IOT[:].indirect(T.R16[:, 0:16]), AF.Copy, 256, "IOT R16", "BB", k="ag")
+            act(T.PX[:], row("BB").indirect(T.PLS[:, 0:NP]), AF.Copy, 16 * NP, "BB PLS", "PX0", k="ag")
+            tt(T.EB[:, L:ne], T.RU[:, 0:16].indirect(T.PLS[:, NP:2 * NP]), T.PX[:], A.is_equal, 16 * NP, "RUb PLS PX0", "PX1", k="vg")
+        for gg in range(8):
+            o, sc = T.EX[:, :, 16 * gg:16 * gg + 16], T.GM[:, 8 + gg:9 + gg]
+            if gg < CFG["exv"]:
+                ts(o, T.EB[:], sc, None, A.mult, None, ne // 2, "A1 PX1 GM", "EX%d" % gg)
+            else:
+                act(o, T.EB[:], AF.Identity, ne, "A1 PX1 GM", "EX%d" % gg, scale=sc)
+        mm([(T.P6[:, 96:112], T.ROT[:, t, :], T.RT[:, 32:48], True, True, 256)], "ROT%d RTw" % t, "P6")
+        act(T.RU[:, 32:48], T.P6[:, 96:112], AF.Copy, 16, "P6", "RUw")
+        if not last:
+            for h in range(NB):
+                column(h, 0)
+        act(rb("JK"), rf("ANS"), AF.Sign, 192, "ANS", "JK THa", scale=-1.0, bias=-0.5, accum_out=T.TH[:, 4:5])
+        if not last:
+            ts(T.THI[:, 0:1], T.TH[:, 4:5], -0.5, 96.0, A.mult, A.add, 1, "THa", "THI0")
+            ts(T.THI[:, 1:2], T.THI[:, 0:1], 7, None, A.bitwise_and, None, 1, "THI0", "THI1")
+            ts(T.TH[:, 0:1], T.THI[:, 1:2], 8192.0, None, A.mult, None, 1, "THI1", "TH")
+        cp(T.PLF[:, 0:12], T.PL[:, 16:28], 12, "PLb", "PLF")
+        act(rf("PR"), T.IOT[:].indirect(T.PL16[:, 0:12]), AF.Copy, 192, "IOT PL16", "PR", k="ag", scale=-1.0)
+        act(rf("PB"), T.PLF[:, 0:12].indirect(T.BC[:, 0:12]), AF.Copy, 192, "PLF BC", "PB", k="ag")
+        act(rb("N2"), R, AF.Relu, 192, rr, "N2", scale=-64.0)
+        mm([(T.P7[:, 0:192], IDF, rf("PR"), True, False, 768), (T.P7[:, 0:192], IDF, rf("PB"), False, False, 768),
+            (T.P7[:, 0:192], ID, rb("TRI"), False, False, 192), (T.P7[:, 0:192], ID, rb("N2"), False, False, 192)],
+           "ROT0 ID PR PB TRI N2", "P7")
+        mm([(T.P7[:, 0:192], mat("NI"), rb("JK"), False, True, 192)], "NI JK", "P7")
+        ts(rb("EE"), T.P7[:, 0:192], 0.0, None, A.is_equal, None, 192, "P7", "EE")
+        scan(rf("ES"), rb("D2"), rb("EE"), 0.0, A.mult, A.add, 192, "D2 EE", "ES")
+        ts(T.SM[:, 0:12], rf("ES", 15, 192, 16), 1.0, 2048.0, A.not_equal, A.mult, 12, "ES", "SMa")
+        tt(T.SM[:, 16:28], T.SM[:, 0:12], T.PLF[:, 0:12], A.add, 24, "SMa PLF", "SMb")
+        tt(T.SM[:, 32:44], T.SM[:, 16:28], T.DM[:, 16:28], A.min, 24, "SMb DM1", "SMc")
+        cp(T.LS[:, 0::2], T.SM[:, 32:44], 12, "SMc", "LS")
+        for q in range(11, -1, -1):
+            cp(T.X[:].indirect(T.LS[:, 2 * q:2 * q + 1]), T.R[:, t, 16 * q:16 * q + 16], 16, "LS " + rr, "X", k="vs")
+        for q in range(11, -1, -1):
+            cp(T.V[:].indirect(T.LS[:, 2 * q:2 * q + 1]), T.RW[:, t, 16 * q:16 * q + 16], 16, "LS %s %sx" % (rwn, rwn), "V", k="vs")
+        tt(row("AG"), T.AR[:].indirect(T.R16[:, 16:32]), row("BMF"), A.add, 256, "AR ARx R16 BMF", "AG", k="vg")
+        scan(row("SC"), row("RS"), row("AG"), 0.0, A.add, A.min, 256, "RS AG", "SC")
+        Wr = T.RU[:, 32:48]
+        Z = lambda j: T.ZI[:, 16 * j:16 * j + 16]
+        cp(Z(0), row("SC", 15, L, 16), 16, "SC", "Z0")
+        ts(T.ZF[:, 0:16], row("SC", 15, L, 16), 0.0, None, A.is_ge, None, 16, "SC", "ZFk")
+        ts(Z(1), Z(0), Q - 1, None, A.bitwise_and, None, 16, "Z0", "Z1")
+        tt(T.ZF[:, 16:32], Z(1), Wr, A.not_equal, 32, "Z1 RUw", "ZFn")
+        tt(Z(2), Z(1), Wr, A.mult, 32, "Z1 RUw", "Z2")
+        tt(T.UP[:], T.ZF[:, 16:32], T.ZF[:, 0:16], A.mult, 32, "ZFn ZFk", "UP")
+        mm([(T.P6[:, 128:144], IDF, T.RU[:, 48:64], True, False, 256)], "ROT0 RUc", "P6")
+        mm([(T.P6[:, 128:144], mat("NI"), T.UP[:], False, False, 16)] +
+           [(T.P6[:, 128 + qb:129 + qb], T.EX[:, 16 + u, :], T.UP[:, qa:qa + 1], False, False, 1) for u, (qa, qb) in enumerate(PAIRS)] +
+           [(T.P6[:, 128 + q:129 + q], T.EX[:, q, :], T.UP[:, q:q + 1], False, q == 15, 1) for q in range(16)],
+           "NI UP" + "".join(" EX%d" % gg for gg in range(8)), "P6")
+        tt(T.ZF[:, 32:48], Z(1), Wr, A.add, 32, "Z1 RUw", "ZFs")
+        ts(Z(3), Z(2), 5, None, A.arith_shift_right, None, 16, "Z2", "Z3")
+        tt(Z(4), Z(3), T.ZF[:, 32:48], A.add, 32, "Z3 ZFs", "Z4")
+        ts(Z(5), Z(4), Q - 1, None, A.bitwise_and, None, 16, "Z4", "Z5")
+        tt(row("ZD"), Z(5).indirect(T.BC[:]), row("DG"), A.mult, 256, "Z5 BC DG", "ZD", k="vg")
+        tt(T.ZF[:, 48:64], T.P6[:, 128:144], T.DM[:, 0:16], A.min, 16, "P6 DM0", "ZFl")
+        cp(T.LH[:, 0:16] if NP else T.LH[:, 0::2], T.ZF[:, 48:64], 16, "ZFl", "LH")
+        if last:
+            for u in range(2):
+                mm([(T.XF1[:], T.KW[:], T.S[:, 512 * u:512 * u + 512], True, True, 2048)], "KW S", "XF1")
+                act(T.YH[:, 512 * u:512 * u + 512], T.XF1[:], AF.Copy, 512, "XF1", "YH")
+            mm([(T.XF0[:, 0:L], T.KW[:], row("HM"), True, False, 1024)], "KW HM", "XF0")
+            mm([(T.XF0[:, 0:L], T.KW[:], row("ZD"), False, True, 1024)], "KW ZD", "XF0")
+            cp(row("AG"), T.XF0[:, 0:L], 256, "XF0", "AG")
+        for q in range(16 - BLK, -1, -BLK):
+            ls = T.LH[:, q:q + BLK] if NP else T.LH[:, 2 * q:2 * q + 1]
+            a, b = 16 * q, 16 * (q + BLK)
+            if last:
+                cp(T.YH[:].indirect(ls), row("AG", a, b), b - a, "LH AG", "YH", k="vs")
+            else:
+                tt(T.S[:].indirect(ls), row("ZD", a, b), row("HM", a, b), A.add, b - a, "LH ZD HM", "S", k="vs")
+    dma("s", T.yx[:], T.XO[:], 64, allh("XO%d"), "")
+    dma("s", T.yw[:], T.FM[0::16, ROWS.index("WR"), :], 8, "WR", "")
+    dma("s", T.ys[:], T.X[:, 0:H], 128, "X", "")
+    dma("s", T.yv[:], T.V[0::16, 0:H], 16, "V", "")
+    dma("a", T.yh[:], T.YH[0::16, 0:B], 32, "YH", "")
+    return ops
+
+
+def link(ops):
+    wr, rd, deps = {}, {}, []
+    ps = lambda k: k[:2] in ("XF", "P6", "P7") or k[:3] == "KEY"
+    for i, o in enumerate(ops):
+        d = {}
+        for k in o["r"] + o["w"]:
+            if k in wr:
+                j = wr[k]
+                same = ops[j]["eng"] == o["eng"] and ops[j]["kind"] == "c"
+                raw = k in o["r"] and not ps(k)
+                d[j] = d.get(j, False) or (not same) or raw or (CFG["safe"] and not ps(k) and k[:4] != "gord")
+            if k in o["w"] or ps(k):
+                for j in rd.get(k, []):
+                    same = ops[j]["eng"] == o["eng"] and ops[j]["kind"] == "c"
+                    d[j] = d.get(j, False) or (not same) or CFG["safe"]
+        d.pop(i, None)
+        deps.append(d)
+        for k in o["r"] + o["w"]:
+            if k in o["w"] or ps(k):
+                wr[k] = i
+                rd[k] = []
+        for k in o["r"]:
+            if not (k in o["w"] or ps(k)):
+                rd.setdefault(k, []).append(i)
+    return deps
+
+
+def span(o, par):
+    k, n = o["cost"]
+    c = par["cyc"] * 0.83
+    if k == "v":
+        return par["vfix"] + max(64, n) * c, 0.0
+    if k == "vg":
+        return 50 * par["cyc"] + par["gam"] * n * c, 0.0
+    if k == "vs":
+        return 50 * par["cyc"] + par["sig"] * n * c, 0.0
+    if k == "a":
+        return par["afix"] + n * c, 0.0
+    if k == "ag":
+        return 65 * par["cyc"] + par["gam"] * n * c, 0.0
+    if k == "p":
+        return par["pe"] * n * c, 60.0
+    if k == "q":
+        return 130 + 2 * n * c, 0.0
+    if k == "d":
+        return 60.0, par["dma"] + 5.0 * n
+    if k == "r":
+        return 300.0, 0.0
+    return 0.0, par["rem"]
+
+
+def order(ops, deps, par):
+    n = len(ops)
+    sp = [span(o, par) for o in ops]
+    succ = [[] for _ in range(n)]
+    for i, d in enumerate(deps):
+        for j in d:
+            succ[j].append(i)
+    pri = [0.0] * n
+    for i in range(n - 1, -1, -1):
+        pri[i] = sp[i][0] + sp[i][1] + max([pri[j] + (par["lat"] if deps[j][i] else 0.0) for j in succ[i]] + [0.0])
+    noise = np.random.RandomState(CFG["seed"]).rand(n) * CFG["noise"]
+    for i in range(n):
+        pri[i] += float(noise[i])
+        if ops[i]["tag"] is not None:
+            pri[i] += CFG["stag"] * (NB - 1 - ops[i]["tag"])
+            if ops[i]["cost"][0] == "ag" or ops[i]["w"][0][0] == "M":
+                pri[i] -= CFG["heavy"]
+    lag = lambda j, i: (sp[j][1] + par["lat"]) if deps[i][j] else 0.001
+    before = [[(j, lag(j, i)) for j in deps[i]] for i in range(n)]
+    after = [[(i, lag(j, i)) for i in succ[j]] for j in range(n)]
+    best = None
+    for it in range(CFG["passes"]):
+        start = place(ops, sp, before, after, pri, [0.0] * n)
+        end = max(start[i] + sp[i][0] + sp[i][1] for i in range(n))
+        if best is None or end < best[0]:
+            best = (end, start)
+        back = place(ops, sp, after, before, [start[i] + sp[i][0] for i in range(n)], [x[1] for x in sp])
+        pri = [back[i] + sp[i][0] for i in range(n)]
+    start = best[1]
+    return sorted(range(n), key=lambda i: (start[i], i))
+
+
+def place(ops, sp, before, after, pri, t0):
+    n = len(ops)
+    left = [len(d) for d in before]
+    ready = [i for i in range(n) if left[i] == 0]
+    start = [0.0] * n
+    busy = {}
+    while ready:
+        i = max(ready, key=lambda j: (pri[j], -j))
+        ready.remove(i)
+        t = t0[i]
+        for j, lg in before[i]:
+            t = max(t, start[j] + sp[j][0] + lg)
+        lst = busy.setdefault(ops[i]["eng"], [])
+        dur = sp[i][0]
+        lo, hi = 0, len(lst)
+        while lo < hi:
+            mid = (lo + hi) // 2
+            if lst[mid][1] <= t:
+                lo = mid + 1
+            else:
+                hi = mid
+        while lo < len(lst) and lst[lo][0] < t + dur:
+            t = max(t, lst[lo][1])
+            lo += 1
+        lst.insert(lo, (t, t + dur))
+        start[i] = t
+        for j, lg in after[i]:
+            left[j] -= 1
+            if left[j] == 0:
+                ready.append(j)
+    return start
+
+
+def rank_program(g, core, T, topo):
+    rank = T.rank_of(core)
+    if rank is None:
+        return
+    ops = build(g, core, T, topo, rank)
+    deps = link(ops)
+    seq = order(ops, deps, PAR)
+    queue = {"v": g.vector, "a": g.scalar, "p": g.tensor, "q": g, "s": g.sync}
+    need = set()
+    for i, d in enumerate(deps):
+        if ops[i]["kind"] != "x":
+            need.update(j for j, hard in d.items() if hard)
+    count, mark, seen, extra = {}, {}, {}, []
+    for i in seq:
+        o = ops[i]
+        if o["kind"] == "x":
+            mark[i] = o["sem"]
+            extra.append(o["sem"])
+            continue
+        e = o["eng"]
+        want = {}
+        for j, hard in deps[i].items():
+            if hard:
+                s, val = mark[j]
+                want[s] = max(want.get(s, 0), val)
+        for s, val in want.items():
+            if seen.get((e, s), 0) < val:
+                queue[e].wait_ge(T.sem[s], val)
+                seen[(e, s)] = val
+        ins = o["fn"]()
+        if o["kind"] == "d":
+            ins.then_inc(T.sem[o["sem"][0]], 16)
+        if o["kind"] != "c":
+            mark[i] = o["sem"]
+            extra.append(o["sem"])
+        elif i in need:
+            count[e] = count.get(e, 0) + 1
+            ins.then_inc(T.sem[e], 1)
+            mark[i] = (e, count[e])
+    for s, val in list(count.items()) + extra:
+        g.wait_ge(T.sem[s], val)

@@ -10,10 +10,14 @@ CFG = dict(bat=[8, 8], nch=2, wq=2, keymode="act", safe=True, blk=2, exv=4, vsha
 PAR = dict(cyc=1.0, gam=1.56, sig=3.8, pe=0.5, lat=80.0, vfix=0.0, afix=65.0, rem=3000.0, dma=2000.0)
 CFG.update(passes=6, gp=4, stag=2000.0, heavy=300.0, pes=2, vshare=[[2, 2], [1, 1], [1, 1], [1, 1]], blk=2, exv=5, noise=100.0, seed=9)
 PAR.update(lat=100.0)
+CFG.update(bat=[4, 4, 4, 4], nch=1, wq=1, noise=0.0, stag=1300.0, vshare=[[1, 1, 0, 0]] + [[0] * 4] * 3,
+           blk=4, exv=3, passes=4, heavy=600.0, pes=2, keymode="q", xq="a")
+PAR.update(lat=220.0, pe=0.85, rem=4000.0)
 BAT = CFG["bat"]
 NB = len(BAT)
 WQ = CFG["wq"]
 Q0 = [sum(BAT[:h]) for h in range(NB)]
+XFN = ["XF0", "XF1", "P6", "P7"] if NB == 4 else ["XF0", "XF1", "XF2"]
 BLK = CFG["blk"]
 PAIRS = [(a, b) for b in range(16) for a in range(b - b % BLK, b)]
 NP = len(PAIRS)
@@ -48,7 +52,7 @@ for _n, _s, _t in [
     SCRATCH[_n] = ("sbuf", [128] + _s, _t)
 for _h in range(NB):
     SCRATCH["GR%d" % _h] = ("sbuf", [128, BAT[_h] // WQ, 16 + 256 * WQ], b16)
-    SCRATCH["XF%d" % _h] = ("psum", [128, 512], f32)
+    SCRATCH[XFN[_h]] = ("psum", [128, 512], f32)
     SCRATCH["KEY%d" % _h] = ("psum", [128, 16, 32], f32)
 SCRATCH["P6"] = ("psum", [128, 512], f32)
 SCRATCH["P7"] = ("psum", [128, 512], f32)
@@ -269,7 +273,7 @@ def build(g, core, T, topo, rank):
     def column(h, s):
         nq, q0 = BAT[h], Q0[h]
         n, n2, o = 16 * nq, 20 * nq, 20 * q0
-        XF, xf = T["XF%d" % h], "XF%d" % h
+        XF, xf = T[XFN[h]], XFN[h]
         quarter(h)
         mm([(XF[:, 0:n2], ID, T.BM20[:, 0:nq, :], True, False, n2)], "ID BM20", xf)
         mm([(XF[:, 0:n2], mat("A4"), T.XQ[:, q0:q0 + nq, :], False, True, n2)], "A4 XQ%d" % h, xf)
@@ -284,8 +288,8 @@ def build(g, core, T, topo, rank):
     def step(h, s, first):
         nq, q0 = BAT[h], Q0[h]
         n, n2, o, nw = 16 * nq, 20 * nq, 20 * q0, nq // WQ
-        GR, KEY, XF = T["GR%d" % h], T["KEY%d" % h], T["XF%d" % h]
-        key, xf, xn = "KEY%d" % h, "XF%d" % h, "x%d" % h
+        GR, KEY, XF = T["GR%d" % h], T["KEY%d" % h], T[XFN[h]]
+        key, xf, xn = "KEY%d" % h, XFN[h], "x%d" % h
         c = 16 * s + q0
         win, wn = (T.H32[:], "H32") if first else (T.S[:, 0:B], "S")
         cp(T.HS[:, 16 * q0:16 * q0 + n], win.indirect(T.B16[:, c:c + nq]), n, "%s B16_%d_%d" % (wn, s, h), "HS%d" % h, k="vg")
@@ -368,7 +372,7 @@ def build(g, core, T, topo, rank):
         for h in range(NB):
             nq, q0 = BAT[h], Q0[h]
             n, a, o = 16 * nq, 16 * q0, 20 * q0
-            XF, xf = T["XF%d" % h], "XF%d" % h
+            XF, xf = T[XFN[h]], XFN[h]
             tag[0] = h
             quarter(h)
             mm([(XF[:, 0:n], ID, mat("DN", n), True, False, n)], "ID DN", xf)

@@ -1,62 +1,52 @@
-import numpy as np
+import math
 from concourse.bass import DstId, RemoteDMATransfer
 from concourse.mybir import dt, AluOpType, AxisListType, ActivationFunctionType
 
 A = AluOpType
 AF = ActivationFunctionType
 N, Q, B, H, L, CAP, TR, ST = 4, 4096, 1024, 512, 256, 48, 3, 4
-CFG = dict(bat=[8, 8], nch=2, wq=2, keymode="act", safe=True, blk=2, exv=4, vshare=[[0, 0]] * 4, xq="v", eng=[2, 2, 2], pes=4, gp=4,
-           stag=2500.0, heavy=600.0, seed=0, noise=0.0, passes=8)
-PAR = dict(cyc=1.0, gam=1.56, sig=3.8, pe=0.5, lat=80.0, vfix=0.0, afix=65.0, rem=3000.0, dma=2000.0)
-CFG.update(passes=6, gp=4, stag=2000.0, heavy=300.0, pes=2, vshare=[[2, 2], [1, 1], [1, 1], [1, 1]], blk=2, exv=5, noise=100.0, seed=9)
-PAR.update(lat=100.0)
-CFG.update(bat=[4, 4, 4, 4], nch=1, wq=1, noise=0.0, stag=1300.0, vshare=[[1, 1, 0, 0]] + [[0] * 4] * 3,
-           blk=4, exv=3, passes=4, heavy=600.0, pes=2, keymode="q", xq="a")
-PAR.update(lat=220.0, pe=0.85, rem=4000.0)
-BAT = CFG["bat"]
-NB = len(BAT)
-WQ = CFG["wq"]
-Q0 = [sum(BAT[:h]) for h in range(NB)]
-XFN = ["XF0", "XF1", "P6", "P7"] if NB == 4 else ["XF0", "XF1", "XF2"]
-BLK = CFG["blk"]
-PAIRS = [(a, b) for b in range(16) for a in range(b - b % BLK, b)]
-NP = len(PAIRS)
+NB = 4
+CFG = dict(eng=[4, 2, 2], pes=2, t0=7500.0, beat=[2000.0, 2100.0], gap=11000.0, tail=22000.0, passes=5, fit=0.6, xq="addda", own=0, vs0=0)
+SPREAD = [dict(lat=170.0), dict(lat=260.0), dict(lat=200.0, gam=2.0, sig=5.0, afix=100.0), dict(lat=150.0, gam=1.15, sig=2.0)]
+PAR = dict(cyc=1.0, gam=1.56, sig=3.8, pe=0.6, lat=220.0, vfix=0.0, afix=65.0, rem=4000.0, big=18000.0, dma=2000.0)
 BIG, RST = float(2 ** 40), float(2 ** 41)
-C32, C4, C1K = 1.5 * 2 ** 28, 1.5 * 2 ** 25, 1.5 * 2 ** 33
+C1, C4, C32, C512, C1K = 1.5 * 2 ** 23, 1.5 * 2 ** 25, 1.5 * 2 ** 28, 1.5 * 2 ** 32, 1.5 * 2 ** 33
+PIT, MSG, GW = 720, 528, 2112
 f32, b16, i32, u16 = "float32", "bfloat16", "int32", "uint16"
-MATS = ["A4", "CC", "N8", "SEL4", "SELD", "ID", "DN", "BI", "NI", "MI"]
-ROWS = ["BMF", "RS", "DG", "NDG", "HM", "BR", "BB", "AG", "ZD", "WR", "SC", "A1"]
-R192 = ["RQ", "RD", "RA", "JK", "N2", "EE", "TRI", "D2"]
-F192 = ["VG", "ANS", "PR", "PB", "ES"]
+MATS = ["A4", "NA", "CC", "CC4", "WT", "N8", "SEL4", "SELD", "NEG", "ON2", "THM", "ID", "KI", "NI", "I3", "SV", "KF", "DN", "BI", "MI", "PT", "OI"]
+FMAT = ["IDF", "NIF", "AI", "NAI", "IDH", "S12", "ONF", "KW", "SELG", "PM0", "PM1", "PM2", "PM3"]
+ROWS = ["RS", "HM", "ZD", "WR", "SC", "S3", "AN", "VA", "CF", "AG", "FS", "YW"]
+BROW = ["BM", "RSB", "TT", "CM", "MQ", "CN", "MC", "SP", "RA", "X", "D", "XO", "BC", "GJ", "XF", "RD", "HI", "CB",
+        "K0", "K1", "K2", "N0", "N1", "N2"]
+R192 = ["RQ", "RX", "JS", "AB", "ES", "TRI", "TR2"]
+F192 = ["RW", "PR", "PB", "SO"]
+CROSS = [(d, m) for d in (1, 2, 3) for m in range(4)]
+OFF = [16 + sum(4 - d for d, m in CROSS[:u]) for u in range(len(CROSS) + 1)]
 SCRATCH = {}
 for _n, _s, _t in [
-        ("G", [Q], b16), ("H32", [B], i32), ("S", [1280], f32), ("XLD", [L], b16), ("X", [704], b16), ("V", [704], f32),
-        ("COD", [16], b16), ("COL", [32], f32), ("PI", [8], i32), ("VI", [768], i32), ("VF", [768], f32),
-        ("IOT", [Q], f32), ("DI", [16, 128], b16), ("J", [544], b16),
-        ("W1", [16, 128], b16), ("W2", [16, 128], b16), ("ONE", [16, 128], f32), ("MAT", [len(MATS), 128], b16),
-        ("ROT", [3, 128], f32), ("SELG", [128], f32), ("KW", [128], f32), ("C768", [8], b16),
-        ("BM", [L], b16), ("BM20", [8, 20], b16), ("FD", [160], f32), ("FM", [len(ROWS), L], f32),
-        ("RB", [len(R192), 192], b16), ("RF", [len(F192), 192], f32), ("TT", [3, L], b16), ("OH", [528], b16),
-        ("KC", [8, 20], b16), ("KD", [320], f32), ("DM", [32], f32), ("BC", [16], u16), ("GM", [24], f32),
-        ("B16", [64], u16), ("BF", [16], f32), ("IXF", [64], f32), ("IX4", [64], u16), ("HF", [1024], f32), ("MK", [1024], f32),
-        ("SF", [128], f32), ("WI", [16], i32), ("WP", [48], i32), ("WT", [16], f32), ("W16", [16], u16),
-        ("TQ", [128], f32), ("MQ", [L], b16), ("CN", [L], b16), ("MC", [L], b16), ("SL", [16], u16),
-        ("SE", [3, 1056], b16), ("SW", [1056], f32), ("AR", [1056], f32), ("R", [3, 192], b16), ("RW", [3, 192], f32),
-        ("PL", [32], i32), ("PL16", [16], u16), ("PLF", [16], f32),
+        ("G", [Q], b16), ("H32", [B], i32), ("S", [1280], f32), ("XB", [PIT], b16), ("XR", [N * PIT], b16), ("PW", [3, 16], f32),
+        ("COD", [16], b16), ("COL", [40], f32), ("PI", [8], i32), ("VI", [768], i32), ("VF", [768], f32),
+        ("IOT", [Q + 16], f32), ("DI", [16, 128], b16), ("J", [544], b16), ("LF", [40], f32), ("OH", [GW], b16),
+        ("W1", [16, 128], b16), ("W2", [16, 128], b16), ("MAT", [len(MATS), 128], b16), ("FT", [len(FMAT), 128], f32),
+        ("C768", [8], b16), ("BM20", [4, 20], b16), ("BM22", [4, 22], b16), ("FD", [80], f32), ("FE", [88], f32),
+        ("FM", [len(ROWS), L], f32), ("BR", [len(BROW), L], b16), ("RB", [len(R192), 192], b16), ("RF", [len(F192), 192], f32),
+        ("KC", [4, 35], b16), ("KD", [4, 36], f32), ("DM", [32], f32), ("LA", [40], u16), ("LB", [40], u16),
+        ("RS4", [64], f32), ("SB", [64, 4], f32), ("BO", [64], u16), ("B2", [4, 4], f32), ("B2N", [16], f32), ("B21", [16], f32),
+        ("B16", [64], u16), ("BF", [64], f32), ("IXF", [16], f32), ("IX", [64], u16), ("HF", [1024], f32), ("MK", [1024], f32),
+        ("SF", [16], f32), ("WI", [16], i32), ("WP", [48], i32), ("WT", [16], f32), ("W16", [16], u16), ("WK", [16], u16),
+        ("TQ", [L], f32), ("SL", [16], u16), ("XI", [16], u16), ("F2", [352], f32), ("FB", [320], f32),
+        ("SE", [3, 1056], b16), ("SW", [1056], f32), ("R", [3, 192], b16), ("SG", [H], b16), ("HY", [H], f32), ("PL", [32], i32), ("PL16", [16], u16), ("PLF", [16], f32),
         ("SM", [48], f32), ("LS", [24], u16), ("TH", [8], f32), ("THI", [8], i32),
-        ("RT", [48], f32), ("RU", [64], f32), ("R16", [32], u16),
-        ("EX", [16 + NP, 128], b16), ("PX", [16 * max(NP, 1)], f32), ("EB", [L + 16 * NP], b16), ("PLS", [2 * max(NP, 1)], u16), ("ZI", [96], i32), ("ZF", [64], f32), ("UP", [16], b16),
-        ("LH", [32], u16), ("XO", [L], b16), ("YH", [1280], f32),
-        ("M", [L, 17], b16), ("XQ", [16, 20], b16), ("D", [L], b16), ("HS", [L], u16), ("KP", [320], f32),
-        ("SO", [320], f32), ("FS", [320], f32), ("SV", [32], f32), ("IX", [32], u16)]:
+        ("B2R", [640], f32), ("TE", [640], b16), ("ZI", [96], i32), ("ZF", [96], f32), ("Z16", [16], u16), ("LH", [16], u16),
+        ("YH", [1280], f32), ("YV", [PIT], f32), ("HV", [H], f32), ("M", [NB, 1024], b16), ("XQ", [64, 5], b16), ("XN", [68, 5], b16), ("XQ2", [16, 22], b16),
+        ("HS", [L], u16), ("SO", [16, 36], f32)]:
     SCRATCH[_n] = ("sbuf", [128] + _s, _t)
 for _h in range(NB):
-    SCRATCH["GR%d" % _h] = ("sbuf", [128, BAT[_h] // WQ, 16 + 256 * WQ], b16)
-    SCRATCH[XFN[_h]] = ("psum", [128, 512], f32)
-    SCRATCH["KEY%d" % _h] = ("psum", [128, 16, 32], f32)
-SCRATCH["P6"] = ("psum", [128, 512], f32)
-SCRATCH["P7"] = ("psum", [128, 512], f32)
-SEMAPHORES = ["v", "a", "p", "q"] + ["d%d" % k for k in range(12)] + ["%s%d" % (s, k) for s in ("ar", "lo") for k in range(9)]
+    SCRATCH["GR%d" % _h] = ("sbuf", [128, GW], b16)
+    SCRATCH["KB%d" % _h] = ("psum", [128, 4, 128], f32)
+for _n in ("XJ0", "XJ1", "P6", "P7"):
+    SCRATCH[_n] = ("psum", [128, 512], f32)
+SEMAPHORES = ["v", "a", "p", "q"] + ["d%d" % k for k in range(24)] + ["%s%d" % (s, k) for s in ("ar", "lo") for k in range(7)]
 
 
 def build(g, core, T, topo, rank):
@@ -82,11 +72,17 @@ def build(g, core, T, topo, rank):
     def scan(o, a, b, init, o0, o1, n, r, w):
         op("v", lambda: V.tensor_tensor_scan(o, a, b, init, o0, o1), ("v", n), r, w)
 
+    def pick(o, a, b, n, r, w):
+        scan(o, a, b, 0.0, A.add, A.min, n, r, w)
+
     def ms(o, c, n, w):
         op("v", lambda: V.memset(o, c), ("v", n), "", w)
 
     def act(o, i, f, n, r, w, k="a", **kw):
         op("a", lambda: S.activation(o, i, f, **kw), (k, n), r, w)
+
+    def fill(o, c, n, w, r=""):
+        act(o, T.J[:, 0:n], AF.Identity, n, "J " + r, w, scale=0.0, bias=c)
 
     def mm(lst, r, w):
         def fn():
@@ -102,6 +98,9 @@ def build(g, core, T, topo, rank):
         else:
             op("q", lambda: g.iota(o, pat, base, ch, allow_small_or_imprecise_dtypes=True), ("q", n), "", w)
 
+    def const(o, c, n, w):
+        iota(o, [[0, n]], c, 0, n, w + " gordq")
+
     nd = [0]
 
     def dma(qn, o, i, kb, r, w):
@@ -112,444 +111,508 @@ def build(g, core, T, topo, rank):
     nr = [0]
     peers = [(rank + j) % N for j in range(1, N)]
 
-    def remote(src, dst, r, w):
+    def remote(src, dst, r, w, same=False):
         k = nr[0]
         nr[0] += 1
         cnt = CFG["eng"]
+        ids = [topo.addr(T.cores[d], core) for d in peers]
+        ids = [DstId(rid=rid, pnc=pid) for rid, pid in ids]
+        es = topo.engines(core, T.cores[peers[0]])
 
         def fn():
-            trs = []
-            used = []
-            for j, d in enumerate(peers):
-                dc = T.cores[d]
-                rid, pid = topo.addr(dc, core)
-                es = topo.engines(core, dc)
-                free = [e for e in es[0::2] + es[1::2] if e not in used][:cnt[j]]
-                used.extend(free)
-                trs.append(RemoteDMATransfer(dst_ids=[DstId(rid=rid, pnc=pid)], dma_engine_mask=sum(1 << e for e in free),
-                                             remote_sem=T.sem["ar%d" % k], src=src(d), dst=dst))
+            if same:
+                trs = [RemoteDMATransfer(dst_ids=ids, dma_engine_mask=topo.mask(core, T.cores[peers[0]]), remote_sem=T.sem["ar%d" % k],
+                                         src=src(0), dsts=[dst] * len(peers))]
+            else:
+                trs = [RemoteDMATransfer(dst_ids=[ids[j]], dma_engine_mask=sum(1 << e for e in es[sum(cnt[:j]):sum(cnt[:j + 1])]),
+                                         remote_sem=T.sem["ar%d" % k], src=src(d), dst=dst) for j, d in enumerate(peers)]
             return g.remote_dma_fused(trs, local_sem=T.sem["lo%d" % k])
-        op("q", fn, ("r", 0), r, "snd%d" % k, kind="r", sem=("lo%d" % k, sum(cnt)))
-        op("x", None, ("x", 0), "snd%d" % k, w, kind="x", sem=("ar%d" % k, sum(cnt)))
+        op("q", fn, ("r", 0), r + " gordq", "snd%d gordq" % k, kind="r", sem=("lo%d" % k, len(es) if same else sum(cnt)))
+        op("x", None, ("X" if same else "x", 0), "snd%d" % k, w, kind="x", sem=("ar%d" % k, len(es) * len(peers) if same else sum(cnt)))
 
     col = lambda j: T.COL[:, j:j + 1]
     mat = lambda n, b=128: T.MAT[:, MATS.index(n), 0:b]
+    fm = lambda n: T.FT[:, FMAT.index(n), :]
     row = lambda n, a=0, b=L, st=1: T.FM[:, ROWS.index(n), a:b:st]
-    rb = lambda n: T.RB[:, R192.index(n), :]
+    br = lambda n, a=0, b=L, st=1: T.BR[:, BROW.index(n), a:b:st]
+    rb = lambda n, a=0, b=192, st=1: T.RB[:, R192.index(n), a:b:st]
     rf = lambda n, a=0, b=192, st=1: T.RF[:, F192.index(n), a:b:st]
     allh = lambda f: " ".join(f % h for h in range(NB))
     reg = lambda d: slice(256 * d + 16, 256 * d + 16 + CAP)
-    ID, IDF = mat("ID"), T.ROT[:, 0, :]
+    ID, IDF = mat("ID"), fm("IDF")
+    own = PIT * rank
     dma("s", T.COD[:, 0:3], T.co[:], 1, "", "CO")
-    dma("s", T.XLD[:], T.xl[:], 64, "", "XL")
+    dma("s", br("X"), T.xl[:], 64, "", allh("x%d"))
     dma("a", T.H32[:], T.hlp[:], 512, "", "H32")
     dma("s", T.G[:], T.gen[:], 1024, "", "G")
     dma("a", T.VI[0:8, 512:768], T.wl[:], 8, "", "VIw")
     dma("a", T.VI[0:8, 0:512], T.vst[:], 16, "", "VIv")
-    dma("a", T.X[:, 0:H], T.xst[:], 128, "", "X")
+    dma("a", T.XB[:, 0:H], T.xst[:], 128, "", "XB")
     iota(T.PI[:, 0:1], [[0, 1]], 0, 1, 1, "PI0 gordq", True)
     iota(T.J[:], [[0, 34], [1, 16]], 0, 0, 544, "J gordq")
     iota(mat("BI"), [[16, 8], [0, 16]], 0, 0, 128, "BI gordq")
     iota(mat("MI"), [[1, 128]], 0, 0, 128, "MI gordq")
     iota(T.DI[:], [[-1, 16], [1, 128]], 0, 0, 2048, "DI gordq")
-    iota(T.KC[:], [[0, 8], [1, 20]], -1, 0, 160, "KC gordq")
-    iota(T.DM[:, 0:16], [[16, 16]], 0, 0, 16, "DM0 gordq")
-    iota(T.GM[:, 0:8], [[1, 8]], 0, 0, 8, "GM0 gordq")
-    iota(T.IOT[:], [[1, Q]], 0, 0, Q, "IOT gordq")
+    iota(T.KC[:, :, 16:32], [[0, 4], [2, 16]], -15, 0, 64, "KCk gordq")
     cp(col(0), T.PI[:, 0:1], 1, "PI0", "c0")
     ts(T.PI[:, 1:2], T.PI[:, 0:1], 15, None, A.bitwise_and, None, 1, "PI0", "PI1")
     ts(T.PI[:, 2:3], T.PI[:, 0:1], 3, None, A.bitwise_and, None, 1, "PI0", "PI2")
+    ts(T.PI[:, 3:4], T.PI[:, 0:1], 2, 3, A.arith_shift_right, A.bitwise_and, 1, "PI0", "PI3")
     cp(col(1), T.PI[:, 1:2], 1, "PI1", "c1")
-    cp(col(3), T.PI[:, 2:3], 1, "PI2", "c3")
+    cp(T.COL[:, 3:5], T.PI[:, 2:4], 1, "PI2 PI3", "c3")
     ts(col(2), col(0), col(1), None, A.subtract, None, 1, "c0 c1", "c2")
     ts(T.COL[:, 9:11], T.COD[:, 1:3], 0.25, None, A.mult, None, 2, "CO", "c9")
-    ts(col(7), T.COD[:, 0:1], 64.0, None, A.mult, None, 1, "CO", "c7")
-    ts(col(8), T.COD[:, 0:1], -32.0, None, A.mult, None, 1, "CO", "c8")
+    act(col(7), T.COD[:, 0:1], AF.Identity, 1, "CO", "c7", scale=64.0)
+    act(col(8), T.COD[:, 0:1], AF.Identity, 1, "CO", "c8", scale=-32.0)
     ts(mat("A4"), mat("BI"), col(2), col(9), A.is_equal, A.mult, 64, "BI c2 c9", "A4")
     ts(ID, mat("MI"), col(0), None, A.is_equal, None, 64, "MI c0", "ID")
-    ts(T.BM[:], T.J[:, 0:L], col(1), BIG, A.not_equal, A.mult, 128, "J c1", "BM")
-    ms(T.BM20[:], BIG, 80, "BM20")
-    ts(T.BM20[:, :, 0:16], T.J[:, 0:128], col(1), BIG, A.not_equal, A.mult, 64, "J c1", "BM20")
-    ms(T.XQ[:], 0.0, 160, allh("XQ%d"))
-    ms(T.C768[:], 768.0, 8, "C768")
+    ts(br("BM"), T.J[:, 0:L], col(1), BIG, A.not_equal, A.mult, 128, "J c1", "BM")
+    ms(T.BM20[:], BIG, 40, "BM20")
+    ts(T.BM20[:, :, 0:16], T.J[:, 0:64], col(1), BIG, A.not_equal, A.mult, 32, "J c1", "BM20")
+    ms(T.XQ[:, :, 4], 0.0, 32, allh("XQ%d"))
+    ms(T.XN[:, :, 4], 0.0, 34, allh("XN%d") + " XNc")
+    ms(T.XN[:, 64:68, 0:4], -768.0, 8, "XNc")
+    ts(mat("NA"), mat("A4"), -1.0, None, A.mult, None, 64, "A4", "NA")
+    ms(T.C768[:, 0:1], 1536.0, 1, "C768")
+    ms(T.C768[:, 1:2], 768.0, 1, "C768")
     ts(mat("CC"), mat("BI"), col(2), col(10), A.is_equal, A.mult, 64, "BI c2 c9", "CC")
-    mm([(T.P6[:, 0:1], mat("A4"), T.C768[:, 0:1], True, True, 1), (T.P6[:, 1:2], mat("CC"), T.C768[:, 0:1], True, True, 1)],
+    mm([(T.P6[:, 0:1], mat("A4"), T.C768[:, 0:1], True, True, 1), (T.P6[:, 1:2], mat("CC"), T.C768[:, 1:2], True, True, 1)],
        "A4 CC C768", "P6")
     cp(T.COL[:, 13:15], T.P6[:, 0:2], 2, "P6", "c13")
-    ms(T.FD[:], 0.0, 160, "FD")
-    ms(T.FD[:, 0::20], RST, 8, "FD")
-    ms(T.FD[:, 17::20], C1K, 8, "FD")
-    ms(T.FD[:, 18::20], -C1K, 8, "FD")
-    ts(T.FD[:, 16::20], T.FD[:, 16::20], col(13), -511.5, A.subtract, A.add, 8, "FD c13", "FDa")
-    ts(T.FD[:, 19::20], T.FD[:, 19::20], col(13), None, A.add, None, 8, "FD c13", "FDb")
-    ts(T.W1[:], T.DI[:], col(2), col(7), A.is_equal, A.mult, 1024, "DI c2 c7", "W1")
+    ms(T.FD[:], 0.0, 80, "FD")
+    ms(T.FD[:, 0::20], RST, 4, "FD")
+    ms(T.FD[:, 17::20], C1K, 4, "FD")
+    ms(T.FD[:, 18::20], -C1K, 4, "FD")
+    ts(T.FD[:, 16::20], T.FD[:, 16::20], col(13), -511.5, A.subtract, A.add, 4, "FD c13", "FDa")
+    ts(T.FD[:, 19::20], T.FD[:, 19::20], col(13), None, A.add, None, 4, "FD c13", "FDb")
+    ts(mat("WT"), mat("BI"), col(2), col(7), A.is_equal, A.mult, 64, "BI c2 c7", "WTm")
     ts(T.W2[:], T.DI[:], col(2), col(8), A.is_equal, A.mult, 1024, "DI c2 c8", "W2")
-    ms(T.KC[:, :, 0], -15.0, 8, "KC")
-    ms(T.KC[:, :, 17:20], BIG, 24, "KC")
-    ms(T.KD[:], 0.0, 320, "KD")
-    ms(T.KD[:, 0::20], RST, 16, "KD")
-    ms(T.KD[:, 17::20], C32, 16, "KD")
-    ms(T.KD[:, 18::20], -C32, 16, "KD")
-    for j in range(WQ):
-        ts(col(24 + j), col(1), -16.0, -16.0 - 256.0 * j, A.mult, A.add, 1, "c1", "c%d" % (24 + j))
-        for h in range(NB):
-            o = T.KD[:, 20 * (Q0[h] + j) + 19:20 * (Q0[h] + BAT[h]):20 * WQ]
-            ts(o, o, col(24 + j), None, A.add, None, 8, "KD c%d" % (24 + j), "KD%d_%d" % (h, j))
-    for h in range(NB):
-        ms(T["GR%d" % h][:, :, 0:16], 0.0, 64, "GZ%d" % h)
-    ms(T.TH[:], 0.0, 8, "TH THa")
-    ts(row("RS"), T.J[:, 0:L], 0.0, RST, A.is_equal, A.mult, 256, "J", "RS")
     for u in range(4):
-        cp(T.S[:, 256 * u:256 * u + 256], T.H32[:, 256 * u:256 * u + 256], 256, "H32", "S")
-    ts(col(4), col(2), -1.0, None, A.mult, None, 1, "c2", "c4")
-    for u in range(8):
-        o = T.ONE[:, 2 * u:2 * u + 2, :]
-        act(o, T.DI[:, 2 * u:2 * u + 2, :], AF.Abs, 256, "DI c4", "ONE%d" % u, bias=col(4))
-        act(o, o, AF.Relu, 256, "ONE%d" % u, "ONE%d" % u, scale=-1.0, bias=1.0)
-    ts(mat("N8"), mat("BI"), col(2), -8192.0, A.is_equal, A.mult, 64, "BI c2", "N8")
-    ts(mat("NI"), mat("MI"), col(0), -2048.0, A.is_equal, A.mult, 64, "MI c0", "NI")
-    ts(col(11), col(1), 4.0, None, A.is_lt, None, 1, "c1", "c11")
-    ts(col(12), col(1), col(11), 256.0, A.mult, A.mult, 1, "c1 c11", "c12")
-    ts(mat("SEL4"), mat("BI"), col(2), col(11), A.is_equal, A.mult, 64, "BI c2 c11", "SEL4")
-    ts(mat("SELD"), mat("BI"), col(2), col(12), A.is_equal, A.mult, 64, "BI c2 c12", "SELD")
-    ts(mat("DN"), mat("BI"), 0.0, col(3), A.mult, A.subtract, 64, "BI c3", "DN")
-    ts(col(16), col(0), 16.0, None, A.mult, None, 1, "c0", "c16")
-    ts(T.SELG[:], mat("BI"), col(16), None, A.is_equal, None, 128, "BI c16", "SELG")
-    ts(col(15), col(1), 1.0, None, A.add, None, 1, "c1", "c15")
-    ts(col(23), col(2), 1.0 / 16, None, A.mult, None, 1, "c2", "c23")
-    ts(T.KW[:], mat("BI"), col(2), col(15), A.is_equal, A.mult, 128, "BI c2 c15", "KW")
-    ts(T.GM[:, 8:16], T.GM[:, 0:8], col(23), 2048.0, A.is_equal, A.mult, 8, "GM0 c23", "GM")
-    act(row("BMF"), T.BM[:], AF.Copy, 256, "BM", "BMF")
-    act(row("DG"), T.BM[:], AF.Identity, 256, "BM", "DG", scale=-1.0 / BIG, bias=1.0)
-    act(row("NDG"), T.BM[:], AF.Copy, 256, "BM", "NDG", scale=1.0 / BIG)
-    ts(rb("TRI"), T.J[:, 0:192], col(1), 4096.0, A.is_gt, A.mult, 96, "J c1", "TRI")
-    ts(rb("TRI"), rb("TRI"), 2048.0, None, A.add, None, 96, "TRI", "TRI")
-    ts(rb("D2"), T.J[:, 0:192], col(1), 1.0, A.is_equal, A.add, 96, "J c1", "D2")
-    ms(T.RB[:, R192.index("D2"), 0::16], 0.0, 12, "D2")
-    ts(T.OH[:], T.J[:, 0:528], col(1), None, A.is_equal, None, 264, "J c1", "OH")
-    ms(T.OH[:, 0:16], 0.0, 16, "OH")
-    cp(T.BC[:], T.IOT[:, 0:16], 16, "IOT", "BC")
-    ts(T.DM[:, 16:32], T.DM[:, 0:16], col(1), float(H), A.add, A.add, 16, "DM0 c1", "DM1")
-    ts(T.DM[:, 0:16], T.DM[:, 0:16], col(1), float(B), A.add, A.add, 16, "DM0 DM1 c1", "DM0")
-    for u, (qa, qb) in enumerate(PAIRS):
-        ts(T.PLS[:, u:u + 1], col(1), 16.0 * qb, None, A.add, None, 1, "c1", "PLS%d" % u)
-        ms(T.PLS[:, NP + u:NP + u + 1], qa, 1, "PLT%d" % u)
-    if NP:
-        ts(col(5), col(1), 0.0, None, A.add, None, 1, "c1 " + " ".join("PLS%d PLT%d" % (u, u) for u in range(NP)), "PLS")
-    for t in range(TR):
-        for sg, c in ((t, 17 + t), (16 - t, 20 + t)):
-            ts(T.PI[:, 4:5], T.PI[:, 1:2], float(sg), None, A.add, None, 1, "PI1", "PI4")
-            ts(T.PI[:, 5:6], T.PI[:, 4:5], 15, None, A.bitwise_and, None, 1, "PI4", "PI5")
-            cp(col(c), T.PI[:, 5:6], 1, "PI5", "c%d" % c)
-        ts(col(17 + t), col(17 + t), col(2), None, A.add, None, 1, "c%d c2" % (17 + t), "c%d" % (17 + t))
-        ts(T.ROT[:, t, :], mat("MI"), col(17 + t), None, A.is_equal, None, 128, "MI c%d" % (17 + t), "ROT%d" % t)
-        ts(T.TT[:, t, :], T.J[:, 16 - t:16 - t + L], col(20 + t), 4096.0, A.is_le, A.mult, 128, "J c%d" % (20 + t), "TT%d" % t)
-        for d in range(N):
-            act(T.SE[:, t, reg(d)], T.J[:, 0:CAP], AF.Identity, 48, "J", "SE%d" % t, scale=0.0, bias=-64.0)
-    for d in range(N):
-        act(T.SW[:, reg(d)], T.J[:, 0:CAP], AF.Copy, 48, "J", "SW")
-    for d in range(2):
-        act(T.AR[:, 528 * d:528 * d + 528], T.J[:, 0:528], AF.Identity, 528, "J", "AR ARx", scale=0.0, bias=-8192.0)
+        act(T.W1[:, 4 * u:4 * u + 4, :], T.W2[:, 4 * u:4 * u + 4, :], AF.Identity, 512, "W2", "W1_%d" % u, scale=-2.0)
+    act(T.KC[:, :, 0:16], T.BM20[:, :, 0:16], AF.Identity, 64, "BM20", "KCt", bias=-16.0)
+    fill(T.KC[:, :, 32:35], BIG, 12, "KCx")
+    fill(T.KD[:], 0.0, 144, "KD")
+    fill(T.KD[:, :, 0], RST, 4, "KD")
+    fill(T.KD[:, :, 32], C32, 4, "KD")
+    fill(T.KD[:, :, 33], -C32, 4, "KD")
+    act(col(20), col(1), AF.Identity, 1, "c1", "c20", scale=-128.0)
+    for q in range(4):
+        act(T.KD[:, q, 34:35], col(20), AF.Identity, 1, "c20 KD", "KD%d" % q, bias=-48.0 - 32.0 * q)
+    for h in range(NB):
+        ms(T["GR%d" % h][:, 0::32], 0.0, 33, "GZ%d" % h)
+    act(col(16), col(0), AF.Identity, 1, "c0", "c16", scale=16.0)
+    ts(fm("SELG"), mat("BI"), col(16), None, A.is_equal, None, 128, "BI c16", "SELG")
     cp(T.VF[0:8, 0:H], T.VI[0:8, 0:H], 512, "VIv", "VFv")
     cp(T.VF[0:8, H:H + L], T.VI[0:8, H:H + L], 256, "VIw", "VFw")
-    mm([(T.P6[:], T.SELG[0:8, :], T.VF[0:8, 0:H], True, True, 2048)], "SELG VFv", "P6")
-    act(T.V[:, 0:H], T.P6[:], AF.Copy, 512, "P6", "V")
-    mm([(T.P7[:, 0:L], T.SELG[0:8, :], T.VF[0:8, H:H + L], True, False, 1024), (T.P7[:, 0:L], ID, T.BM[:], False, True, 256)],
-       "SELG VFw ID BM", "P7")
-    scan(row("SC"), row("RS"), T.P7[:, 0:L], 0.0, A.add, A.min, 256, "RS P7", "SC")
+    selg = T.FT[0:8, FMAT.index("SELG"), :]
+    for nm, c in (("IDF", 1.0), ("NIF", -1.0), ("AI", 4.0 * PIT), ("NAI", -4.0 * PIT), ("IDH", 0.5)):
+        act(fm(nm), ID, AF.Identity, 128, "ID", nm, scale=c)
+    for t in range(TR):
+        ts(br("K%d" % t), T.J[:, t:t + L], col(1), None, A.is_equal, None, 128, "J c1", "K%d" % t)
+        ts(br("N%d" % t), T.J[:, t:t + L], col(1), None, A.not_equal, None, 128, "J c1", "N%d" % t)
+    ms(T.PW[:], 0.0, 48, "PW")
+    ms(T.SM[:, 0:16], 0.5, 16, "SMa")
+    ms(T.SM[:, 16:28], 2.0, 12, "SMb")
+    scan(T.PW[:, 0, :], T.SM[:, 0:16], T.PW[:, 2, :], 1.0, A.mult, A.add, 16, "SMa PW", "PWa")
+    scan(T.PW[:, 1, 0:12], T.SM[:, 16:28], T.PW[:, 2, 0:12], -0.25, A.mult, A.add, 12, "SMb PW", "PWb")
+    ms(T.PW[:, 1, 13:14], -0.5, 1, "PW")
+    ms(T.PW[:, 2, 12:16:2], -1024.0, 1, "PW")
+    tt(T.PW[:], T.PW[:], br("K0", 0, 48), A.mult, 96, "PW PWa PWb K0", "PW")
+    for u, c in enumerate((23, 25, 26)):
+        op("v", lambda u=u, c=c: V.tensor_reduce(col(c), T.PW[:, u, :], AxisListType.X, A.add), ("v", 16), "PW", "c%d" % c)
+    act(col(24), col(23), AF.Identity, 1, "c23", "c24", scale=0.5)
+    fill(br("CB"), C1, L, "CB")
+
+    def signs(o, src, n, r, w, bank, k="a"):
+        act(T.HY[:, 0:n], src, AF.Identity, n, r + " c23 c24", "HY", k=k, scale=col(23), bias=col(24))
+        act(T.HV[:, 0:n], T.HY[:, 0:n], AF.Identity, n, "HY", "HV", bias=C1)
+        mm([(T[bank][:, a:a + L], ID, br("CB"), a == 0, False, L) for a in range(0, n, L)], "ID CB", bank)
+        mm([(T[bank][:, 0:n], fm("NIF"), T.HV[:, 0:n], False, False, 4 * n), (T[bank][:, 0:n], IDF, T.HY[:, 0:n], False, True, 4 * n)],
+           "NIF IDF HV HY", bank)
+        act(o, T[bank][:, 0:n], AF.Sign, n, bank, w)
+
+    mm([(T.P6[:], selg, T.VF[0:8, 0:H], True, True, 2048)], "SELG VFv", "P6")
+    signs(T.P6[:], T.P6[:], H, "P6", "P6", "P6")
+    ts(T.XB[:, 0:H], T.XB[:, 0:H], 1.0, None, A.add, None, 256, "XB", "XB")
+    for u in range(2):
+        tt(T.XR[:, own + L * u:own + L * u + L], T.XB[:, L * u:L * u + L], T.P6[:, L * u:L * u + L], A.mult, L, "XB P6", "XRo")
+    for d in [rank] + peers:
+        a = PIT * d + (H if d == rank else MSG)
+        const(T.XR[:, a:PIT * d + PIT], 0, PIT * d + PIT - a, "XRo" if d == rank else "XRd")
+    remote(lambda d: T.XR[:, own:own + MSG], T.XR[:, own:own + MSG], "XRo XRd G", "XRx", same=True)
+    iota(T.DM[:, 0:16], [[16, 16]], 0, 0, 16, "DM0 gordq")
+    iota(mat("OI"), [[0, 4], [1, 32]], 0, 0, 128, "OI gordq")
+    iota(mat("PT"), [[16, 8], [0, 4], [4, 4]], 0, 0, 128, "PT gordq")
+    iota(br("CM", 0, 128), [[0, 8], [1, 4], [0, 4]], 0, 0, 128, "CM gordq")
+    iota(T.LF[:, 0:16], [[1, 16]], 0, 0, 16, "LF0 gordq")
+    for d in (1, 2, 3):
+        iota(T.LF[:, OFF[4 * d - 4]:OFF[4 * d]], [[4, 4], [1, 4 - d]], 0, 0, 12, "LF%d gordq" % d)
+    iota(T.IOT[:], [[1, Q + 16]], 0, 0, Q + 16, "IOT IOTx gordq")
+    ts(row("RS"), T.J[:, 0:L], 0.0, RST, A.is_equal, A.mult, 256, "J", "RS")
+    mm([(T.P7[:, 0:L], selg, T.VF[0:8, H:H + L], True, False, 1024), (T.P7[:, 0:L], ID, br("BM"), False, True, 256)], "SELG VFw ID BM", "P7")
+    pick(row("SC"), row("RS"), T.P7[:, 0:L], 256, "RS P7", "SC")
     cp(T.WI[:], row("SC", 15, L, 16), 16, "SC", "WI")
+    for u in range(4):
+        cp(T.S[:, 256 * u:256 * u + 256], T.H32[:, 256 * u:256 * u + 256], 256, "H32", "S")
+    act(br("RSB"), row("RS"), AF.Copy, 256, "RS", "RSB")
+    ts(mat("N8"), mat("BI"), col(2), 8192.0, A.is_equal, A.mult, 64, "BI c2", "N8")
+    ts(mat("ON2"), mat("N8"), 0.25, None, A.mult, None, 64, "N8", "ON2")
+    act(fm("ONF"), mat("N8"), AF.Identity, 128, "N8", "ONF", scale=1.0 / 8192)
+    for nm, c in (("KI", 1024.0), ("NI", -1.0), ("I3", 512.0)):
+        ts(mat(nm), ID, c, None, A.mult, None, 64, "ID", nm)
+    ts(col(11), col(1), 4.0, None, A.is_lt, None, 1, "c1", "c11")
+    ts(col(12), col(1), col(11), 256.0, A.mult, A.mult, 1, "c1 c11", "c12")
+    act(col(15), col(1), AF.Identity, 1, "c1", "c15", bias=1.0)
+    act(col(17), T.COD[:, 2:3], AF.Identity, 1, "CO", "c17", scale=1.0 / 16)
+    ts(col(22), col(1), -13.0, col(26), A.add, A.mult, 1, "c1 c26", "c22")
+    act(col(18), col(22), AF.Identity, 1, "c22", "c18", scale=-1.0 / 2048)
+    ts(col(19), col(1), float(rank), -8192.0, A.is_equal, A.mult, 1, "c1", "c19")
+    act(col(5), col(1), AF.Identity, 1, "c1", "c5", scale=2.0, bias=1.0)
+    act(col(21), col(14), AF.Identity, 1, "c13", "c21", scale=-0.25, bias=-0.375)
+    for nm, c in (("SEL4", 11), ("SELD", 12), ("CC4", 17), ("SV", 25), ("KF", 26)):
+        ts(mat(nm), mat("BI"), col(2), col(c), A.is_equal, A.mult, 64, "BI c2 c%d" % c, nm)
+    for nm, c in (("S12", 18), ("KW", 15)):
+        act(fm(nm), fm("ONF"), AF.Identity, 128, "ONF c%d" % c, nm, scale=col(c))
+    ts(mat("NEG"), mat("SEL4"), 65536.0, None, A.mult, None, 64, "SEL4", "NEG")
+    ts(mat("DN"), mat("BI"), 0.0, col(3), A.mult, A.subtract, 64, "BI c3", "DN")
+    for q in range(4):
+        ts(fm("PM%d" % q), mat("PT"), float(q), col(0), A.add, A.is_equal, 128, "PT c0", "PM%d" % q)
+    ts(br("CM", 0, 128), br("CM", 0, 128), col(4), BIG, A.not_equal, A.mult, 64, "CM c3", "CM")
+    const(T.RS4[:, 0:32], 0, 32, "RS4")
+    fill(T.RS4[:, 0:32:4], RST, 8, "RS4")
+    ts(T.OH[:, 0:128], mat("OI"), col(5), None, A.is_equal, None, 64, "OI c5", "OH")
+    for a, n in ((128, 128), (256, 256), (512, 512), (1024, 1024), (2048, GW - 2048)):
+        dma("s", T.OH[:, a:a + n], T.OH[:, 0:n], n // 4, "OH", "OH")
+    fill(T.BM22[:, :, 16:22], BIG, 24, "BM22x")
+    act(T.BM22[:, :, 0:16], T.BM20[:, :, 0:16], AF.Copy, 64, "BM20", "BM22")
+    const(T.XQ2[:, :, 16:22], 0, 96, allh("XQ2%d"))
+    const(T.FE[:], 0, 88, "FE")
+    for sl, c in ((0, RST), (17, C1), (18, -C1), (19, -255.5), (20, C512), (21, -C512)):
+        fill(T.FE[:, sl::22], c, 4, "FE")
+    fill(T.FE[:, 16::22], col(21), 4, "FE", "c21")
+    ts(rb("TRI"), T.J[:, 0:192], col(1), 8192.0, A.is_gt, A.mult, 96, "J c1", "TRI")
+    ts(rb("TR2"), T.J[:, 0:192], col(1), -2048.0, A.is_equal, A.mult, 96, "J c1", "TR2")
+    mm([(T.P6[:, 0:192], ID, rb("TRI"), True, False, 192), (T.P6[:, 0:192], ID, rb("TR2"), False, True, 192)], "ID TRI TR2", "P6")
+    act(rb("TRI"), T.P6[:, 0:192], AF.Identity, 192, "P6", "TRI", bias=1024.0)
+    act(rb("TR2"), T.P6[:, 0:192], AF.Identity, 192, "P6", "TR2", bias=2048.0)
+    act(br("BC", 0, 64), br("BM", 0, 64), AF.Identity, 64, "BM", "BC", bias=2048.0)
+    for d in range(N):
+        for t in range(TR):
+            const(T.SE[:, t, reg(d)], 0, CAP, "SE%d" % t)
+        const(T.SW[:, reg(d)], Q, CAP, "SW")
+    ts(br("TT"), T.J[:, 0:L], col(1), 4096.0, A.is_lt, A.mult, 128, "J c1", "TT")
+    mm([(T.P7[:, 0:L], ID, br("TT"), True, False, L), (T.P7[:, 0:L], ID, br("K0"), False, True, L)], "ID TT K0", "P7")
+    act(br("TT"), T.P7[:, 0:L], AF.Copy, L, "P7", "TT")
+    cp(T.LA[:], T.LF[:], 40, "LF0 LF1 LF2 LF3", "LA")
+    ts(T.DM[:, 16:32], T.DM[:, 0:16], col(1), float(MSG), A.add, A.add, 16, "DM0 c1", "DM1")
+    ts(T.DM[:, 0:16], T.DM[:, 0:16], col(1), B + 0.5, A.add, A.add, 16, "DM0 DM1 c1", "DM0")
 
-    def xslot(h):
-        return T.M[:, 16 * Q0[h]:16 * (Q0[h] + BAT[h]), 0]
+    def lanes(n, h):
+        return br(n, 64 * h, 64 * h + 64)
 
-    def quarter(h):
-        n = 16 * BAT[h]
-        o = T.XQ[:, Q0[h]:Q0[h] + BAT[h], 0:16]
-        if CFG["xq"] == "v":
-            ts(o, xslot(h), 766.5, None, A.add, None, n // 2, "x%d" % h, "XQ%d" % h)
+    def quarter(o, h, w, e):
+        if e == "v":
+            ts(o, lanes("X", h), 766.5, None, A.add, None, 32, "x%d" % h, w)
         else:
-            act(o, xslot(h), AF.Identity, n, "x%d" % h, "XQ%d" % h, bias=766.5)
+            act(o, lanes("X", h), AF.Identity, 64, "x%d" % h, w, bias=766.5)
 
     def column(h, s):
-        nq, q0 = BAT[h], Q0[h]
-        n, n2, o = 16 * nq, 20 * nq, 20 * q0
-        XF, xf = T[XFN[h]], XFN[h]
-        quarter(h)
-        mm([(XF[:, 0:n2], ID, T.BM20[:, 0:nq, :], True, False, n2)], "ID BM20", xf)
-        mm([(XF[:, 0:n2], mat("A4"), T.XQ[:, q0:q0 + nq, :], False, True, n2)], "A4 XQ%d" % h, xf)
-        scan(T.FS[:, o:o + n2], T.FD[:, 0:n2], XF[:, 0:n2], 0.0, A.add, A.min, n2, "FD FDa FDb " + xf, "FS%d" % h)
-        mm([(XF[:, 256:256 + n], ID, xslot(h), True, True, n)], "ID x%d" % h, xf)
-        bo = (T.RT if s == ST - 1 else T.BF)[:, q0:q0 + nq]
-        on = ("RTb%d" if s == ST - 1 else "BF%d") % h
-        tt(bo, T.FS[:, o + 15:o + n2:20], T.FS[:, o + 19:o + n2:20], A.subtract, 2 * nq, "FS%d" % h, on)
-        c = 16 * s + q0
-        cp(T.B16[:, c:c + nq], bo, nq, on, "B16_%d_%d" % (s, h))
+        KB, kb, c = T["KB%d" % h], "KB%d" % h, 16 * s + 4 * h
+        part = lambda m, X, a, st, sp: [(KB[:, 0, 48 + q:128:4], mat(m), X[:, a + st * q:a + st * q + 4, :], False, sp and q == 3, 20)
+                                        for q in range(4)]
+        mm([(KB[:, 0, 48:128], ID, T.BM20[:], True, False, 80)], "ID BM20", kb)
+        if CFG["xq"][s] == "d":
+            ts(T.XQ[:, 16 * h:16 * h + 16, 0:4], lanes("D", h), 766.5, 766.5, A.add, A.max, 32, "D%d" % h, "XQ%d" % h)
+            ts(T.XN[:, 16 * h:16 * h + 16, 0:4], lanes("D", h), -766.5, -766.5, A.add, A.min, 32, "D%d" % h, "XN%d" % h)
+            mm(part("A4", T.XQ, 16 * h, 4, False), "A4 XQ%d" % h, kb)
+            mm(part("NA", T.XN, 16 * h, 4, True), "NA XN%d" % h, kb)
+        else:
+            mm(part("NA", T.XN, 64, 0, False), "NA XNc", kb)
+            quarter(T.XQ[:, 16 * h:16 * h + 16, 0:4], h, "XQ%d" % h, CFG["xq"][s])
+            mm(part("A4", T.XQ, 16 * h, 4, True), "A4 XQ%d" % h, kb)
+        o = 80 * h
+        pick(T.FB[:, o:o + 80], T.FD[:], KB[:, 0, 48:128], 80, "FD FDa FDb " + kb, "FB%d" % h)
+        tt(T.BF[:, c:c + 4], T.FB[:, o + 15:o + 80:20], T.FB[:, o + 19:o + 80:20], A.subtract, 8, "FB%d" % h, "BF%d" % c)
+        cp(T.B16[:, c:c + 4], T.BF[:, c:c + 4], 4, "BF%d" % c, "B16_%d" % c)
 
     def step(h, s, first):
-        nq, q0 = BAT[h], Q0[h]
-        n, n2, o, nw = 16 * nq, 20 * nq, 20 * q0, nq // WQ
-        GR, KEY, XF = T["GR%d" % h], T["KEY%d" % h], T[XFN[h]]
-        key, xf, xn = "KEY%d" % h, XFN[h], "x%d" % h
-        c = 16 * s + q0
+        GR, KB, XJ, M = T["GR%d" % h], T["KB%d" % h], T["XJ%d" % (h % 2)], T.M
+        kb, xj, xn, gr = "KB%d" % h, "XJ%d" % (h % 2), "x%d" % h, "GR%d" % h
+        c, a = 16 * s + 4 * h, 64 * (h // 2)
         win, wn = (T.H32[:], "H32") if first else (T.S[:, 0:B], "S")
-        cp(T.HS[:, 16 * q0:16 * q0 + n], win.indirect(T.B16[:, c:c + nq]), n, "%s B16_%d_%d" % (wn, s, h), "HS%d" % h, k="vg")
-        mm([(KEY[:, 0:nq, 0:20], ID, T.KC[:, 0:nq, :], True, False, n2)], "ID KC", key)
-        nch = CFG["nch"]
-        cut = [nq * j // nch for j in range(nch + 1)]
-        allg = []
-        for j in range(nch):
-            a, b = cut[j], cut[j + 1]
-            m = 16 * (b - a)
-            vs = nq - CFG["vshare"][s][h]
-            ends = sorted(set(list(range(a, b + 1, WQ)) + ([vs] if a < vs < b else [])))
-            for a2, b2 in zip(ends[:-1], ends[1:]):
-                nm = " ".join("GR%d_%d" % (h, q) for q in range(a2, b2))
-                off = 16 + 256 * (a2 % WQ)
-                go, gi = GR[:, a2 // WQ, off:off + 256 * (b2 - a2)], T.G[:].indirect(T.HS[:, 16 * (q0 + a2):16 * (q0 + b2)])
-                if a2 < vs:
-                    act(go, gi, AF.Copy, 256 * (b2 - a2), "G HS%d" % h, nm + " gord%d" % h, k="ag")
-                else:
-                    cp(go, gi, 256 * (b2 - a2), "G HS%d" % h, nm, k="vg")
-            gr = " ".join("GR%d_%d" % (h, q) for q in range(a, b))
-            allg.append(gr)
-            pes = CFG["pes"]
-            if WQ == 1 or j == nch - 1:
-                ga = a if WQ == 1 else 0
-                for u in range(pes * WQ):
-                    w, p0 = u // pes, 16 * (u % pes) // pes
-                    off = 16 + 256 * w
-                    mm([(KEY[:, ga + w:b:WQ, 1:17], T.W2[:, p, :], GR[:, ga // WQ:b // WQ, off + 16 * p:off + 16 + 16 * p], False, False,
-                         16 * (b - ga) // WQ) for p in range(p0, p0 + 16 // pes)], "W2 " + (gr if WQ == 1 else " ".join(allg)), key)
-            for k in range(16):
-                tt(T.M[:, 16 * (q0 + a):16 * (q0 + b), 1 + k], GR[:, a // WQ:b // WQ, 16 + k:16 + 256 * WQ:16],
-                   XF[:, 256 + 16 * a:256 + 16 * b], A.max, m, gr + " " + xf, "M%d_%d_%d" % (h, j, k))
-            for u in range(pes):
-                mm([(KEY[:, a:b, 0:17], T.W1[:, p, :], T.M[:, 16 * (q0 + a) + p:16 * (q0 + b):16, :], False, j == nch - 1 and p == 15,
-                     17 * (b - a))
-                    for p in range(16 * u // pes, 16 * (u + 1) // pes)],
-                   "W1 " + xn + "".join(" M%d_%d_%d" % (h, j, k) for k in range(16)), key)
-        kd = "KD" + "".join(" KD%d_%d" % (h, j) for j in range(WQ))
-        if CFG["keymode"] == "act":
-            act(T.KP[:, o:o + n2], KEY[:, 0:nq, 0:20], AF.Copy, n2, key, "KP%d" % h)
-            scan(T.SO[:, o:o + n2], T.KD[:, o:o + n2], T.KP[:, o:o + n2], 0.0, A.add, A.min, n2, kd + " KP%d" % h, "SO%d" % h)
-            so = "SO%d" % h
+        hs = T.HS[:, 64 * h:64 * h + 64]
+        cp(hs, win.indirect(T.B16[:, c:c + 4]), 64, "%s B16_%d" % (wn, c), "HS%d" % h, k="vg")
+        mm([(KB[:, :, 0:35], ID, T.KC[:], True, False, 140), (KB[:, :, 0:16], mat("WT"), lanes("X", h), False, False, 64)],
+           "ID KCk KCt KCx WTm " + xn, kb)
+        if s == 0 and h < CFG["vs0"]:
+            cp(GR[:, 33:2081:2], T.G[:].indirect(hs), 1024, "G HS%d" % h, gr, k="vg")
         else:
-            for q in range(nq):
-                u = o + 20 * q
-                scan(T.SO[:, u:u + 20], T.KD[:, u:u + 20], KEY[:, q, 0:20], 0.0, A.add, A.min, 20, kd + " " + key, "SO%d_%d" % (h, q))
-            so = " ".join("SO%d_%d" % (h, q) for q in range(nq))
-        tt(T.SV[:, q0:q0 + nq], T.SO[:, o + 16:o + n2:20], T.SO[:, o + 19:o + n2:20], A.subtract, 2 * nq, so, "SVa%d" % h)
-        tt(T.SV[:, 16 + q0:16 + q0 + nq], T.SO[:, o + 16:o + n2:20], T.SO[:, o + 18:o + n2:20], A.is_ge, 2 * nq, so, "SVb%d" % h)
-        ixn = "IXF_%d_%d" % (s, h)
-        tt(T.IXF[:, c:c + nq], T.SV[:, q0:q0 + nq], T.SV[:, 16 + q0:16 + q0 + nq], A.mult, 2 * nq, "SVa%d SVb%d" % (h, h), ixn)
-        if WQ == 1:
-            cp(T.IX[:, 2 * q0:2 * q0 + 2 * nq:2], T.IXF[:, c:c + nq], nq, ixn, "IX%d" % h)
-        ix4 = "IX4_%d_%d" % (s, h)
-        cp(T.IX4[:, c:c + nq], T.IXF[:, c:c + nq], nq, ixn, ix4)
-        rd = " ".join(allg) + " GZ%d %s " % (h, xn) + ("IX%d" % h if WQ == 1 else ix4)
-        for a in range(nw):
-            ls = T.IX[:, 2 * (q0 + a):2 * (q0 + a) + 1] if WQ == 1 else T.IX4[:, c + 2 * a:c + 2 * a + 2]
-            l0, l1 = 16 * (q0 + a * WQ), 16 * (q0 + a * WQ + WQ)
-            tt(T.D[:, l0:l1], GR[:, a, :].indirect(ls), T.M[:, l0:l1, 0], A.subtract, 16 * WQ, rd, "D%d_%d" % (h, a), k="vg")
-        act(xslot(h), T.D[:, 16 * q0:16 * q0 + n], AF.Abs, n, " ".join("D%d_%d" % (h, a) for a in range(nw)), xn)
+            act(GR[:, 33:2081:2], T.G[:].indirect(hs), AF.Copy, 1024, "G HS%d" % h, gr, k="ag")
+        mm([(XJ[:, a + q:a + 64:4], ID, br("X", 64 * h + 16 * q, 64 * h + 16 * q + 16), True, True, 16) for q in range(4)], "ID " + xn, xj)
+        pes = CFG["pes"]
+        for u in range(pes):
+            mm([(KB[:, :, 16:32], T.W2[:, p, :], GR[:, 33 + 128 * p:161 + 128 * p:2], False, False, 64)
+                for p in range(16 * u // pes, 16 * (u + 1) // pes)], "W2 " + gr, kb)
+        for k in range(16):
+            tt(M[:, h, k::16], GR[:, 33 + 2 * k:2081:32], XJ[:, a:a + 64], A.max, 64, gr + " " + xj, "M%d_%d" % (h, k))
+        for u in range(pes):
+            mm([(KB[:, :, 16:32], T.W1[:, p, :], M[:, h, 64 * p:64 * p + 64], False, p == 15, 64)
+                for p in range(16 * u // pes, 16 * (u + 1) // pes)],
+               "W1_0 W1_1 W1_2 W1_3" + "".join(" M%d_%d" % (h, k) for k in range(16)), kb)
+        for q in range(4):
+            pick(T.SO[:, 4 * h + q, 0:35], T.KD[:, q, 0:35], KB[:, q, 0:35], 35, "KD KD%d %s" % (q, kb), "SO%d_%d" % (h, q))
+        tt(T.IXF[:, 4 * h:4 * h + 4], T.SO[:, 4 * h:4 * h + 4, 31], T.SO[:, 4 * h:4 * h + 4, 34], A.subtract, 8,
+           " ".join("SO%d_%d" % (h, q) for q in range(4)), "IXF%d" % h)
+        cp(T.IX[:, c:c + 4], T.IXF[:, 4 * h:4 * h + 4], 4, "IXF%d" % h, "IX%d" % c)
+        tt(lanes("D", h), GR[:].indirect(T.IX[:, c:c + 4]), lanes("X", h), A.subtract, 64,
+           "%s GZ%d IX%d %s" % (gr, h, c, xn), "D%d" % h, k="vg")
+        act(lanes("X", h), lanes("D", h), AF.Abs, 64, "D%d" % h, xn)
+
+    def words(s, bank, nm):
+        tt(T.MK[:, L * s:L * s + L], T.OH[:].indirect(T.IX[:, 16 * s:16 * s + 16]), T.HF[:, L * s:L * s + L], A.mult, L,
+           "OH HF%d" % s + "".join(" IX%d" % c for c in range(16 * s, 16 * s + 16, 4)), "MK%d" % s, k="vg")
+        mm([(T[bank][:, 0:L], ID, br("BM"), True, False, 256)], "ID BM", bank)
+        mm([(T[bank][:, 0:L], fm("ONF"), T.MK[:, L * s:L * s + L], False, True, 1024)], "ONF MK%d" % s, bank)
+        pick(row(nm), row("RS"), T[bank][:, 0:L], 256, "RS " + bank, nm)
+        sv = row(nm, 15, L, 16)
+        act(T.SF[:], sv, AF.Copy, 16, nm, "SF", scale=37.0)
+        tt(T.WP[:, 0:16], T.WI[:], sv, A.mult, 32, "WI " + nm, "WPa")
+        tt(T.WT[:], T.WI[:], T.SF[:], A.add, 32, "WI SF", "WT")
+        ts(T.WP[:, 16:32], T.WP[:, 0:16], 5, None, A.arith_shift_right, None, 16, "WPa", "WPb")
+        tt(T.WP[:, 32:48], T.WP[:, 16:32], T.WT[:], A.add, 32, "WPb WT", "WPc")
+        ts(T.WI[:], T.WP[:, 32:48], Q - 1, None, A.bitwise_and, None, 16, "WPc", "WI")
+
+    def in_order(s):
+        a = 16 * s
+        mm([(T.P6[:, 0:128], ID, br("CM", 0, 128), True, False, 128)] +
+           [(T.P6[:, q:128:4], fm("PM%d" % q), T.BF[:, a:a + 32], False, q == 3, 256) for q in range(4)],
+           "ID CM PM0 PM1 PM2 PM3 " + " ".join("BF%d" % c for c in range(a, a + 32, 4)), "P6")
+        for q in range(4):
+            pick(T.SB[:, a:a + 32, q], T.RS4[:, 0:32], T.P6[:, q:128:4], 32, "RS4 P6", "SB%d" % q)
+        cp(T.BO[:, a:a + 32], T.SB[:, a + 3:a + 32:4, :], 32, allh("SB%d"), "BO%d" % s)
+        for u in (s, s + 1):
+            act(T.HF[:, L * u:L * u + L], T.S[:, 0:B].indirect(T.BO[:, 16 * u:16 * u + 16]), AF.Copy, L, "S BO%d" % s, "HF%d" % u, k="ag")
+
+    def last_columns(t):
+        act(T.B2[:], T.SB[:, 51::4, :], AF.Identity, 16, allh("SB%d"), "B2", scale=2.0)
+        act(T.B21[:], T.SB[:, 51::4, :], AF.Identity, 16, allh("SB%d"), "B21", scale=2.0, bias=1.0)
+        cp(T.LB[:, 0:16], T.B2[:], 16, "B2", "LB0")
+        for d in (1, 2, 3):
+            cp(T.LB[:, OFF[4 * d - 4]:OFF[4 * d]], T.B2[:, :, d:4], 12, "B2", "LB%d" % d)
+        tt(T.B2R[:, 0:L], T.IOT[:].indirect(T.LB[:, 0:16]), br("TT"), A.add, L, "IOT IOTx LB0 TT", "B2Ra", k="vg")
+        act(T.B2R[:, L:640], T.IOT[:].indirect(T.LB[:, 16:40]), AF.Copy, 384, "IOT IOTx LB1 LB2 LB3", "B2Rb", k="ag")
+        tt(row("HM"), T.S[:, 0:B].indirect(T.BO[:, 48:64]), br("N%d" % t), A.mult, L, "S BO2 N%d" % t, "HM", k="vg")
+
+    def query(h, t):
+        KB, kb, xn = T["KB%d" % h], "KB%d" % h, "x%d" % h
+        pn = "P6" if h % 2 == 0 else "P7"
+        PB, a, o = T[pn], 64 * h, 88 * h
+        fr = lambda n: row(n, a, a + 64)
+        xq = T.XQ2[:, 4 * h:4 * h + 4, 0:16]
+        quarter(xq, h, "XQ2%d" % h, CFG["xq"][4])
+        if t < TR - 1:
+            act(lanes("XF", h), lanes("X", h), AF.Identity, 64, xn, "XF%d" % h, bias=1.0)
+        mm([(KB[:, 1, 40:128], ID, T.BM22[:], True, False, 88)], "ID BM22 BM22x", kb)
+        mm([(KB[:, 1, 40:128], mat("CC4"), T.XQ2[:, 4 * h:4 * h + 4, :], False, True, 88)], "CC4 XQ2%d" % h, kb)
+        pick(T.F2[:, o:o + 88], T.FE[:], KB[:, 1, 40:128], 88, "FE " + kb, "F2%d" % h)
+        sl = lambda u: T.F2[:, o + u:o + 88:22]
+        mm([(KB[:, 2, 48:52], fm("AI"), sl(16), True, False, 256), (KB[:, 2, 48:52], fm("NAI"), sl(18), False, False, 256),
+            (KB[:, 2, 48:52], IDF, sl(18), False, False, 256), (KB[:, 2, 48:52], fm("NIF"), sl(21), False, True, 256)],
+           "AI NAI IDF NIF F2%d" % h, kb)
+        ts(T.XI[:, 4 * h:4 * h + 4], KB[:, 2, 48:52], 1.5 * PIT, None, A.add, None, 4, kb, "XI%d" % h)
+        for nm, f in (("RD", AF.Abs), ("HI", AF.Sign)):
+            act(lanes(nm, h), T.XR[:].indirect(T.XI[:, 4 * h:4 * h + 4]), f, 64, "XRo XRx XRd XI%d" % h, "%s%d" % (nm, h), k="ag")
+        dl = KB[:, 2, 64:128]
+        mm([(dl, mat("NI"), lanes("X", h), True, False, 64), (dl, ID, lanes("RD", h), False, True, 64)], "ID NI RD%d %s" % (h, xn), kb)
+        act(lanes("RA", h), dl, AF.Abs, 64, kb, "RA%d" % h, bias=-1.0)
+        mm([(PB[:, 0:64], ID, mat("DN", 64), True, False, 64)], "ID DN", pn)
+        mm([(PB[:, 0:64], mat("CC"), xq, False, True, 64)], "CC XQ2%d" % h, pn)
+        ts(T.TQ[:, a:a + 64], PB[:, 0:64], C4, C4, A.add, A.subtract, 64, pn, "TQ%d" % h)
+        tt(lanes("MQ", h), T.TQ[:, a:a + 64], PB[:, 0:64], A.is_equal, 64, "TQ%d %s" % (h, pn), "MQ%d" % h)
+        scan(lanes("CN", h), lanes("MQ", h), lanes("MQ", h), 0.0 if h == 0 else br("CN", a - 1, a), A.add, A.max, 32,
+             "MQ%d" % h + (" CN%d" % (h - 1) if h else ""), "CN%d" % h)
+        mm([(PB[:, 128:192], mat("I3"), lanes("MQ", h), True, False, 64), (PB[:, 128:192], ID, lanes("CN", h), False, True, 64)],
+           "I3 ID MQ%d CN%d" % (h, h), pn)
+        act(lanes("SP", h), PB[:, 128:192], AF.Relu, 64, pn, "SP%d" % h, bias=-512.0 - CAP)
+        act(lanes("MC", h), PB[:, 128:192], AF.Relu, 64, pn, "MC%d" % h, bias=-512.0)
+        vv, an = KB[:, 1, 64:128], KB[:, 3, 64:128]
+        mm([(vv, ID, br("BC", 0, 64), True, False, 64), (vv, mat("SV"), lanes("HI", h), False, True, 64)], "ID BC SV HI%d" % h, kb)
+        pick(fr("VA"), row("RS", 0, 64), vv, 64, "RS " + kb, "VA%d" % h)
+        mm([(an, ID, br("BM", 0, 64), True, False, 64), (an, mat("THM"), lanes("MQ", h), False, False, 64),
+            (an, mat("NEG"), lanes("SP", h), False, False, 64)], "ID BM THM NEG MQ%d SP%d" % (h, h), kb)
+        mm([(an, mat("N8"), lanes("RA", h), False, True, 64)], "N8 RA%d" % h, kb)
+        pick(fr("AN"), row("RS", 0, 64), an, 64, "RS " + kb, "AN%d" % h)
+        mm([(PB[:, 64:128], ID, br("BM", 0, 64), True, False, 64), (PB[:, 64:128], mat("SELD"), lanes("MQ", h), False, False, 64),
+            (PB[:, 64:128], mat("SEL4"), lanes("MC", h), False, True, 64)], "ID BM SELD SEL4 MQ%d MC%d" % (h, h), pn)
+        pick(fr("FS"), row("RS", 0, 64), PB[:, 64:128], 64, "RS " + pn, "FS%d" % h)
+
+    def store(t):
+        last = t == TR - 1
+        R, rr = T.R[:, t, :], "R%d R%dx" % (t, t)
+        if last:
+            ts(rb("RQ"), R, 766.5, None, A.add, None, 96, rr, "RQ")
+        else:
+            act(rb("RX"), R, AF.Abs, 192, rr, "RX")
+            ts(rb("RQ"), rb("RX"), 765.5, None, A.add, None, 96, "RX", "RQ")
+        mm([(T.P6[:, 0:192], ID, br("BM", 0, 192), True, False, 192)], "ID BM", "P6")
+        mm([(T.P6[:, 0:192], mat("CC"), rb("RQ"), False, True, 192)], "CC RQ", "P6")
+        pick(rf("SO"), row("RS", 0, 192), T.P6[:, 0:192], 192, "RS P6", "SOo")
+        ts(T.PL[:, 0:12], rf("SO", 15, 192, 16), col(14), None, A.subtract, None, 12, "SOo c13", "PLa")
+        ts(T.PL[:, 16:28], T.PL[:, 0:12], 2, H - 1, A.arith_shift_right, A.bitwise_and, 12, "PLa", "PLb")
+        cp(T.PL16[:, 0:12], T.PL[:, 16:28], 12, "PLb", "PL16")
+        cp(T.PLF[:, 0:12], T.PL[:, 16:28], 12, "PLb", "PLF")
+        act(rf("PR"), T.IOT[:].indirect(T.PL16[:, 0:12]), AF.Copy, 192, "IOT IOTx PL16", "PR", k="ag")
+        act(rf("PB"), T.PLF[:, 0:12].indirect(T.LA[:, 0:12]), AF.Copy, 192, "PLF LA", "PB", k="ag")
+        if last:
+            act(rb("JS"), rf("RW"), AF.Sign, 192, "RW RWx", "JS", bias=0.5 - Q)
+        else:
+            act(rb("JS"), R, AF.Sign, 192, rr, "JS THa", accum_out=T.TH[:, 4:5])
+            mm([(T.P7[:, 0:1], fm("S12"), T.TH[:, 4:5], True, True, 256)], "S12 THa", "P7")
+            cp(T.THI[:, 0:1], T.P7[:, 0:1], 1, "P7", "THI0")
+            ts(T.THI[:, 1:2], T.THI[:, 0:1], 7, None, A.bitwise_and, None, 1, "THI0", "THI1")
+            ts(T.XR[:, own + H:own + H + 1], T.THI[:, 1:2], col(19), None, A.mult, None, 1, "THI1 c19", "XRo")
+        mm([(T.P6[:, 0:192], ID, rb("TRI" if last else "TR2"), True, False, 192), (T.P6[:, 0:192], IDF, rf("PB"), False, False, 768)],
+           "ID TRI TR2 IDF PB", "P6")
+        mm([(T.P6[:, 0:192], fm("NIF"), rf("PR"), False, False, 768)], "NIF PR", "P6")
+        mm([(T.P6[:, 0:192], mat("KI" if last else "KF"), rb("JS"), False, True, 192)], "KI KF JS", "P6")
+        act(rb("AB"), T.P6[:, 0:192], AF.Abs, 192, "P6", "AB", scale=4096.0)
+        pick(rb("ES"), br("RSB", 0, 192), rb("AB"), 96, "RSB AB", "ES")
+        tt(T.SM[:, 0:12], T.DM[:, 16:28], rb("ES", 15, 192, 16), A.subtract, 24, "ES DM1", "SMa")
+        tt(T.SM[:, 16:28], T.SM[:, 0:12], T.PLF[:, 0:12], A.max, 24, "SMa PLF", "SMb")
+        cp(T.LS[:, 0::2], T.SM[:, 16:28], 12, "SMb", "LS")
+        for q in range(11, -1, -1):
+            ls, src = T.LS[:, 2 * q:2 * q + 1], T.R[:, t, 16 * q:16 * q + 16]
+            if last:
+                cp(T.XB[:].indirect(ls), src, 16, "LS " + rr, "XB", k="vs")
+                cp(T.YV[:].indirect(ls), rf("RW", 16 * q, 16 * q + 16), 16, "LS RW RWx", "YV", k="vs")
+            else:
+                cp(T.XR[:, own:own + PIT].indirect(ls), src, 16, "LS " + rr, "XRo", k="vs")
+        if not last:
+            remote(lambda d: T.XR[:, own:own + MSG], T.XR[:, own:own + MSG], "XRo", "XRx", same=True)
+        if t == TR - 2:
+            act(T.XB[:, 0:H], T.XR[:, own:own + H], AF.Abs, H, "XRo", "XB")
+            ts(T.XB[:, 0:H], T.XB[:, 0:H], -1.0, None, A.add, None, 256, "XB", "XB")
+            act(T.SG[:], T.XR[:, own:own + H], AF.Sign, H, "XRo", "SG")
+            mm([(T.P7[:], mat("SV"), T.SG[:], True, True, H)], "SV SG", "P7")
+            act(T.YV[:, 0:H], T.P7[:], AF.Identity, H, "P7", "YV", bias=2048.0)
 
     for h in range(NB):
-        a = 16 * Q0[h]
         tag[0] = h
-        cp(xslot(h), T.XLD[:, a:a + 16 * BAT[h]], 8 * BAT[h], "XL", "x%d" % h)
         column(h, 0)
     mine = slice(CAP * rank, CAP * rank + CAP)
+
+    def items(t):
+        remote(lambda d: T.SE[:, t, reg(d)], T.R[:, t, mine], "SE%d" % t, "R%dx" % t)
+        dma("s", T.R[:, t, mine], T.SE[:, t, reg(rank)], 12, "SE%d" % t, "R%d" % t)
+
     for t in range(TR):
         last = t == TR - 1
-        sen, rn, rwn = "SE%d" % t, "R%d" % t, "RW%d" % t
-        R = T.R[:, t, :]
         for s in range(ST):
             for h in range(NB):
                 tag[0] = h
                 step(h, s, t == 0 and s == 0)
                 if s < ST - 1:
                     column(h, s + 1)
+            tag[0] = None
+            if t > 0 and s == CFG["own"]:
+                store(t - 1)
+            if s % 2 == 0:
+                in_order(s)
+            if s < ST - 1:
+                words(s, "P7", "SC")
+            if s == ST - 2:
+                last_columns(t)
+                op("v", lambda: V.tensor_reduce(T.TH[:, 0:1], T.XR[:, H::PIT], AxisListType.X, A.add), ("v", 4), "XRo XRx", "TH")
+                ts(mat("THM"), mat("SEL4"), T.TH[:, 0:1], None, A.mult, None, 64, "SEL4 TH", "THM")
         for h in range(NB):
-            nq, q0 = BAT[h], Q0[h]
-            n, a, o = 16 * nq, 16 * q0, 20 * q0
-            XF, xf = T[XFN[h]], XFN[h]
-            tag[0] = h
-            quarter(h)
-            mm([(XF[:, 0:n], ID, mat("DN", n), True, False, n)], "ID DN", xf)
-            mm([(XF[:, 0:n], mat("CC"), T.XQ[:, q0:q0 + nq, 0:16], False, True, n)], "CC XQ%d" % h, xf)
-            ts(T.TQ[:, 0:n], XF[:, 0:n], C4, C4, A.add, A.subtract, n, xf, "TQ")
-            tt(T.MQ[:, a:a + n], T.TQ[:, 0:n], XF[:, 0:n], A.is_equal, n, "TQ " + xf, "MQ%d" % h)
-            init = 0.0 if h == 0 else T.CN[:, a - 1:a]
-            scan(T.CN[:, a:a + n], T.MQ[:, a:a + n], T.MQ[:, a:a + n], init, A.add, A.max, n // 2,
-                 "MQ%d" % h + (" CN%d" % (h - 1) if h else ""), "CN%d" % h)
-            tt(T.MC[:, a:a + n], T.MQ[:, a:a + n], T.CN[:, a:a + n], A.mult, 2 * n, "MQ%d CN%d" % (h, h), "MC%d" % h)
-            mm([(XF[:, 0:n], ID, T.BM[:, 0:n], True, False, n), (XF[:, 0:n], mat("SELD"), T.MQ[:, a:a + n], False, False, n)],
-               "ID BM SELD MQ%d" % h, xf)
-            mm([(XF[:, 0:n], mat("SEL4"), T.MC[:, a:a + n], False, True, n)], "SEL4 MC%d" % h, xf)
-            scan(T.FS[:, o:o + n], row("RS", 0, n), XF[:, 0:n], 0.0, A.add, A.min, n, "RS " + xf, "FS%d" % h)
-            ts(T.SL[:, q0:q0 + nq], T.FS[:, o + 15:o + n:16], 15.0, None, A.add, None, nq, "FS%d" % h, "SL%d" % h)
-            cp(T.SE[:, t, :].indirect(T.SL[:, q0:q0 + nq]), xslot(h), n, "SL%d x%d" % (h, h), sen, k="vs")
-            act(T.RT[:, 16 + q0:16 + q0 + nq], T.FS[:, o + 15:o + n:16], AF.Identity, nq, "FS%d" % h, "RTs%d" % h, bias=15.0)
-        tag[0] = None
-        remote(lambda d, t=t: T.SE[:, t, reg(d)], T.R[:, t, mine], sen + " ARx", rn + "x")
-        cp(T.R[:, t, mine], T.SE[:, t, reg(rank)], 24, sen, rn)
-        mm([(T.P6[:, 64:96], T.ROT[:, t, :], T.RT[:, 0:32], True, True, 256)], "ROT%d %s %s" % (t, allh("RTb%d"), allh("RTs%d")), "P6")
-        cp(T.R16[:], T.P6[:, 64:96], 32, "P6", "R16")
-        act(T.RU[:, 0:16], T.P6[:, 64:80], AF.Copy, 16, "P6", "RUb")
-        act(T.RU[:, 48:64], T.P6[:, 64:80], AF.Identity, 16, "P6", "RUc", bias=2048.0)
-        for s in range(ST):
-            for h in range(NB):
-                c0, c1 = 16 * s + Q0[h], 16 * s + Q0[h] + BAT[h]
-                hf = T.HF[:, 16 * c0:16 * c1]
-                act(hf, T.S[:, 0:B].indirect(T.B16[:, c0:c1]), AF.Copy, 16 * BAT[h], "S B16_%d_%d" % (s, h), "HF%d_%d" % (s, h), k="ag")
-                tt(T.MK[:, 16 * c0:16 * c1], T.OH[:].indirect(T.IX4[:, c0:c1]), hf,
-                   A.mult, 16 * BAT[h], "OH IX4_%d_%d HF%d_%d" % (s, h, s, h), "MK%d_%d" % (s, h), k="vg")
-        for u in range(4):
-            mm([(T.P6[:, 0:64], T.ONE[:, p, :], T.MK[:, p::16], p == 0, p == 15, 256) for p in range(4 * u, 4 * u + 4)],
-               "ONE%d ONE%d " % (2 * u, 2 * u + 1) + " ".join(allh("MK%d_%%d" % s) for s in range(ST)), "P6")
-        act(T.SF[:, 0:64], T.P6[:, 0:64], AF.Copy, 64, "P6", "SFa")
-        act(T.SF[:, 64:128], T.P6[:, 0:64], AF.Copy, 64, "P6", "SFb", scale=37.0)
-        for s in range(ST):
-            tt(T.WP[:, 0:16], T.WI[:], T.SF[:, 16 * s:16 * s + 16], A.mult, 32, "WI SFa", "WPa")
-            tt(T.WT[:], T.WI[:], T.SF[:, 64 + 16 * s:80 + 16 * s], A.add, 32, "WI SFb", "WT")
-            ts(T.WP[:, 16:32], T.WP[:, 0:16], 5, None, A.arith_shift_right, None, 16, "WPa", "WPb")
-            tt(T.WP[:, 32:48], T.WP[:, 16:32], T.WT[:], A.add, 32, "WPb WT", "WPc")
-            ts(T.WI[:], T.WP[:, 32:48], Q - 1, None, A.bitwise_and, None, 16, "WPc", "WI")
+            query(h, t)
+        ts(T.SL[:], row("FS", 15, L, 16), 15.0, None, A.add, None, 16, allh("FS%d"), "SL")
+        if last:
+            cp(T.SE[:, t, :].indirect(T.SL[:]), br("X"), L, "SL " + allh("x%d"), "SE%d" % t, k="vs")
+            items(t)
+        words(ST - 1, "XJ0", "S3")
         cp(T.W16[:], T.WI[:], 16, "WI", "W16")
-        cp(T.RT[:, 32:48], T.WI[:], 16, "WI", "RTw")
-        rr = rn + " " + rn + "x"
-        ts(rb("RQ"), R, 766.5, None, A.add, None, 96, rr, "RQ")
-        mm([(T.P7[:, 0:192], ID, T.BM[:, 0:192], True, False, 192)], "ID BM", "P7")
-        mm([(T.P7[:, 0:192], mat("CC"), rb("RQ"), False, True, 192)], "CC RQ", "P7")
-        scan(row("SC", 0, 192), row("RS", 0, 192), T.P7[:, 0:192], 0.0, A.add, A.min, 192, "RS P7", "SC")
-        ts(T.PL[:, 0:12], row("SC", 15, 192, 16), col(14), None, A.subtract, None, 12, "SC c13", "PLa")
-        ts(T.PL[:, 16:28], T.PL[:, 0:12], 2, H - 1, A.arith_shift_right, A.bitwise_and, 12, "PLa", "PLb")
-        cp(T.PL16[:, 0:12], T.PL[:, 16:28], 12, "PLb", "PL16")
-        tt(rb("RD"), T.X[:, 0:H].indirect(T.PL16[:, 0:12]), R, A.subtract, 192, "X PL16 " + rr, "RD", k="vg")
-        act(rf("VG"), T.V[:, 0:H].indirect(T.PL16[:, 0:12]), AF.Identity, 192, "V PL16 TH", "VG", k="ag", bias=T.TH[:, 0:1])
-        act(rb("RA"), rb("RD"), AF.Abs, 192, "RD", "RA")
-        mm([(T.P7[:, 256:448], mat("N8"), rb("RA"), True, True, 192)], "N8 RA", "P7")
-        tt(rf("ANS"), rf("VG"), T.P7[:, 256:448], A.add, 192, "VG P7", "ANS")
-        remote(lambda d: rf("ANS", CAP * d, CAP * d + CAP), T.AR[:, reg(rank)], "ANS", "ARx")
-        act(T.AR[:, reg(rank)], rf("ANS", CAP * rank, CAP * rank + CAP), AF.Copy, 48, "ANS", "AR")
-        act(row("WR"), T.IOT[:].indirect(T.W16[:]), AF.Copy, 256, "IOT W16", "WR", k="ag")
-        for h in range(NB):
-            cp(T.SW[:].indirect(T.SL[:, Q0[h]:Q0[h] + BAT[h]]), row("WR", 16 * Q0[h], 16 * (Q0[h] + BAT[h])), 16 * BAT[h],
-               "WR SL%d" % h, "SW", k="vs")
-        remote(lambda d: T.SW[:, reg(d)], T.RW[:, t, mine], "SW", rwn + "x")
-        act(T.RW[:, t, mine], T.SW[:, reg(rank)], AF.Copy, 48, "SW", rwn)
-        for h in range(NB):
-            nq, q0 = BAT[h], Q0[h]
-            n = 16 * nq
-            D = T.D[:, 16 * q0:16 * q0 + n]
-            dn = " ".join("D%d_%d" % (h, a) for a in range(nq // WQ))
-            tt(D, T.G[:].indirect(T.W16[:, q0:q0 + nq]), xslot(h), A.subtract, n, "G W16 x%d" % h, dn, k="vg")
-            act(D, D, AF.Abs, n, dn, dn)
-            if last:
-                act(T.XO[:, 16 * q0:16 * q0 + n], D, AF.Identity, n, dn, "XO%d" % h, scale=-1.0, bias=63.0)
-            else:
-                act(xslot(h), D, AF.Identity, n, dn, "x%d" % h, scale=-1.0, bias=63.0)
-        tt(row("HM"), T.S[:, 0:B].indirect(T.R16[:, 0:16]), row("NDG"), A.mult, 256, "S R16 NDG", "HM", k="vg")
-        tt(row("BR"), T.IOT[:].indirect(T.R16[:, 0:16]), T.TT[:, t, :], A.add, 256, "IOT R16 TT%d" % t, "BR", k="vg")
-        tt(T.EB[:, 0:L], T.RU[:, 0:16].indirect(T.BC[:]), row("BR"), A.is_equal, 256, "RUb BC BR", "A1", k="vg")
-        ne = L + 16 * NP
-        if NP:
-            act(row("BB"), T.IOT[:].indirect(T.R16[:, 0:16]), AF.Copy, 256, "IOT R16", "BB", k="ag")
-            act(T.PX[:], row("BB").indirect(T.PLS[:, 0:NP]), AF.Copy, 16 * NP, "BB PLS", "PX0", k="ag")
-            tt(T.EB[:, L:ne], T.RU[:, 0:16].indirect(T.PLS[:, NP:2 * NP]), T.PX[:], A.is_equal, 16 * NP, "RUb PLS PX0", "PX1", k="vg")
-        for gg in range(8):
-            o, sc = T.EX[:, :, 16 * gg:16 * gg + 16], T.GM[:, 8 + gg:9 + gg]
-            if gg < CFG["exv"]:
-                ts(o, T.EB[:], sc, None, A.mult, None, ne // 2, "A1 PX1 GM", "EX%d" % gg)
-            else:
-                act(o, T.EB[:], AF.Identity, ne, "A1 PX1 GM", "EX%d" % gg, scale=sc)
-        mm([(T.P6[:, 96:112], T.ROT[:, t, :], T.RT[:, 32:48], True, True, 256)], "ROT%d RTw" % t, "P6")
-        act(T.RU[:, 32:48], T.P6[:, 96:112], AF.Copy, 16, "P6", "RUw")
+        for u in range(2):
+            D, dn, xn, a = br("D", 128 * u, 128 * u + 128), "D%d D%d" % (2 * u, 2 * u + 1), "x%d x%d" % (2 * u, 2 * u + 1), 128 * u
+            XJ, xj = T["XJ%d" % u], "XJ%d" % u
+            act(br("GJ", a, a + 128), T.G[:].indirect(T.W16[:, 8 * u:8 * u + 8]), AF.Copy, 128, "G W16", "GJ%d" % u, k="ag")
+            mm([(XJ[:, 256:384], mat("NI"), br("X", a, a + 128), True, False, 128), (XJ[:, 256:384], ID, br("GJ", a, a + 128), False, True, 128)],
+               "NI ID GJ%d %s" % (u, xn), xj)
+            act(D, XJ[:, 256:384], AF.Abs, 128, xj, dn)
+            act(br("XO" if last else "X", a, a + 128), D, AF.Identity, 128, dn, "XO%d" % u if last else xn, scale=-1.0, bias=63.0)
         if not last:
             for h in range(NB):
                 column(h, 0)
-        act(rb("JK"), rf("ANS"), AF.Sign, 192, "ANS", "JK THa", scale=-1.0, bias=-0.5, accum_out=T.TH[:, 4:5])
-        if not last:
-            ts(T.THI[:, 0:1], T.TH[:, 4:5], -0.5, 96.0, A.mult, A.add, 1, "THa", "THI0")
-            ts(T.THI[:, 1:2], T.THI[:, 0:1], 7, None, A.bitwise_and, None, 1, "THI0", "THI1")
-            ts(T.TH[:, 0:1], T.THI[:, 1:2], 8192.0, None, A.mult, None, 1, "THI1", "TH")
-        cp(T.PLF[:, 0:12], T.PL[:, 16:28], 12, "PLb", "PLF")
-        act(rf("PR"), T.IOT[:].indirect(T.PL16[:, 0:12]), AF.Copy, 192, "IOT PL16", "PR", k="ag", scale=-1.0)
-        act(rf("PB"), T.PLF[:, 0:12].indirect(T.BC[:, 0:12]), AF.Copy, 192, "PLF BC", "PB", k="ag")
-        act(rb("N2"), R, AF.Relu, 192, rr, "N2", scale=-64.0)
-        mm([(T.P7[:, 0:192], IDF, rf("PR"), True, False, 768), (T.P7[:, 0:192], IDF, rf("PB"), False, False, 768),
-            (T.P7[:, 0:192], ID, rb("TRI"), False, False, 192), (T.P7[:, 0:192], ID, rb("N2"), False, False, 192)],
-           "ROT0 ID PR PB TRI N2", "P7")
-        mm([(T.P7[:, 0:192], mat("NI"), rb("JK"), False, True, 192)], "NI JK", "P7")
-        ts(rb("EE"), T.P7[:, 0:192], 0.0, None, A.is_equal, None, 192, "P7", "EE")
-        scan(rf("ES"), rb("D2"), rb("EE"), 0.0, A.mult, A.add, 192, "D2 EE", "ES")
-        ts(T.SM[:, 0:12], rf("ES", 15, 192, 16), 1.0, 2048.0, A.not_equal, A.mult, 12, "ES", "SMa")
-        tt(T.SM[:, 16:28], T.SM[:, 0:12], T.PLF[:, 0:12], A.add, 24, "SMa PLF", "SMb")
-        tt(T.SM[:, 32:44], T.SM[:, 16:28], T.DM[:, 16:28], A.min, 24, "SMb DM1", "SMc")
-        cp(T.LS[:, 0::2], T.SM[:, 32:44], 12, "SMc", "LS")
-        for q in range(11, -1, -1):
-            cp(T.X[:].indirect(T.LS[:, 2 * q:2 * q + 1]), T.R[:, t, 16 * q:16 * q + 16], 16, "LS " + rr, "X", k="vs")
-        for q in range(11, -1, -1):
-            cp(T.V[:].indirect(T.LS[:, 2 * q:2 * q + 1]), T.RW[:, t, 16 * q:16 * q + 16], 16, "LS %s %sx" % (rwn, rwn), "V", k="vs")
-        tt(row("AG"), T.AR[:].indirect(T.R16[:, 16:32]), row("BMF"), A.add, 256, "AR ARx R16 BMF", "AG", k="vg")
-        scan(row("SC"), row("RS"), row("AG"), 0.0, A.add, A.min, 256, "RS AG", "SC")
-        Wr = T.RU[:, 32:48]
+        an, av = allh("AN%d"), row("AN", 15, L, 16)
         Z = lambda j: T.ZI[:, 16 * j:16 * j + 16]
-        cp(Z(0), row("SC", 15, L, 16), 16, "SC", "Z0")
-        ts(T.ZF[:, 0:16], row("SC", 15, L, 16), 0.0, None, A.is_ge, None, 16, "SC", "ZFk")
-        ts(Z(1), Z(0), Q - 1, None, A.bitwise_and, None, 16, "Z0", "Z1")
-        tt(T.ZF[:, 16:32], Z(1), Wr, A.not_equal, 32, "Z1 RUw", "ZFn")
-        tt(Z(2), Z(1), Wr, A.mult, 32, "Z1 RUw", "Z2")
-        tt(T.UP[:], T.ZF[:, 16:32], T.ZF[:, 0:16], A.mult, 32, "ZFn ZFk", "UP")
-        mm([(T.P6[:, 128:144], IDF, T.RU[:, 48:64], True, False, 256)], "ROT0 RUc", "P6")
-        mm([(T.P6[:, 128:144], mat("NI"), T.UP[:], False, False, 16)] +
-           [(T.P6[:, 128 + qb:129 + qb], T.EX[:, 16 + u, :], T.UP[:, qa:qa + 1], False, False, 1) for u, (qa, qb) in enumerate(PAIRS)] +
-           [(T.P6[:, 128 + q:129 + q], T.EX[:, q, :], T.UP[:, q:q + 1], False, q == 15, 1) for q in range(16)],
-           "NI UP" + "".join(" EX%d" % gg for gg in range(8)), "P6")
-        tt(T.ZF[:, 32:48], Z(1), Wr, A.add, 32, "Z1 RUw", "ZFs")
+        Y = lambda j: T.ZF[:, 16 * j:16 * j + 16]
+        va, vv = allh("VA%d"), row("VA", 15, L, 16)
+        tt(Y(1), vv, T.WI[:], A.is_equal, 32, va + " WI", "Y1")
+        tt(Y(2), Y(1), T.B2[:], A.add, 32, "Y1 B2", "Y2")
+        tt(Y(0), av, T.B21[:], A.min, 32, an + " B21", "Y0")
+        tt(T.B2N[:], Y(2), Y(0), A.max, 32, "Y2 Y0", "B2N")
+        mm([(T.P7[:, 0:L], ID, br("BM"), True, False, 256), (T.P7[:, 0:L], fm("IDH"), T.B2R[:, 0:L], False, False, 1024)], "ID BM IDH B2Ra", "P7")
+        tt(T.TE[:], T.B2N[:].indirect(T.LA[:]), T.B2R[:], A.is_equal, 640, "B2N B2Ra B2Rb LA", "TE", k="vg")
+        mm([(T.P7[:, 64 * m + 16 * d:64 * m + 64], mat("ON2"), T.TE[:, 16 * OFF[u]:16 * OFF[u + 1]], False, False, 48)
+            for u, (d, m) in enumerate(CROSS)] + [(T.P7[:, 0:L], mat("ON2"), T.TE[:, 0:L], False, True, 256)], "ON2 TE", "P7")
+        pick(row("CF"), row("RS"), T.P7[:, 0:L], 256, "RS P7", "CF")
+        tt(Y(3), row("CF", 15, L, 16), T.DM[:, 0:16], A.min, 32, "CF DM0", "Y3")
+        ts(T.LH[:], Y(3), -0.5, None, A.add, None, 16, "Y3", "LH")
+        tt(Z(2), vv, T.WI[:], A.mult, 32, va + " WI", "Z2")
+        tt(Y(4), vv, T.WI[:], A.add, 32, va + " WI", "Y4")
         ts(Z(3), Z(2), 5, None, A.arith_shift_right, None, 16, "Z2", "Z3")
-        tt(Z(4), Z(3), T.ZF[:, 32:48], A.add, 32, "Z3 ZFs", "Z4")
+        tt(Z(4), Z(3), Y(4), A.add, 32, "Z3 Y4", "Z4")
         ts(Z(5), Z(4), Q - 1, None, A.bitwise_and, None, 16, "Z4", "Z5")
-        tt(row("ZD"), Z(5).indirect(T.BC[:]), row("DG"), A.mult, 256, "Z5 BC DG", "ZD", k="vg")
-        tt(T.ZF[:, 48:64], T.P6[:, 128:144], T.DM[:, 0:16], A.min, 16, "P6 DM0", "ZFl")
-        cp(T.LH[:, 0:16] if NP else T.LH[:, 0::2], T.ZF[:, 48:64], 16, "ZFl", "LH")
+        cp(T.Z16[:], Z(5), 16, "Z5", "Z16")
+        tt(row("ZD"), T.IOT[:].indirect(T.Z16[:]), br("K%d" % t), A.mult, L, "IOT IOTx Z16 K%d" % t, "ZD", k="vg")
+        ts(Y(5), av, 0.0, float(Q), A.is_le, A.mult, 16, an, "Y5")
+        tt(Y(5), Y(5), T.WI[:], A.max, 32, "Y5 WI", "Y5")
+        cp(T.WK[:], Y(5), 16, "Y5", "WK")
+        if last:
+            act(row("WR"), T.IOT[:].indirect(T.WK[:]), AF.Copy, L, "IOT IOTx WK", "WR", k="ag")
+            cp(T.SW[:].indirect(T.SL[:]), row("WR"), L, "WR SL", "SW", k="vs")
+            remote(lambda d: T.SW[:, reg(d)], rf("RW", mine.start, mine.stop), "SW", "RWx")
+            dma("s", rf("RW", mine.start, mine.stop), T.SW[:, reg(rank)], 24, "SW", "RW")
+        else:
+            signs(T.SG[:, 0:L], T.IOT[:].indirect(T.WK[:]), L, "IOT IOTx WK", "SG", "XJ1", k="ag")
+            tt(T.SE[:, t, :].indirect(T.SL[:]), T.SG[:, 0:L], br("XF"), A.mult, L, "SG SL " + allh("XF%d"), "SE%d" % t, k="vs")
+            items(t)
         if last:
             for u in range(2):
-                mm([(T.XF1[:], T.KW[:], T.S[:, 512 * u:512 * u + 512], True, True, 2048)], "KW S", "XF1")
-                act(T.YH[:, 512 * u:512 * u + 512], T.XF1[:], AF.Copy, 512, "XF1", "YH")
-            mm([(T.XF0[:, 0:L], T.KW[:], row("HM"), True, False, 1024)], "KW HM", "XF0")
-            mm([(T.XF0[:, 0:L], T.KW[:], row("ZD"), False, True, 1024)], "KW ZD", "XF0")
-            cp(row("AG"), T.XF0[:, 0:L], 256, "XF0", "AG")
-        for q in range(16 - BLK, -1, -BLK):
-            ls = T.LH[:, q:q + BLK] if NP else T.LH[:, 2 * q:2 * q + 1]
-            a, b = 16 * q, 16 * (q + BLK)
+                mm([(T.XJ1[:], fm("KW"), T.S[:, 512 * u:512 * u + 512], True, True, 2048)], "KW S", "XJ1")
+                act(T.YH[:, 512 * u:512 * u + 512], T.XJ1[:], AF.Copy, 512, "XJ1", "YH")
+            mm([(T.XJ0[:, 0:L], fm("KW"), row("HM"), True, False, 1024)], "KW HM", "XJ0")
+            mm([(T.XJ0[:, 0:L], fm("KW"), row("ZD"), False, True, 1024)], "KW ZD", "XJ0")
+            act(row("AG"), T.XJ0[:, 0:L], AF.Copy, 256, "XJ0", "AG")
+        for m in range(3, -1, -1):
+            ls, a, b = T.LH[:, 4 * m:4 * m + 4], 64 * m, 64 * m + 64
             if last:
-                cp(T.YH[:].indirect(ls), row("AG", a, b), b - a, "LH AG", "YH", k="vs")
+                cp(T.YH[:].indirect(ls), row("AG", a, b), 64, "LH AG", "YH", k="vs")
             else:
-                tt(T.S[:].indirect(ls), row("ZD", a, b), row("HM", a, b), A.add, b - a, "LH ZD HM", "S", k="vs")
-    dma("s", T.yx[:], T.XO[:], 64, allh("XO%d"), "")
-    dma("s", T.yw[:], T.FM[0::16, ROWS.index("WR"), :], 8, "WR", "")
-    dma("s", T.ys[:], T.X[:, 0:H], 128, "X", "")
-    dma("s", T.yv[:], T.V[0::16, 0:H], 16, "V", "")
-    dma("a", T.yh[:], T.YH[0::16, 0:B], 32, "YH", "")
+                tt(T.S[:].indirect(ls), row("ZD", a, b), row("HM", a, b), A.add, 64, "LH ZD HM", "S", k="vs")
+    store(TR - 1)
+    act(row("YW"), T.IOT[:].indirect(T.W16[:]), AF.Copy, L, "IOT IOTx W16", "YW", k="ag")
+    dma("s", T.yx[:], br("XO"), 64, "XO0 XO1", "")
+    dma("s", T.yw[:], T.FM[0::16, ROWS.index("YW"), :], 8, "YW", "")
+    dma("s", T.yh[:], T.YH[0::16, 0:B], 32, "YH", "")
+    dma("s", T.ys[:], T.XB[:, 0:H], 128, "XB", "")
+    dma("a", T.yv[:], T.YV[0::16, 0:H], 16, "YV", "")
     return ops
 
 
 def link(ops):
     wr, rd, deps = {}, {}, []
-    ps = lambda k: k[:2] in ("XF", "P6", "P7") or k[:3] == "KEY"
+    ps = lambda k: k[:2] in ("XJ", "P6", "P7", "KB")
     for i, o in enumerate(ops):
         d = {}
         for k in o["r"] + o["w"]:
             if k in wr:
                 j = wr[k]
-                same = ops[j]["eng"] == o["eng"] and ops[j]["kind"] == "c"
-                raw = k in o["r"] and not ps(k)
-                d[j] = d.get(j, False) or (not same) or raw or (CFG["safe"] and not ps(k) and k[:4] != "gord")
+                same = ops[j]["eng"] == o["eng"] and (ops[j]["kind"] == "c" or k[:4] == "gord")
+                d[j] = d.get(j, False) or (not same) or (not ps(k) and k[:4] != "gord")
             if k in o["w"] or ps(k):
                 for j in rd.get(k, []):
-                    same = ops[j]["eng"] == o["eng"] and ops[j]["kind"] == "c"
-                    d[j] = d.get(j, False) or (not same) or CFG["safe"]
+                    d[j] = True
         d.pop(i, None)
         deps.append(d)
         for k in o["r"] + o["w"]:
@@ -583,39 +646,50 @@ def span(o, par):
         return 60.0, par["dma"] + 5.0 * n
     if k == "r":
         return 300.0, 0.0
-    return 0.0, par["rem"]
+    return 0.0, par["rem" if k == "x" else "big"]
+
+
+def edges(ops, deps, par):
+    sp = [span(o, par) for o in ops]
+    before = [[(j, (sp[j][1] + par["lat"]) if hard else 0.001) for j, hard in d.items()] for d in deps]
+    after = [[] for _ in ops]
+    for i, lst in enumerate(before):
+        for j, lg in lst:
+            after[j].append((i, lg))
+    return sp, before, after
+
+
+def clock(ops, seq, sp, before):
+    fin, free = [0.0] * len(ops), {}
+    for i in seq:
+        e = ops[i]["eng"]
+        t = max([fin[j] + lg for j, lg in before[i]] + [0.0 if e == "x" else free.get(e, 0.0)])
+        fin[i] = free[e] = t + sp[i][0]
+    return max(fin[i] + sp[i][1] for i in seq)
 
 
 def order(ops, deps, par):
     n = len(ops)
-    sp = [span(o, par) for o in ops]
-    succ = [[] for _ in range(n)]
-    for i, d in enumerate(deps):
-        for j in d:
-            succ[j].append(i)
-    pri = [0.0] * n
-    for i in range(n - 1, -1, -1):
-        pri[i] = sp[i][0] + sp[i][1] + max([pri[j] + (par["lat"] if deps[j][i] else 0.0) for j in succ[i]] + [0.0])
-    noise = np.random.RandomState(CFG["seed"]).rand(n) * CFG["noise"]
-    for i in range(n):
-        pri[i] += float(noise[i])
-        if ops[i]["tag"] is not None:
-            pri[i] += CFG["stag"] * (NB - 1 - ops[i]["tag"])
-            if ops[i]["cost"][0] == "ag" or ops[i]["w"][0][0] == "M":
-                pri[i] -= CFG["heavy"]
-    lag = lambda j, i: (sp[j][1] + par["lat"]) if deps[i][j] else 0.001
-    before = [[(j, lag(j, i)) for j in deps[i]] for i in range(n)]
-    after = [[(i, lag(j, i)) for i in succ[j]] for j in range(n)]
+    tests = [edges(ops, deps, dict(par, **u)) for u in SPREAD]
+    sp, before, after = edges(ops, deps, par)
+    big = [i for i in range(n) if ops[i]["cost"] == ("ag", 1024)]
     best = None
-    for it in range(CFG["passes"]):
-        start = place(ops, sp, before, after, pri, [0.0] * n)
-        end = max(start[i] + sp[i][0] + sp[i][1] for i in range(n))
-        if best is None or end < best[0]:
-            best = (end, start)
-        back = place(ops, sp, after, before, [start[i] + sp[i][0] for i in range(n)], [x[1] for x in sp])
-        pri = [back[i] + sp[i][0] for i in range(n)]
-    start = best[1]
-    return sorted(range(n), key=lambda i: (start[i], i))
+    for beat in CFG["beat"]:
+        aim = {i: CFG["t0"] + beat * u + CFG["gap"] * (u // (NB * ST)) for u, i in enumerate(big)}
+        end = aim[big[-1]] + CFG["tail"]
+        due = [0.0] * n
+        for i in range(n - 1, -1, -1):
+            due[i] = aim[i] if i in aim else min([due[j] - lg for j, lg in after[i]] + [end - sp[i][1]]) - sp[i][0]
+        pri = [-d for d in due]
+        for it in range(CFG["passes"]):
+            start = place(ops, sp, before, after, pri, [0.0] * n)
+            seq = sorted(range(n), key=lambda i: (start[i], i))
+            score = sum(math.log(clock(ops, seq, s, b)) for s, b, a in tests)
+            if best is None or score < best[0]:
+                best = (score, seq)
+            back = place(ops, sp, after, before, [start[i] + sp[i][0] for i in range(n)], [x[1] for x in sp])
+            pri = [back[i] + sp[i][0] for i in range(n)]
+    return best[1]
 
 
 def place(ops, sp, before, after, pri, t0):
@@ -639,10 +713,10 @@ def place(ops, sp, before, after, pri, t0):
                 lo = mid + 1
             else:
                 hi = mid
-        while lo < len(lst) and lst[lo][0] < t + dur:
+        while lo < len(lst) and lst[lo][0] < t + dur * CFG["fit"]:
             t = max(t, lst[lo][1])
             lo += 1
-        lst.insert(lo, (t, t + dur))
+        lst.insert(lo, (t, t + dur if lo == len(lst) else min(t + dur, max(t, lst[lo][0]))))
         start[i] = t
         for j, lg in after[i]:
             left[j] -= 1
@@ -651,13 +725,18 @@ def place(ops, sp, before, after, pri, t0):
     return start
 
 
+ORDER = []
+
+
 def rank_program(g, core, T, topo):
     rank = T.rank_of(core)
     if rank is None:
         return
     ops = build(g, core, T, topo, rank)
     deps = link(ops)
-    seq = order(ops, deps, PAR)
+    if not ORDER:
+        ORDER.append(order(ops, deps, PAR))
+    seq = ORDER[0]
     queue = {"v": g.vector, "a": g.scalar, "p": g.tensor, "q": g, "s": g.sync}
     need = set()
     for i, d in enumerate(deps):

import math
from concourse.bass import DstId, RemoteDMATransfer
from concourse.mybir import dt, AluOpType, AxisListType, ActivationFunctionType

A = AluOpType
AF = ActivationFunctionType
N, Q, B, H, L, CAP, TR, ST = 4, 4096, 1024, 512, 256, 48, 3, 4
NB = 4
CFG = dict(eng=[4, 2, 2], pes=2, t0=7500.0, beat=[2000.0, 2100.0], gap=11000.0, tail=22000.0, passes=5, fit=0.6, xq="addda", own=0, vs0=0)
SPREAD = [dict(lat=170.0), dict(lat=260.0), dict(lat=200.0, gam=2.0, sig=5.0, afix=100.0), dict(lat=150.0, gam=1.15, sig=2.0)]
PAR = dict(cyc=1.0, gam=1.56, sig=3.8, pe=0.6, lat=220.0, vfix=0.0, afix=65.0, rem=4000.0, big=18000.0, dma=2000.0)
BIG, RST = float(2 ** 40), float(2 ** 41)
C1, C4, C32, C512, C1K = 1.5 * 2 ** 23, 1.5 * 2 ** 25, 1.5 * 2 ** 28, 1.5 * 2 ** 32, 1.5 * 2 ** 33
PIT, MSG, GW = 720, 528, 2112
f32, b16, i32, u16 = "float32", "bfloat16", "int32", "uint16"
MATS = ["A4", "NA", "CC", "CC4", "WT", "N8", "SEL4", "SELD", "NEG", "ON2", "THM", "ID", "KI", "NI", "I3", "SV", "KF", "DN", "BI", "MI", "PT", "OI"]
FMAT = ["IDF", "NIF", "AI", "NAI", "IDH", "S12", "ONF", "KW", "SELG", "PM0", "PM1", "PM2", "PM3"]
ROWS = ["RS", "HM", "ZD", "WR", "SC", "S3", "AN", "VA", "CF", "AG", "FS", "YW"]
BROW = ["BM", "RSB", "TT", "CM", "MQ", "CN", "MC", "SP", "RA", "X", "D", "XO", "BC", "GJ", "XF", "RD", "HI", "CB",
        "K0", "K1", "K2", "N0", "N1", "N2"]
R192 = ["RQ", "RX", "JS", "AB", "ES", "TRI", "TR2"]
F192 = ["RW", "PR", "PB", "SO"]
CROSS = [(d, m) for d in (1, 2, 3) for m in range(4)]
OFF = [16 + sum(4 - d for d, m in CROSS[:u]) for u in range(len(CROSS) + 1)]
SCRATCH = {}
for _n, _s, _t in [
        ("G", [Q], b16), ("H32", [B], i32), ("S", [1280], f32), ("XB", [PIT], b16), ("XR", [N * PIT], b16), ("PW", [3, 16], f32),
        ("COD", [16], b16), ("COL", [40], f32), ("PI", [8], i32), ("VI", [768], i32), ("VF", [768], f32),
        ("IOT", [Q + 16], f32), ("DI", [16, 128], b16), ("J", [544], b16), ("LF", [40], f32), ("OH", [GW], b16),
        ("W1", [16, 128], b16), ("W2", [16, 128], b16), ("MAT", [len(MATS), 128], b16), ("FT", [len(FMAT), 128], f32),
        ("C768", [8], b16), ("BM20", [4, 20], b16), ("BM22", [4, 22], b16), ("FD", [80], f32), ("FE", [88], f32),
        ("FM", [len(ROWS), L], f32), ("BR", [len(BROW), L], b16), ("RB", [len(R192), 192], b16), ("RF", [len(F192), 192], f32),
        ("KC", [4, 35], b16), ("KD", [4, 36], f32), ("DM", [32], f32), ("LA", [40], u16), ("LB", [40], u16),
        ("RS4", [64], f32), ("SB", [64, 4], f32), ("BO", [64], u16), ("B2", [4, 4], f32), ("B2N", [16], f32), ("B21", [16], f32),
        ("B16", [64], u16), ("BF", [64], f32), ("IXF", [16], f32), ("IX", [64], u16), ("HF", [1024], f32), ("MK", [1024], f32),
        ("SF", [16], f32), ("WI", [16], i32), ("WP", [48], i32), ("WT", [16], f32), ("W16", [16], u16), ("WK", [16], u16),
        ("TQ", [L], f32), ("SL", [16], u16), ("XI", [16], u16), ("F2", [352], f32), ("FB", [320], f32),
        ("SE", [3, 1056], b16), ("SW", [1056], f32), ("R", [3, 192], b16), ("SG", [H], b16), ("HY", [H], f32), ("PL", [32], i32), ("PL16", [16], u16), ("PLF", [16], f32),
        ("SM", [48], f32), ("LS", [24], u16), ("TH", [8], f32), ("THI", [8], i32),
        ("B2R", [640], f32), ("TE", [640], b16), ("ZI", [96], i32), ("ZF", [96], f32), ("Z16", [16], u16), ("LH", [16], u16),
        ("YH", [1280], f32), ("YV", [PIT], f32), ("HV", [H], f32), ("M", [NB, 1024], b16), ("XQ", [64, 5], b16), ("XN", [68, 5], b16), ("XQ2", [16, 22], b16),
        ("HS", [L], u16), ("SO", [16, 36], f32)]:
    SCRATCH[_n] = ("sbuf", [128] + _s, _t)
for _h in range(NB):
    SCRATCH["GR%d" % _h] = ("sbuf", [128, GW], b16)
    SCRATCH["KB%d" % _h] = ("psum", [128, 4, 128], f32)
for _n in ("XJ0", "XJ1", "P6", "P7"):
    SCRATCH[_n] = ("psum", [128, 512], f32)
SEMAPHORES = ["v", "a", "p", "q"] + ["d%d" % k for k in range(24)] + ["%s%d" % (s, k) for s in ("ar", "lo") for k in range(7)]


def build(g, core, T, topo, rank):
    V, S, P = g.vector, g.scalar, g.tensor
    ops = []
    tag = [None]

    def op(eng, fn, cost, r, w, kind="c", sem=None):
        ops.append(dict(eng=eng, fn=fn, cost=cost, r=r.split(), w=w.split(), kind=kind, sem=sem, tag=tag[0]))

    def cp(o, i, n, r, w, k="v"):
        op("v", lambda: V.tensor_copy(o, i), (k, n), r, w)

    def ts(o, i, s1, s2, o0, o1, n, r, w):
        if o1 is None:
            op("v", lambda: V.tensor_scalar(o, i, s1, None, o0), ("v", n), r, w)
        else:
            op("v", lambda: V.tensor_scalar(o, i, s1, s2, o0, o1), ("v", n), r, w)

    def tt(o, a, b, o0, n, r, w, k="v"):
        op("v", lambda: V.tensor_tensor(o, a, b, o0), (k, n), r, w)

    def scan(o, a, b, init, o0, o1, n, r, w):
        op("v", lambda: V.tensor_tensor_scan(o, a, b, init, o0, o1), ("v", n), r, w)

    def pick(o, a, b, n, r, w):
        scan(o, a, b, 0.0, A.add, A.min, n, r, w)

    def ms(o, c, n, w):
        op("v", lambda: V.memset(o, c), ("v", n), "", w)

    def act(o, i, f, n, r, w, k="a", **kw):
        op("a", lambda: S.activation(o, i, f, **kw), (k, n), r, w)

    def fill(o, c, n, w, r=""):
        act(o, T.J[:, 0:n], AF.Identity, n, "J " + r, w, scale=0.0, bias=c)

    def mm(lst, r, w):
        def fn():
            ins = None
            for (o, l, rh, st, sp, n) in lst:
                ins = P.matmul(o, l, rh, st, sp)
            return ins
        op("p", fn, ("p", sum(max(64, x[5]) for x in lst)), r, w)

    def iota(o, pat, base, ch, n, w, isint=False):
        if isint:
            op("q", lambda: g.iota(o, pat, base, ch), ("q", n), "", w)
        else:
            op("q", lambda: g.iota(o, pat, base, ch, allow_small_or_imprecise_dtypes=True), ("q", n), "", w)

    def const(o, c, n, w):
        iota(o, [[0, n]], c, 0, n, w + " gordq")

    nd = [0]

    def dma(qn, o, i, kb, r, w):
        e = g.sync if qn == "s" else S
        op(qn, lambda: e.dma_start(o, i), ("d", kb), r, w, kind="d", sem=("d%d" % nd[0], 16))
        nd[0] += 1

    nr = [0]
    peers = [(rank + j) % N for j in range(1, N)]

    def remote(src, dst, r, w, same=False):
        k = nr[0]
        nr[0] += 1
        cnt = CFG["eng"]
        ids = [topo.addr(T.cores[d], core) for d in peers]
        ids = [DstId(rid=rid, pnc=pid) for rid, pid in ids]
        es = topo.engines(core, T.cores[peers[0]])

        def fn():
            if same:
                trs = [RemoteDMATransfer(dst_ids=ids, dma_engine_mask=topo.mask(core, T.cores[peers[0]]), remote_sem=T.sem["ar%d" % k],
                                         src=src(0), dsts=[dst] * len(peers))]
            else:
                trs = [RemoteDMATransfer(dst_ids=[ids[j]], dma_engine_mask=sum(1 << e for e in es[sum(cnt[:j]):sum(cnt[:j + 1])]),
                                         remote_sem=T.sem["ar%d" % k], src=src(d), dst=dst) for j, d in enumerate(peers)]
            return g.remote_dma_fused(trs, local_sem=T.sem["lo%d" % k])
        op("q", fn, ("r", 0), r + " gordq", "snd%d gordq" % k, kind="r", sem=("lo%d" % k, len(es) if same else sum(cnt)))
        op("x", None, ("X" if same else "x", 0), "snd%d" % k, w, kind="x", sem=("ar%d" % k, len(es) * len(peers) if same else sum(cnt)))

    col = lambda j: T.COL[:, j:j + 1]
    mat = lambda n, b=128: T.MAT[:, MATS.index(n), 0:b]
    fm = lambda n: T.FT[:, FMAT.index(n), :]
    row = lambda n, a=0, b=L, st=1: T.FM[:, ROWS.index(n), a:b:st]
    br = lambda n, a=0, b=L, st=1: T.BR[:, BROW.index(n), a:b:st]
    rb = lambda n, a=0, b=192, st=1: T.RB[:, R192.index(n), a:b:st]
    rf = lambda n, a=0, b=192, st=1: T.RF[:, F192.index(n), a:b:st]
    allh = lambda f: " ".join(f % h for h in range(NB))
    reg = lambda d: slice(256 * d + 16, 256 * d + 16 + CAP)
    ID, IDF = mat("ID"), fm("IDF")
    own = PIT * rank
    dma("s", T.COD[:, 0:3], T.co[:], 1, "", "CO")
    dma("s", br("X"), T.xl[:], 64, "", allh("x%d"))
    dma("a", T.H32[:], T.hlp[:], 512, "", "H32")
    dma("s", T.G[:], T.gen[:], 1024, "", "G")
    dma("a", T.VI[0:8, 512:768], T.wl[:], 8, "", "VIw")
    dma("a", T.VI[0:8, 0:512], T.vst[:], 16, "", "VIv")
    dma("a", T.XB[:, 0:H], T.xst[:], 128, "", "XB")
    iota(T.PI[:, 0:1], [[0, 1]], 0, 1, 1, "PI0 gordq", True)
    iota(T.J[:], [[0, 34], [1, 16]], 0, 0, 544, "J gordq")
    iota(mat("BI"), [[16, 8], [0, 16]], 0, 0, 128, "BI gordq")
    iota(mat("MI"), [[1, 128]], 0, 0, 128, "MI gordq")
    iota(T.DI[:], [[-1, 16], [1, 128]], 0, 0, 2048, "DI gordq")
    iota(T.KC[:, :, 16:32], [[0, 4], [2, 16]], -15, 0, 64, "KCk gordq")
    cp(col(0), T.PI[:, 0:1], 1, "PI0", "c0")
    ts(T.PI[:, 1:2], T.PI[:, 0:1], 15, None, A.bitwise_and, None, 1, "PI0", "PI1")
    ts(T.PI[:, 2:3], T.PI[:, 0:1], 3, None, A.bitwise_and, None, 1, "PI0", "PI2")
    ts(T.PI[:, 3:4], T.PI[:, 0:1], 2, 3, A.arith_shift_right, A.bitwise_and, 1, "PI0", "PI3")
    cp(col(1), T.PI[:, 1:2], 1, "PI1", "c1")
    cp(T.COL[:, 3:5], T.PI[:, 2:4], 1, "PI2 PI3", "c3")
    ts(col(2), col(0), col(1), None, A.subtract, None, 1, "c0 c1", "c2")
    ts(T.COL[:, 9:11], T.COD[:, 1:3], 0.25, None, A.mult, None, 2, "CO", "c9")
    act(col(7), T.COD[:, 0:1], AF.Identity, 1, "CO", "c7", scale=64.0)
    act(col(8), T.COD[:, 0:1], AF.Identity, 1, "CO", "c8", scale=-32.0)
    ts(mat("A4"), mat("BI"), col(2), col(9), A.is_equal, A.mult, 64, "BI c2 c9", "A4")
    ts(ID, mat("MI"), col(0), None, A.is_equal, None, 64, "MI c0", "ID")
    ts(br("BM"), T.J[:, 0:L], col(1), BIG, A.not_equal, A.mult, 128, "J c1", "BM")
    ms(T.BM20[:], BIG, 40, "BM20")
    ts(T.BM20[:, :, 0:16], T.J[:, 0:64], col(1), BIG, A.not_equal, A.mult, 32, "J c1", "BM20")
    ms(T.XQ[:, :, 4], 0.0, 32, allh("XQ%d"))
    ms(T.XN[:, :, 4], 0.0, 34, allh("XN%d") + " XNc")
    ms(T.XN[:, 64:68, 0:4], -768.0, 8, "XNc")
    ts(mat("NA"), mat("A4"), -1.0, None, A.mult, None, 64, "A4", "NA")
    ms(T.C768[:, 0:1], 1536.0, 1, "C768")
    ms(T.C768[:, 1:2], 768.0, 1, "C768")
    ts(mat("CC"), mat("BI"), col(2), col(10), A.is_equal, A.mult, 64, "BI c2 c9", "CC")
    mm([(T.P6[:, 0:1], mat("A4"), T.C768[:, 0:1], True, True, 1), (T.P6[:, 1:2], mat("CC"), T.C768[:, 1:2], True, True, 1)],
       "A4 CC C768", "P6")
    cp(T.COL[:, 13:15], T.P6[:, 0:2], 2, "P6", "c13")
    ms(T.FD[:], 0.0, 80, "FD")
    ms(T.FD[:, 0::20], RST, 4, "FD")
    ms(T.FD[:, 17::20], C1K, 4, "FD")
    ms(T.FD[:, 18::20], -C1K, 4, "FD")
    ts(T.FD[:, 16::20], T.FD[:, 16::20], col(13), -511.5, A.subtract, A.add, 4, "FD c13", "FDa")
    ts(T.FD[:, 19::20], T.FD[:, 19::20], col(13), None, A.add, None, 4, "FD c13", "FDb")
    ts(mat("WT"), mat("BI"), col(2), col(7), A.is_equal, A.mult, 64, "BI c2 c7", "WTm")
    ts(T.W2[:], T.DI[:], col(2), col(8), A.is_equal, A.mult, 1024, "DI c2 c8", "W2")
    for u in range(4):
        act(T.W1[:, 4 * u:4 * u + 4, :], T.W2[:, 4 * u:4 * u + 4, :], AF.Identity, 512, "W2", "W1_%d" % u, scale=-2.0)
    act(T.KC[:, :, 0:16], T.BM20[:, :, 0:16], AF.Identity, 64, "BM20", "KCt", bias=-16.0)
    fill(T.KC[:, :, 32:35], BIG, 12, "KCx")
    fill(T.KD[:], 0.0, 144, "KD")
    fill(T.KD[:, :, 0], RST, 4, "KD")
    fill(T.KD[:, :, 32], C32, 4, "KD")
    fill(T.KD[:, :, 33], -C32, 4, "KD")
    act(col(20), col(1), AF.Identity, 1, "c1", "c20", scale=-128.0)
    for q in range(4):
        act(T.KD[:, q, 34:35], col(20), AF.Identity, 1, "c20 KD", "KD%d" % q, bias=-48.0 - 32.0 * q)
    for h in range(NB):
        ms(T["GR%d" % h][:, 0::32], 0.0, 33, "GZ%d" % h)
    act(col(16), col(0), AF.Identity, 1, "c0", "c16", scale=16.0)
    ts(fm("SELG"), mat("BI"), col(16), None, A.is_equal, None, 128, "BI c16", "SELG")
    cp(T.VF[0:8, 0:H], T.VI[0:8, 0:H], 512, "VIv", "VFv")
    cp(T.VF[0:8, H:H + L], T.VI[0:8, H:H + L], 256, "VIw", "VFw")
    selg = T.FT[0:8, FMAT.index("SELG"), :]
    for nm, c in (("IDF", 1.0), ("NIF", -1.0), ("AI", 4.0 * PIT), ("NAI", -4.0 * PIT), ("IDH", 0.5)):
        act(fm(nm), ID, AF.Identity, 128, "ID", nm, scale=c)
    for t in range(TR):
        ts(br("K%d" % t), T.J[:, t:t + L], col(1), None, A.is_equal, None, 128, "J c1", "K%d" % t)
        ts(br("N%d" % t), T.J[:, t:t + L], col(1), None, A.not_equal, None, 128, "J c1", "N%d" % t)
    ms(T.PW[:], 0.0, 48, "PW")
    ms(T.SM[:, 0:16], 0.5, 16, "SMa")
    ms(T.SM[:, 16:28], 2.0, 12, "SMb")
    scan(T.PW[:, 0, :], T.SM[:, 0:16], T.PW[:, 2, :], 1.0, A.mult, A.add, 16, "SMa PW", "PWa")
    scan(T.PW[:, 1, 0:12], T.SM[:, 16:28], T.PW[:, 2, 0:12], -0.25, A.mult, A.add, 12, "SMb PW", "PWb")
    ms(T.PW[:, 1, 13:14], -0.5, 1, "PW")
    ms(T.PW[:, 2, 12:16:2], -1024.0, 1, "PW")
    tt(T.PW[:], T.PW[:], br("K0", 0, 48), A.mult, 96, "PW PWa PWb K0", "PW")
    for u, c in enumerate((23, 25, 26)):
        op("v", lambda u=u, c=c: V.tensor_reduce(col(c), T.PW[:, u, :], AxisListType.X, A.add), ("v", 16), "PW", "c%d" % c)
    act(col(24), col(23), AF.Identity, 1, "c23", "c24", scale=0.5)
    fill(br("CB"), C1, L, "CB")

    def signs(o, src, n, r, w, bank, k="a"):
        act(T.HY[:, 0:n], src, AF.Identity, n, r + " c23 c24", "HY", k=k, scale=col(23), bias=col(24))
        act(T.HV[:, 0:n], T.HY[:, 0:n], AF.Identity, n, "HY", "HV", bias=C1)
        mm([(T[bank][:, a:a + L], ID, br("CB"), a == 0, False, L) for a in range(0, n, L)], "ID CB", bank)
        mm([(T[bank][:, 0:n], fm("NIF"), T.HV[:, 0:n], False, False, 4 * n), (T[bank][:, 0:n], IDF, T.HY[:, 0:n], False, True, 4 * n)],
           "NIF IDF HV HY", bank)
        act(o, T[bank][:, 0:n], AF.Sign, n, bank, w)

    mm([(T.P6[:], selg, T.VF[0:8, 0:H], True, True, 2048)], "SELG VFv", "P6")
    signs(T.P6[:], T.P6[:], H, "P6", "P6", "P6")
    ts(T.XB[:, 0:H], T.XB[:, 0:H], 1.0, None, A.add, None, 256, "XB", "XB")
    for u in range(2):
        tt(T.XR[:, own + L * u:own + L * u + L], T.XB[:, L * u:L * u + L], T.P6[:, L * u:L * u + L], A.mult, L, "XB P6", "XRo")
    for d in [rank] + peers:
        a = PIT * d + (H if d == rank else MSG)
        const(T.XR[:, a:PIT * d + PIT], 0, PIT * d + PIT - a, "XRo" if d == rank else "XRd")
    remote(lambda d: T.XR[:, own:own + MSG], T.XR[:, own:own + MSG], "XRo XRd G", "XRx", same=True)
    iota(T.DM[:, 0:16], [[16, 16]], 0, 0, 16, "DM0 gordq")
    iota(mat("OI"), [[0, 4], [1, 32]], 0, 0, 128, "OI gordq")
    iota(mat("PT"), [[16, 8], [0, 4], [4, 4]], 0, 0, 128, "PT gordq")
    iota(br("CM", 0, 128), [[0, 8], [1, 4], [0, 4]], 0, 0, 128, "CM gordq")
    iota(T.LF[:, 0:16], [[1, 16]], 0, 0, 16, "LF0 gordq")
    for d in (1, 2, 3):
        iota(T.LF[:, OFF[4 * d - 4]:OFF[4 * d]], [[4, 4], [1, 4 - d]], 0, 0, 12, "LF%d gordq" % d)
    iota(T.IOT[:], [[1, Q + 16]], 0, 0, Q + 16, "IOT IOTx gordq")
    ts(row("RS"), T.J[:, 0:L], 0.0, RST, A.is_equal, A.mult, 256, "J", "RS")
    mm([(T.P7[:, 0:L], selg, T.VF[0:8, H:H + L], True, False, 1024), (T.P7[:, 0:L], ID, br("BM"), False, True, 256)], "SELG VFw ID BM", "P7")
    pick(row("SC"), row("RS"), T.P7[:, 0:L], 256, "RS P7", "SC")
    cp(T.WI[:], row("SC", 15, L, 16), 16, "SC", "WI")
    for u in range(4):
        cp(T.S[:, 256 * u:256 * u + 256], T.H32[:, 256 * u:256 * u + 256], 256, "H32", "S")
    act(br("RSB"), row("RS"), AF.Copy, 256, "RS", "RSB")
    ts(mat("N8"), mat("BI"), col(2), 8192.0, A.is_equal, A.mult, 64, "BI c2", "N8")
    ts(mat("ON2"), mat("N8"), 0.25, None, A.mult, None, 64, "N8", "ON2")
    act(fm("ONF"), mat("N8"), AF.Identity, 128, "N8", "ONF", scale=1.0 / 8192)
    for nm, c in (("KI", 1024.0), ("NI", -1.0), ("I3", 512.0)):
        ts(mat(nm), ID, c, None, A.mult, None, 64, "ID", nm)
    ts(col(11), col(1), 4.0, None, A.is_lt, None, 1, "c1", "c11")
    ts(col(12), col(1), col(11), 256.0, A.mult, A.mult, 1, "c1 c11", "c12")
    act(col(15), col(1), AF.Identity, 1, "c1", "c15", bias=1.0)
    act(col(17), T.COD[:, 2:3], AF.Identity, 1, "CO", "c17", scale=1.0 / 16)
    ts(col(22), col(1), -13.0, col(26), A.add, A.mult, 1, "c1 c26", "c22")
    act(col(18), col(22), AF.Identity, 1, "c22", "c18", scale=-1.0 / 2048)
    ts(col(19), col(1), float(rank), -8192.0, A.is_equal, A.mult, 1, "c1", "c19")
    act(col(5), col(1), AF.Identity, 1, "c1", "c5", scale=2.0, bias=1.0)
    act(col(21), col(14), AF.Identity, 1, "c13", "c21", scale=-0.25, bias=-0.375)
    for nm, c in (("SEL4", 11), ("SELD", 12), ("CC4", 17), ("SV", 25), ("KF", 26)):
        ts(mat(nm), mat("BI"), col(2), col(c), A.is_equal, A.mult, 64, "BI c2 c%d" % c, nm)
    for nm, c in (("S12", 18), ("KW", 15)):
        act(fm(nm), fm("ONF"), AF.Identity, 128, "ONF c%d" % c, nm, scale=col(c))
    ts(mat("NEG"), mat("SEL4"), 65536.0, None, A.mult, None, 64, "SEL4", "NEG")
    ts(mat("DN"), mat("BI"), 0.0, col(3), A.mult, A.subtract, 64, "BI c3", "DN")
    for q in range(4):
        ts(fm("PM%d" % q), mat("PT"), float(q), col(0), A.add, A.is_equal, 128, "PT c0", "PM%d" % q)
    ts(br("CM", 0, 128), br("CM", 0, 128), col(4), BIG, A.not_equal, A.mult, 64, "CM c3", "CM")
    const(T.RS4[:, 0:32], 0, 32, "RS4")
    fill(T.RS4[:, 0:32:4], RST, 8, "RS4")
    ts(T.OH[:, 0:128], mat("OI"), col(5), None, A.is_equal, None, 64, "OI c5", "OH")
    for a, n in ((128, 128), (256, 256), (512, 512), (1024, 1024), (2048, GW - 2048)):
        dma("s", T.OH[:, a:a + n], T.OH[:, 0:n], n // 4, "OH", "OH")
    fill(T.BM22[:, :, 16:22], BIG, 24, "BM22x")
    act(T.BM22[:, :, 0:16], T.BM20[:, :, 0:16], AF.Copy, 64, "BM20", "BM22")
    const(T.XQ2[:, :, 16:22], 0, 96, allh("XQ2%d"))
    const(T.FE[:], 0, 88, "FE")
    for sl, c in ((0, RST), (17, C1), (18, -C1), (19, -255.5), (20, C512), (21, -C512)):
        fill(T.FE[:, sl::22], c, 4, "FE")
    fill(T.FE[:, 16::22], col(21), 4, "FE", "c21")
    ts(rb("TRI"), T.J[:, 0:192], col(1), 8192.0, A.is_gt, A.mult, 96, "J c1", "TRI")
    ts(rb("TR2"), T.J[:, 0:192], col(1), -2048.0, A.is_equal, A.mult, 96, "J c1", "TR2")
    mm([(T.P6[:, 0:192], ID, rb("TRI"), True, False, 192), (T.P6[:, 0:192], ID, rb("TR2"), False, True, 192)], "ID TRI TR2", "P6")
    act(rb("TRI"), T.P6[:, 0:192], AF.Identity, 192, "P6", "TRI", bias=1024.0)
    act(rb("TR2"), T.P6[:, 0:192], AF.Identity, 192, "P6", "TR2", bias=2048.0)
    act(br("BC", 0, 64), br("BM", 0, 64), AF.Identity, 64, "BM", "BC", bias=2048.0)
    for d in range(N):
        for t in range(TR):
            const(T.SE[:, t, reg(d)], 0, CAP, "SE%d" % t)
        const(T.SW[:, reg(d)], Q, CAP, "SW")
    ts(br("TT"), T.J[:, 0:L], col(1), 4096.0, A.is_lt, A.mult, 128, "J c1", "TT")
    mm([(T.P7[:, 0:L], ID, br("TT"), True, False, L), (T.P7[:, 0:L], ID, br("K0"), False, True, L)], "ID TT K0", "P7")
    act(br("TT"), T.P7[:, 0:L], AF.Copy, L, "P7", "TT")
    cp(T.LA[:], T.LF[:], 40, "LF0 LF1 LF2 LF3", "LA")
    ts(T.DM[:, 16:32], T.DM[:, 0:16], col(1), float(MSG), A.add, A.add, 16, "DM0 c1", "DM1")
    ts(T.DM[:, 0:16], T.DM[:, 0:16], col(1), B + 0.5, A.add, A.add, 16, "DM0 DM1 c1", "DM0")

    def lanes(n, h):
        return br(n, 64 * h, 64 * h + 64)

    def quarter(o, h, w, e):
        if e == "v":
            ts(o, lanes("X", h), 766.5, None, A.add, None, 32, "x%d" % h, w)
        else:
            act(o, lanes("X", h), AF.Identity, 64, "x%d" % h, w, bias=766.5)

    def column(h, s):
        KB, kb, c = T["KB%d" % h], "KB%d" % h, 16 * s + 4 * h
        part = lambda m, X, a, st, sp: [(KB[:, 0, 48 + q:128:4], mat(m), X[:, a + st * q:a + st * q + 4, :], False, sp and q == 3, 20)
                                        for q in range(4)]
        mm([(KB[:, 0, 48:128], ID, T.BM20[:], True, False, 80)], "ID BM20", kb)
        if CFG["xq"][s] == "d":
            ts(T.XQ[:, 16 * h:16 * h + 16, 0:4], lanes("D", h), 766.5, 766.5, A.add, A.max, 32, "D%d" % h, "XQ%d" % h)
            ts(T.XN[:, 16 * h:16 * h + 16, 0:4], lanes("D", h), -766.5, -766.5, A.add, A.min, 32, "D%d" % h, "XN%d" % h)
            mm(part("A4", T.XQ, 16 * h, 4, False), "A4 XQ%d" % h, kb)
            mm(part("NA", T.XN, 16 * h, 4, True), "NA XN%d" % h, kb)
        else:
            mm(part("NA", T.XN, 64, 0, False), "NA XNc", kb)
            quarter(T.XQ[:, 16 * h:16 * h + 16, 0:4], h, "XQ%d" % h, CFG["xq"][s])
            mm(part("A4", T.XQ, 16 * h, 4, True), "A4 XQ%d" % h, kb)
        o = 80 * h
        pick(T.FB[:, o:o + 80], T.FD[:], KB[:, 0, 48:128], 80, "FD FDa FDb " + kb, "FB%d" % h)
        tt(T.BF[:, c:c + 4], T.FB[:, o + 15:o + 80:20], T.FB[:, o + 19:o + 80:20], A.subtract, 8, "FB%d" % h, "BF%d" % c)
        cp(T.B16[:, c:c + 4], T.BF[:, c:c + 4], 4, "BF%d" % c, "B16_%d" % c)

    def step(h, s, first):
        GR, KB, XJ, M = T["GR%d" % h], T["KB%d" % h], T["XJ%d" % (h % 2)], T.M
        kb, xj, xn, gr = "KB%d" % h, "XJ%d" % (h % 2), "x%d" % h, "GR%d" % h
        c, a = 16 * s + 4 * h, 64 * (h // 2)
        win, wn = (T.H32[:], "H32") if first else (T.S[:, 0:B], "S")
        hs = T.HS[:, 64 * h:64 * h + 64]
        cp(hs, win.indirect(T.B16[:, c:c + 4]), 64, "%s B16_%d" % (wn, c), "HS%d" % h, k="vg")
        mm([(KB[:, :, 0:35], ID, T.KC[:], True, False, 140), (KB[:, :, 0:16], mat("WT"), lanes("X", h), False, False, 64)],
           "ID KCk KCt KCx WTm " + xn, kb)
        if s == 0 and h < CFG["vs0"]:
            cp(GR[:, 33:2081:2], T.G[:].indirect(hs), 1024, "G HS%d" % h, gr, k="vg")
        else:
            act(GR[:, 33:2081:2], T.G[:].indirect(hs), AF.Copy, 1024, "G HS%d" % h, gr, k="ag")
        mm([(XJ[:, a + q:a + 64:4], ID, br("X", 64 * h + 16 * q, 64 * h + 16 * q + 16), True, True, 16) for q in range(4)], "ID " + xn, xj)
        pes = CFG["pes"]
        for u in range(pes):
            mm([(KB[:, :, 16:32], T.W2[:, p, :], GR[:, 33 + 128 * p:161 + 128 * p:2], False, False, 64)
                for p in range(16 * u // pes, 16 * (u + 1) // pes)], "W2 " + gr, kb)
        for k in range(16):
            tt(M[:, h, k::16], GR[:, 33 + 2 * k:2081:32], XJ[:, a:a + 64], A.max, 64, gr + " " + xj, "M%d_%d" % (h, k))
        for u in range(pes):
            mm([(KB[:, :, 16:32], T.W1[:, p, :], M[:, h, 64 * p:64 * p + 64], False, p == 15, 64)
                for p in range(16 * u // pes, 16 * (u + 1) // pes)],
               "W1_0 W1_1 W1_2 W1_3" + "".join(" M%d_%d" % (h, k) for k in range(16)), kb)
        for q in range(4):
            pick(T.SO[:, 4 * h + q, 0:35], T.KD[:, q, 0:35], KB[:, q, 0:35], 35, "KD KD%d %s" % (q, kb), "SO%d_%d" % (h, q))
        tt(T.IXF[:, 4 * h:4 * h + 4], T.SO[:, 4 * h:4 * h + 4, 31], T.SO[:, 4 * h:4 * h + 4, 34], A.subtract, 8,
           " ".join("SO%d_%d" % (h, q) for q in range(4)), "IXF%d" % h)
        cp(T.IX[:, c:c + 4], T.IXF[:, 4 * h:4 * h + 4], 4, "IXF%d" % h, "IX%d" % c)
        tt(lanes("D", h), GR[:].indirect(T.IX[:, c:c + 4]), lanes("X", h), A.subtract, 64,
           "%s GZ%d IX%d %s" % (gr, h, c, xn), "D%d" % h, k="vg")
        act(lanes("X", h), lanes("D", h), AF.Abs, 64, "D%d" % h, xn)

    def words(s, bank, nm):
        tt(T.MK[:, L * s:L * s + L], T.OH[:].indirect(T.IX[:, 16 * s:16 * s + 16]), T.HF[:, L * s:L * s + L], A.mult, L,
           "OH HF%d" % s + "".join(" IX%d" % c for c in range(16 * s, 16 * s + 16, 4)), "MK%d" % s, k="vg")
        mm([(T[bank][:, 0:L], ID, br("BM"), True, False, 256)], "ID BM", bank)
        mm([(T[bank][:, 0:L], fm("ONF"), T.MK[:, L * s:L * s + L], False, True, 1024)], "ONF MK%d" % s, bank)
        pick(row(nm), row("RS"), T[bank][:, 0:L], 256, "RS " + bank, nm)
        sv = row(nm, 15, L, 16)
        act(T.SF[:], sv, AF.Copy, 16, nm, "SF", scale=37.0)
        tt(T.WP[:, 0:16], T.WI[:], sv, A.mult, 32, "WI " + nm, "WPa")
        tt(T.WT[:], T.WI[:], T.SF[:], A.add, 32, "WI SF", "WT")
        ts(T.WP[:, 16:32], T.WP[:, 0:16], 5, None, A.arith_shift_right, None, 16, "WPa", "WPb")
        tt(T.WP[:, 32:48], T.WP[:, 16:32], T.WT[:], A.add, 32, "WPb WT", "WPc")
        ts(T.WI[:], T.WP[:, 32:48], Q - 1, None, A.bitwise_and, None, 16, "WPc", "WI")

    def in_order(s):
        a = 16 * s
        mm([(T.P6[:, 0:128], ID, br("CM", 0, 128), True, False, 128)] +
           [(T.P6[:, q:128:4], fm("PM%d" % q), T.BF[:, a:a + 32], False, q == 3, 256) for q in range(4)],
           "ID CM PM0 PM1 PM2 PM3 " + " ".join("BF%d" % c for c in range(a, a + 32, 4)), "P6")
        for q in range(4):
            pick(T.SB[:, a:a + 32, q], T.RS4[:, 0:32], T.P6[:, q:128:4], 32, "RS4 P6", "SB%d" % q)
        cp(T.BO[:, a:a + 32], T.SB[:, a + 3:a + 32:4, :], 32, allh("SB%d"), "BO%d" % s)
        for u in (s, s + 1):
            act(T.HF[:, L * u:L * u + L], T.S[:, 0:B].indirect(T.BO[:, 16 * u:16 * u + 16]), AF.Copy, L, "S BO%d" % s, "HF%d" % u, k="ag")

    def last_columns(t):
        act(T.B2[:], T.SB[:, 51::4, :], AF.Identity, 16, allh("SB%d"), "B2", scale=2.0)
        act(T.B21[:], T.SB[:, 51::4, :], AF.Identity, 16, allh("SB%d"), "B21", scale=2.0, bias=1.0)
        cp(T.LB[:, 0:16], T.B2[:], 16, "B2", "LB0")
        for d in (1, 2, 3):
            cp(T.LB[:, OFF[4 * d - 4]:OFF[4 * d]], T.B2[:, :, d:4], 12, "B2", "LB%d" % d)
        tt(T.B2R[:, 0:L], T.IOT[:].indirect(T.LB[:, 0:16]), br("TT"), A.add, L, "IOT IOTx LB0 TT", "B2Ra", k="vg")
        act(T.B2R[:, L:640], T.IOT[:].indirect(T.LB[:, 16:40]), AF.Copy, 384, "IOT IOTx LB1 LB2 LB3", "B2Rb", k="ag")
        tt(row("HM"), T.S[:, 0:B].indirect(T.BO[:, 48:64]), br("N%d" % t), A.mult, L, "S BO2 N%d" % t, "HM", k="vg")

    def query(h, t):
        KB, kb, xn = T["KB%d" % h], "KB%d" % h, "x%d" % h
        pn = "P6" if h % 2 == 0 else "P7"
        PB, a, o = T[pn], 64 * h, 88 * h
        fr = lambda n: row(n, a, a + 64)
        xq = T.XQ2[:, 4 * h:4 * h + 4, 0:16]
        quarter(xq, h, "XQ2%d" % h, CFG["xq"][4])
        if t < TR - 1:
            act(lanes("XF", h), lanes("X", h), AF.Identity, 64, xn, "XF%d" % h, bias=1.0)
        mm([(KB[:, 1, 40:128], ID, T.BM22[:], True, False, 88)], "ID BM22 BM22x", kb)
        mm([(KB[:, 1, 40:128], mat("CC4"), T.XQ2[:, 4 * h:4 * h + 4, :], False, True, 88)], "CC4 XQ2%d" % h, kb)
        pick(T.F2[:, o:o + 88], T.FE[:], KB[:, 1, 40:128], 88, "FE " + kb, "F2%d" % h)
        sl = lambda u: T.F2[:, o + u:o + 88:22]
        mm([(KB[:, 2, 48:52], fm("AI"), sl(16), True, False, 256), (KB[:, 2, 48:52], fm("NAI"), sl(18), False, False, 256),
            (KB[:, 2, 48:52], IDF, sl(18), False, False, 256), (KB[:, 2, 48:52], fm("NIF"), sl(21), False, True, 256)],
           "AI NAI IDF NIF F2%d" % h, kb)
        ts(T.XI[:, 4 * h:4 * h + 4], KB[:, 2, 48:52], 1.5 * PIT, None, A.add, None, 4, kb, "XI%d" % h)
        for nm, f in (("RD", AF.Abs), ("HI", AF.Sign)):
            act(lanes(nm, h), T.XR[:].indirect(T.XI[:, 4 * h:4 * h + 4]), f, 64, "XRo XRx XRd XI%d" % h, "%s%d" % (nm, h), k="ag")
        dl = KB[:, 2, 64:128]
        mm([(dl, mat("NI"), lanes("X", h), True, False, 64), (dl, ID, lanes("RD", h), False, True, 64)], "ID NI RD%d %s" % (h, xn), kb)
        act(lanes("RA", h), dl, AF.Abs, 64, kb, "RA%d" % h, bias=-1.0)
        mm([(PB[:, 0:64], ID, mat("DN", 64), True, False, 64)], "ID DN", pn)
        mm([(PB[:, 0:64], mat("CC"), xq, False, True, 64)], "CC XQ2%d" % h, pn)
        ts(T.TQ[:, a:a + 64], PB[:, 0:64], C4, C4, A.add, A.subtract, 64, pn, "TQ%d" % h)
        tt(lanes("MQ", h), T.TQ[:, a:a + 64], PB[:, 0:64], A.is_equal, 64, "TQ%d %s" % (h, pn), "MQ%d" % h)
        scan(lanes("CN", h), lanes("MQ", h), lanes("MQ", h), 0.0 if h == 0 else br("CN", a - 1, a), A.add, A.max, 32,
             "MQ%d" % h + (" CN%d" % (h - 1) if h else ""), "CN%d" % h)
        mm([(PB[:, 128:192], mat("I3"), lanes("MQ", h), True, False, 64), (PB[:, 128:192], ID, lanes("CN", h), False, True, 64)],
           "I3 ID MQ%d CN%d" % (h, h), pn)
        act(lanes("SP", h), PB[:, 128:192], AF.Relu, 64, pn, "SP%d" % h, bias=-512.0 - CAP)
        act(lanes("MC", h), PB[:, 128:192], AF.Relu, 64, pn, "MC%d" % h, bias=-512.0)
        vv, an = KB[:, 1, 64:128], KB[:, 3, 64:128]
        mm([(vv, ID, br("BC", 0, 64), True, False, 64), (vv, mat("SV"), lanes("HI", h), False, True, 64)], "ID BC SV HI%d" % h, kb)
        pick(fr("VA"), row("RS", 0, 64), vv, 64, "RS " + kb, "VA%d" % h)
        mm([(an, ID, br("BM", 0, 64), True, False, 64), (an, mat("THM"), lanes("MQ", h), False, False, 64),
            (an, mat("NEG"), lanes("SP", h), False, False, 64)], "ID BM THM NEG MQ%d SP%d" % (h, h), kb)
        mm([(an, mat("N8"), lanes("RA", h), False, True, 64)], "N8 RA%d" % h, kb)
        pick(fr("AN"), row("RS", 0, 64), an, 64, "RS " + kb, "AN%d" % h)
        mm([(PB[:, 64:128], ID, br("BM", 0, 64), True, False, 64), (PB[:, 64:128], mat("SELD"), lanes("MQ", h), False, False, 64),
            (PB[:, 64:128], mat("SEL4"), lanes("MC", h), False, True, 64)], "ID BM SELD SEL4 MQ%d MC%d" % (h, h), pn)
        pick(fr("FS"), row("RS", 0, 64), PB[:, 64:128], 64, "RS " + pn, "FS%d" % h)

    def store(t):
        last = t == TR - 1
        R, rr = T.R[:, t, :], "R%d R%dx" % (t, t)
        if last:
            ts(rb("RQ"), R, 766.5, None, A.add, None, 96, rr, "RQ")
        else:
            act(rb("RX"), R, AF.Abs, 192, rr, "RX")
            ts(rb("RQ"), rb("RX"), 765.5, None, A.add, None, 96, "RX", "RQ")
        mm([(T.P6[:, 0:192], ID, br("BM", 0, 192), True, False, 192)], "ID BM", "P6")
        mm([(T.P6[:, 0:192], mat("CC"), rb("RQ"), False, True, 192)], "CC RQ", "P6")
        pick(rf("SO"), row("RS", 0, 192), T.P6[:, 0:192], 192, "RS P6", "SOo")
        ts(T.PL[:, 0:12], rf("SO", 15, 192, 16), col(14), None, A.subtract, None, 12, "SOo c13", "PLa")
        ts(T.PL[:, 16:28], T.PL[:, 0:12], 2, H - 1, A.arith_shift_right, A.bitwise_and, 12, "PLa", "PLb")
        cp(T.PL16[:, 0:12], T.PL[:, 16:28], 12, "PLb", "PL16")
        cp(T.PLF[:, 0:12], T.PL[:, 16:28], 12, "PLb", "PLF")
        act(rf("PR"), T.IOT[:].indirect(T.PL16[:, 0:12]), AF.Copy, 192, "IOT IOTx PL16", "PR", k="ag")
        act(rf("PB"), T.PLF[:, 0:12].indirect(T.LA[:, 0:12]), AF.Copy, 192, "PLF LA", "PB", k="ag")
        if last:
            act(rb("JS"), rf("RW"), AF.Sign, 192, "RW RWx", "JS", bias=0.5 - Q)
        else:
            act(rb("JS"), R, AF.Sign, 192, rr, "JS THa", accum_out=T.TH[:, 4:5])
            mm([(T.P7[:, 0:1], fm("S12"), T.TH[:, 4:5], True, True, 256)], "S12 THa", "P7")
            cp(T.THI[:, 0:1], T.P7[:, 0:1], 1, "P7", "THI0")
            ts(T.THI[:, 1:2], T.THI[:, 0:1], 7, None, A.bitwise_and, None, 1, "THI0", "THI1")
            ts(T.XR[:, own + H:own + H + 1], T.THI[:, 1:2], col(19), None, A.mult, None, 1, "THI1 c19", "XRo")
        mm([(T.P6[:, 0:192], ID, rb("TRI" if last else "TR2"), True, False, 192), (T.P6[:, 0:192], IDF, rf("PB"), False, False, 768)],
           "ID TRI TR2 IDF PB", "P6")
        mm([(T.P6[:, 0:192], fm("NIF"), rf("PR"), False, False, 768)], "NIF PR", "P6")
        mm([(T.P6[:, 0:192], mat("KI" if last else "KF"), rb("JS"), False, True, 192)], "KI KF JS", "P6")
        act(rb("AB"), T.P6[:, 0:192], AF.Abs, 192, "P6", "AB", scale=4096.0)
        pick(rb("ES"), br("RSB", 0, 192), rb("AB"), 96, "RSB AB", "ES")
        tt(T.SM[:, 0:12], T.DM[:, 16:28], rb("ES", 15, 192, 16), A.subtract, 24, "ES DM1", "SMa")
        tt(T.SM[:, 16:28], T.SM[:, 0:12], T.PLF[:, 0:12], A.max, 24, "SMa PLF", "SMb")
        cp(T.LS[:, 0::2], T.SM[:, 16:28], 12, "SMb", "LS")
        for q in range(11, -1, -1):
            ls, src = T.LS[:, 2 * q:2 * q + 1], T.R[:, t, 16 * q:16 * q + 16]
            if last:
                cp(T.XB[:].indirect(ls), src, 16, "LS " + rr, "XB", k="vs")
                cp(T.YV[:].indirect(ls), rf("RW", 16 * q, 16 * q + 16), 16, "LS RW RWx", "YV", k="vs")
            else:
                cp(T.XR[:, own:own + PIT].indirect(ls), src, 16, "LS " + rr, "XRo", k="vs")
        if not last:
            remote(lambda d: T.XR[:, own:own + MSG], T.XR[:, own:own + MSG], "XRo", "XRx", same=True)
        if t == TR - 2:
            act(T.XB[:, 0:H], T.XR[:, own:own + H], AF.Abs, H, "XRo", "XB")
            ts(T.XB[:, 0:H], T.XB[:, 0:H], -1.0, None, A.add, None, 256, "XB", "XB")
            act(T.SG[:], T.XR[:, own:own + H], AF.Sign, H, "XRo", "SG")
            mm([(T.P7[:], mat("SV"), T.SG[:], True, True, H)], "SV SG", "P7")
            act(T.YV[:, 0:H], T.P7[:], AF.Identity, H, "P7", "YV", bias=2048.0)

    for h in range(NB):
        tag[0] = h
        column(h, 0)
    mine = slice(CAP * rank, CAP * rank + CAP)

    def items(t):
        remote(lambda d: T.SE[:, t, reg(d)], T.R[:, t, mine], "SE%d" % t, "R%dx" % t)
        dma("s", T.R[:, t, mine], T.SE[:, t, reg(rank)], 12, "SE%d" % t, "R%d" % t)

    for t in range(TR):
        last = t == TR - 1
        for s in range(ST):
            for h in range(NB):
                tag[0] = h
                step(h, s, t == 0 and s == 0)
                if s < ST - 1:
                    column(h, s + 1)
            tag[0] = None
            if t > 0 and s == CFG["own"]:
                store(t - 1)
            if s % 2 == 0:
                in_order(s)
            if s < ST - 1:
                words(s, "P7", "SC")
            if s == ST - 2:
                last_columns(t)
                op("v", lambda: V.tensor_reduce(T.TH[:, 0:1], T.XR[:, H::PIT], AxisListType.X, A.add), ("v", 4), "XRo XRx", "TH")
                ts(mat("THM"), mat("SEL4"), T.TH[:, 0:1], None, A.mult, None, 64, "SEL4 TH", "THM")
        for h in range(NB):
            query(h, t)
        ts(T.SL[:], row("FS", 15, L, 16), 15.0, None, A.add, None, 16, allh("FS%d"), "SL")
        if last:
            cp(T.SE[:, t, :].indirect(T.SL[:]), br("X"), L, "SL " + allh("x%d"), "SE%d" % t, k="vs")
            items(t)
        words(ST - 1, "XJ0", "S3")
        cp(T.W16[:], T.WI[:], 16, "WI", "W16")
        for u in range(2):
            D, dn, xn, a = br("D", 128 * u, 128 * u + 128), "D%d D%d" % (2 * u, 2 * u + 1), "x%d x%d" % (2 * u, 2 * u + 1), 128 * u
            XJ, xj = T["XJ%d" % u], "XJ%d" % u
            act(br("GJ", a, a + 128), T.G[:].indirect(T.W16[:, 8 * u:8 * u + 8]), AF.Copy, 128, "G W16", "GJ%d" % u, k="ag")
            mm([(XJ[:, 256:384], mat("NI"), br("X", a, a + 128), True, False, 128), (XJ[:, 256:384], ID, br("GJ", a, a + 128), False, True, 128)],
               "NI ID GJ%d %s" % (u, xn), xj)
            act(D, XJ[:, 256:384], AF.Abs, 128, xj, dn)
            act(br("XO" if last else "X", a, a + 128), D, AF.Identity, 128, dn, "XO%d" % u if last else xn, scale=-1.0, bias=63.0)
        if not last:
            for h in range(NB):
                column(h, 0)
        an, av = allh("AN%d"), row("AN", 15, L, 16)
        Z = lambda j: T.ZI[:, 16 * j:16 * j + 16]
        Y = lambda j: T.ZF[:, 16 * j:16 * j + 16]
        va, vv = allh("VA%d"), row("VA", 15, L, 16)
        tt(Y(1), vv, T.WI[:], A.is_equal, 32, va + " WI", "Y1")
        tt(Y(2), Y(1), T.B2[:], A.add, 32, "Y1 B2", "Y2")
        tt(Y(0), av, T.B21[:], A.min, 32, an + " B21", "Y0")
        tt(T.B2N[:], Y(2), Y(0), A.max, 32, "Y2 Y0", "B2N")
        mm([(T.P7[:, 0:L], ID, br("BM"), True, False, 256), (T.P7[:, 0:L], fm("IDH"), T.B2R[:, 0:L], False, False, 1024)], "ID BM IDH B2Ra", "P7")
        tt(T.TE[:], T.B2N[:].indirect(T.LA[:]), T.B2R[:], A.is_equal, 640, "B2N B2Ra B2Rb LA", "TE", k="vg")
        mm([(T.P7[:, 64 * m + 16 * d:64 * m + 64], mat("ON2"), T.TE[:, 16 * OFF[u]:16 * OFF[u + 1]], False, False, 48)
            for u, (d, m) in enumerate(CROSS)] + [(T.P7[:, 0:L], mat("ON2"), T.TE[:, 0:L], False, True, 256)], "ON2 TE", "P7")
        pick(row("CF"), row("RS"), T.P7[:, 0:L], 256, "RS P7", "CF")
        tt(Y(3), row("CF", 15, L, 16), T.DM[:, 0:16], A.min, 32, "CF DM0", "Y3")
        ts(T.LH[:], Y(3), -0.5, None, A.add, None, 16, "Y3", "LH")
        tt(Z(2), vv, T.WI[:], A.mult, 32, va + " WI", "Z2")
        tt(Y(4), vv, T.WI[:], A.add, 32, va + " WI", "Y4")
        ts(Z(3), Z(2), 5, None, A.arith_shift_right, None, 16, "Z2", "Z3")
        tt(Z(4), Z(3), Y(4), A.add, 32, "Z3 Y4", "Z4")
        ts(Z(5), Z(4), Q - 1, None, A.bitwise_and, None, 16, "Z4", "Z5")
        cp(T.Z16[:], Z(5), 16, "Z5", "Z16")
        tt(row("ZD"), T.IOT[:].indirect(T.Z16[:]), br("K%d" % t), A.mult, L, "IOT IOTx Z16 K%d" % t, "ZD", k="vg")
        ts(Y(5), av, 0.0, float(Q), A.is_le, A.mult, 16, an, "Y5")
        tt(Y(5), Y(5), T.WI[:], A.max, 32, "Y5 WI", "Y5")
        cp(T.WK[:], Y(5), 16, "Y5", "WK")
        if last:
            act(row("WR"), T.IOT[:].indirect(T.WK[:]), AF.Copy, L, "IOT IOTx WK", "WR", k="ag")
            cp(T.SW[:].indirect(T.SL[:]), row("WR"), L, "WR SL", "SW", k="vs")
            remote(lambda d: T.SW[:, reg(d)], rf("RW", mine.start, mine.stop), "SW", "RWx")
            dma("s", rf("RW", mine.start, mine.stop), T.SW[:, reg(rank)], 24, "SW", "RW")
        else:
            signs(T.SG[:, 0:L], T.IOT[:].indirect(T.WK[:]), L, "IOT IOTx WK", "SG", "XJ1", k="ag")
            tt(T.SE[:, t, :].indirect(T.SL[:]), T.SG[:, 0:L], br("XF"), A.mult, L, "SG SL " + allh("XF%d"), "SE%d" % t, k="vs")
            items(t)
        if last:
            for u in range(2):
                mm([(T.XJ1[:], fm("KW"), T.S[:, 512 * u:512 * u + 512], True, True, 2048)], "KW S", "XJ1")
                act(T.YH[:, 512 * u:512 * u + 512], T.XJ1[:], AF.Copy, 512, "XJ1", "YH")
            mm([(T.XJ0[:, 0:L], fm("KW"), row("HM"), True, False, 1024)], "KW HM", "XJ0")
            mm([(T.XJ0[:, 0:L], fm("KW"), row("ZD"), False, True, 1024)], "KW ZD", "XJ0")
            act(row("AG"), T.XJ0[:, 0:L], AF.Copy, 256, "XJ0", "AG")
        for m in range(3, -1, -1):
            ls, a, b = T.LH[:, 4 * m:4 * m + 4], 64 * m, 64 * m + 64
            if last:
                cp(T.YH[:].indirect(ls), row("AG", a, b), 64, "LH AG", "YH", k="vs")
            else:
                tt(T.S[:].indirect(ls), row("ZD", a, b), row("HM", a, b), A.add, 64, "LH ZD HM", "S", k="vs")
    store(TR - 1)
    act(row("YW"), T.IOT[:].indirect(T.W16[:]), AF.Copy, L, "IOT IOTx W16", "YW", k="ag")
    dma("s", T.yx[:], br("XO"), 64, "XO0 XO1", "")
    dma("s", T.yw[:], T.FM[0::16, ROWS.index("YW"), :], 8, "YW", "")
    dma("s", T.yh[:], T.YH[0::16, 0:B], 32, "YH", "")
    dma("s", T.ys[:], T.XB[:, 0:H], 128, "XB", "")
    dma("a", T.yv[:], T.YV[0::16, 0:H], 16, "YV", "")
    return ops


def link(ops):
    wr, rd, deps = {}, {}, []
    ps = lambda k: k[:2] in ("XJ", "P6", "P7", "KB")
    for i, o in enumerate(ops):
        d = {}
        for k in o["r"] + o["w"]:
            if k in wr:
                j = wr[k]
                same = ops[j]["eng"] == o["eng"] and (ops[j]["kind"] == "c" or k[:4] == "gord")
                d[j] = d.get(j, False) or (not same) or (not ps(k) and k[:4] != "gord")
            if k in o["w"] or ps(k):
                for j in rd.get(k, []):
                    d[j] = True
        d.pop(i, None)
        deps.append(d)
        for k in o["r"] + o["w"]:
            if k in o["w"] or ps(k):
                wr[k] = i
                rd[k] = []
        for k in o["r"]:
            if not (k in o["w"] or ps(k)):
                rd.setdefault(k, []).append(i)
    return deps


def span(o, par):
    k, n = o["cost"]
    c = par["cyc"] * 0.83
    if k == "v":
        return par["vfix"] + max(64, n) * c, 0.0
    if k == "vg":
        return 50 * par["cyc"] + par["gam"] * n * c, 0.0
    if k == "vs":
        return 50 * par["cyc"] + par["sig"] * n * c, 0.0
    if k == "a":
        return par["afix"] + n * c, 0.0
    if k == "ag":
        return 65 * par["cyc"] + par["gam"] * n * c, 0.0
    if k == "p":
        return par["pe"] * n * c, 60.0
    if k == "q":
        return 130 + 2 * n * c, 0.0
    if k == "d":
        return 60.0, par["dma"] + 5.0 * n
    if k == "r":
        return 300.0, 0.0
    return 0.0, par["rem" if k == "x" else "big"]


def edges(ops, deps, par):
    sp = [span(o, par) for o in ops]
    before = [[(j, (sp[j][1] + par["lat"]) if hard else 0.001) for j, hard in d.items()] for d in deps]
    after = [[] for _ in ops]
    for i, lst in enumerate(before):
        for j, lg in lst:
            after[j].append((i, lg))
    return sp, before, after


def clock(ops, seq, sp, before):
    fin, free = [0.0] * len(ops), {}
    for i in seq:
        e = ops[i]["eng"]
        t = max([fin[j] + lg for j, lg in before[i]] + [0.0 if e == "x" else free.get(e, 0.0)])
        fin[i] = free[e] = t + sp[i][0]
    return max(fin[i] + sp[i][1] for i in seq)


def order(ops, deps, par):
    n = len(ops)
    tests = [edges(ops, deps, dict(par, **u)) for u in SPREAD]
    sp, before, after = edges(ops, deps, par)
    big = [i for i in range(n) if ops[i]["cost"] == ("ag", 1024)]
    best = None
    for beat in CFG["beat"]:
        aim = {i: CFG["t0"] + beat * u + CFG["gap"] * (u // (NB * ST)) for u, i in enumerate(big)}
        end = aim[big[-1]] + CFG["tail"]
        due = [0.0] * n
        for i in range(n - 1, -1, -1):
            due[i] = aim[i] if i in aim else min([due[j] - lg for j, lg in after[i]] + [end - sp[i][1]]) - sp[i][0]
        pri = [-d for d in due]
        for it in range(CFG["passes"]):
            start = place(ops, sp, before, after, pri, [0.0] * n)
            seq = sorted(range(n), key=lambda i: (start[i], i))
            score = sum(math.log(clock(ops, seq, s, b)) for s, b, a in tests)
            if best is None or score < best[0]:
                best = (score, seq)
            back = place(ops, sp, after, before, [start[i] + sp[i][0] for i in range(n)], [x[1] for x in sp])
            pri = [back[i] + sp[i][0] for i in range(n)]
    return best[1]


def place(ops, sp, before, after, pri, t0):
    n = len(ops)
    left = [len(d) for d in before]
    ready = [i for i in range(n) if left[i] == 0]
    start = [0.0] * n
    busy = {}
    while ready:
        i = max(ready, key=lambda j: (pri[j], -j))
        ready.remove(i)
        t = t0[i]
        for j, lg in before[i]:
            t = max(t, start[j] + sp[j][0] + lg)
        lst = busy.setdefault(ops[i]["eng"], [])
        dur = sp[i][0]
        lo, hi = 0, len(lst)
        while lo < hi:
            mid = (lo + hi) // 2
            if lst[mid][1] <= t:
                lo = mid + 1
            else:
                hi = mid
        while lo < len(lst) and lst[lo][0] < t + dur * CFG["fit"]:
            t = max(t, lst[lo][1])
            lo += 1
        lst.insert(lo, (t, t + dur if lo == len(lst) else min(t + dur, max(t, lst[lo][0]))))
        start[i] = t
        for j, lg in after[i]:
            left[j] -= 1
            if left[j] == 0:
                ready.append(j)
    return start


ORDER = []


def rank_program(g, core, T, topo):
    rank = T.rank_of(core)
    if rank is None:
        return
    ops = build(g, core, T, topo, rank)
    deps = link(ops)
    if not ORDER:
        ORDER.append(order(ops, deps, PAR))
    seq = ORDER[0]
    queue = {"v": g.vector, "a": g.scalar, "p": g.tensor, "q": g, "s": g.sync}
    need = set()
    for i, d in enumerate(deps):
        if ops[i]["kind"] != "x":
            need.update(j for j, hard in d.items() if hard)
    count, mark, seen, extra = {}, {}, {}, []
    for i in seq:
        o = ops[i]
        if o["kind"] == "x":
            mark[i] = o["sem"]
            extra.append(o["sem"])
            continue
        e = o["eng"]
        want = {}
        for j, hard in deps[i].items():
            if hard:
                s, val = mark[j]
                want[s] = max(want.get(s, 0), val)
        for s, val in want.items():
            if seen.get((e, s), 0) < val:
                queue[e].wait_ge(T.sem[s], val)
                seen[(e, s)] = val
        ins = o["fn"]()
        if o["kind"] == "d":
            ins.then_inc(T.sem[o["sem"][0]], 16)
        if o["kind"] != "c":
            mark[i] = o["sem"]
            extra.append(o["sem"])
        elif i in need:
            count[e] = count.get(e, 0) + 1
            ins.then_inc(T.sem[e], 1)
            mark[i] = (e, count[e])
    for s, val in list(count.items()) + extra:
        g.wait_ge(T.sem[s], val)
